import numpy as np, ml_dtypes
CORES = [1,5,17,21,33,37,49,53]
N = 8
BF = ml_dtypes.bfloat16
V, P, Q, RO, TS = 128, 2, 1, 3, 1024
M, B = 8 * N * V, V // P
def clip(a):
    return np.minimum(np.maximum(np.floor(a), -2 ** 20), 2 ** 20 - 1).astype(np.int64)
def walls(rng, base, size, gap):
    mid = base + size * (rng.random((N, 8, 16, V)) - 0.5)
    h = gap * (16 - np.arange(16)[:, None]) * 0.0625
    l = mid + h * rng.random((N, 8, 16, V)); r = mid - h * rng.random((N, 8, 16, V)); turn = rng.random((N, 8, 1, V)) < 0.25
    return clip(np.where(turn, r, l)), clip(np.where(turn, l, r))
def common(rng):
    return walls(rng, rng.integers(-2 ** 18, 2 ** 18, (N, 8, 1, V)), np.exp2(rng.integers(8, 18, (N, 8, 1, V))), 2.0 ** 17 * rng.random((N, 8, 1, V)))
def slots(rng):
    share = rng.choice(np.array([0.1, 0.4, 0.7, 0.9]), (N, 8, 2, 1, V))
    o = rng.integers(0, M, (N, 8, 16, V)); none = (rng.random((N, 8, 2, 8, V)) < share).reshape(N, 8, 16, V)
    return np.where(none, M, o)
def pack(l, r, o):
    return {"lw": np.ascontiguousarray(l.reshape(N, 128, V)).astype(np.int32), "rw": np.ascontiguousarray(r.reshape(N, 128, V)).astype(np.int32),
            "opts": np.ascontiguousarray(o.reshape(N, 128, V)).astype(np.int32)}
def setup_inputs(rng):
    l, r = common(rng)
    return pack(l, r, slots(rng))
def setup_inputs_ties(rng):
    ix = rng.integers(0, 5, (N, 8, V)); base = 65536 * np.array([0, 0, 12, 12, -13])[:, None] + 2 * rng.integers(-4, 5, (5, 1)); out = []
    for up in (rng.integers(0, 6), 0):
        prof = base + up + rng.integers(0, 2, (5, 16))
        a = prof[ix].transpose(0, 1, 3, 2)
        i = rng.integers(0, 16, (N, 8, 1, V)); d = rng.choice(np.array([-1, 1]), (N, 8, 1, V)) * (rng.random((N, 8, 1, V)) < 0.3)
        far = 65536 * (rng.random((N, 8, 1, V)) < 0.125)
        out.append(a + d * (np.arange(16)[:, None] == i) + far)
    return pack(out[0], out[1], np.where(rng.random((N, 8, 16, V)) < 0.3, M, rng.integers(0, M, (N, 8, 16, V))))
def setup_inputs_bare(rng):
    l, r = common(rng); kinds = np.zeros((7, 16), bool)
    kinds[1, :8] = True; kinds[2, 8:] = True; kinds[3] = True; kinds[4, [0, 15]] = True; kinds[5, [7, 8]] = True; kinds[6, 0] = True
    cls = rng.integers(0, 7, (N, 8, V)); cls[:, 3] = 0; cls[:, 5] = 3
    o = np.where(kinds[cls].transpose(0, 1, 3, 2), rng.integers(0, M, (N, 8, 16, V)), M)
    for g, s, e, d in ((1, 0, -2 ** 20, 1), (6, 15, 2 ** 20 - 1, -1)):
        l[:, g] = e + d * rng.integers(0, 64, (N, 16, V)); r[:, g] = e + d * rng.integers(0, 64, (N, 16, V))
        o[:, g] = M; o[:, g, s] = V * (8 * rng.integers(0, N, (N, V)) + g) + rng.integers(0, B, (N, V))
    return pack(l, r, o)
def setup_inputs_ends(rng):
    l, r = common(rng); o = slots(rng)
    o[:, ::2] = rng.choice(np.array([0, V - 1, V, 8 * V - 1, 8 * V, M - 1, M]), (N, 4, 16, V))
    o[:, 2] = rng.integers(0, M)
    own = V * np.arange(8 * N).reshape(N, 8, 1, 1) + np.arange(V)
    o[:, 1] = np.where(rng.random((N, 16, V)) < 0.5, own[:, 1], o[:, 1])
    o[:, 3, :8] = o[:, 3, :1]; o[:, 3, 8:] = o[:, 3, 8:9]
    here = 8 * V * np.arange(N)[:, None, None]; nxt = 8 * V * ((np.arange(N) + 1) % N)[:, None, None]
    o[:, 5] = nxt + rng.integers(0, 8 * V, (N, 16, V))
    o[:, 7] = np.where(o[:, 7] < M, here + rng.integers(0, 8 * V, (N, 16, V)), M)
    return pack(l, r, o)
def setup_inputs_late(rng):
    bump = rng.random((N, 8, 1, V)) < 0.0625; bump[:, 4] = False
    l = rng.integers(-2 ** 12, 2 ** 12, (16, 1)) + bump
    r = l + rng.choice(np.array([-3, 0, 3, 5001]), (16, 1))
    z = rng.integers(0, 8, (N, 8, 2, 1, V)); s = np.arange(8)[:, None]
    has = np.where(rng.random((N, 8, 2, 1, V)) < 0.4, s == z, s >= z).reshape(N, 8, 16, V)
    o = np.where(has, rng.integers(0, M, (N, 8, 16, V)), M)
    o[:, 4] = V * (8 * rng.integers(0, N, (N, 16, V)) + 4) + rng.integers(0, V, (N, 16, V))
    return pack(l, r, o)
def setup_inputs_spread(rng):
    base = rng.choice(np.array([-1.0, 1.0]), (N, 8, 1, V)) * np.exp2(20 * rng.random((N, 8, 1, V)))
    l, r = walls(rng, base, np.abs(base) * rng.random((N, 8, 1, V)), np.exp2(18 * rng.random((N, 8, 1, V))))
    e = rng.integers(1, 5, (1, 8, 1, 1))
    o = np.minimum((M * rng.random((N, 8, 16, V)) ** e).astype(np.int64), M - 1)
    share = rng.random((N, 8, 1, V)); share[rng.integers(0, N)] = 0.0
    return pack(l, r, np.where(rng.random((N, 8, 16, V)) < share, M, o))
def check_inputs(d):
    bad = []
    for k, lo, hi in (("lw", -2 ** 20, 2 ** 20 - 1), ("rw", -2 ** 20, 2 ** 20 - 1), ("opts", 0, M)):
        if np.min(d[k]) < lo or np.max(d[k]) > hi: bad.append("range of " + k)
    return bad
def world(a, last):
    w = a.reshape(N, 8, 16, V).transpose(2, 0, 1, 3).reshape(16, M).astype(np.int32)
    return np.concatenate([w, np.full((16, 1), last, np.int32)], axis=1)
def back(w):
    return np.ascontiguousarray(w[:, :M].reshape(16, N, 8, V).transpose(1, 2, 0, 3)).reshape(N, 128, V).astype(np.float32)
def inner(L, R, ix):
    return np.concatenate([R[:, ix[:8]], -L[:, ix[8:]]], axis=1)
def reference(lw, rw, opts):
    L, R, O = world(lw, 0), world(rw, 0), world(opts, M)
    temp = (TS * np.arange(16, dtype=np.int32))[:, None]; s16 = np.arange(16); left = (s16 < 8)[:, None]
    for t in range(RO):
        nL, nR, nO = L.copy(), R.copy(), O.copy()
        v = np.tile(B * (t % P) + np.arange(B), 8 * N); c = V * np.repeat(np.arange(8 * N), B) + v
        o = O[:, c]; xl, xr = L[:, c], R[:, c]; has = o < M
        u = inner(L, R, o); gone = np.zeros(o.shape, bool)
        for q in range(Q):
            p = s16 ^ (1 + (t + 3 * q) % 7); up = u[:, p]
            ge = np.all(up >= u, axis=0); eq = np.all(up == u, axis=0)
            gone = gone | (has & has[p] & ge & (~eq | (p < s16)[:, None]))
        sl = (v + t) & 7; k = O[np.where(left, 8 + sl, sl), o]
        kl, kr = L[:, k], R[:, k]; yl, yr = xl[:, None, :], xr[:, None, :]
        under = np.all((kl[:, :8] <= yl) & (kr[:, :8] <= yr), axis=0); over = np.all((kl[:, 8:] >= yl) & (kr[:, 8:] >= yr), axis=0)
        rev = (has & ~gone & (k < M) & np.concatenate([under, over], axis=0)).reshape(2, 8, -1).astype(np.int64)
        first = (rev == 1) & (np.add.accumulate(rev, axis=1) == 1)
        ch = np.where(np.any(first, axis=1), np.add.reduce(first * k.reshape(2, 8, -1), axis=1), M)
        ent = O[s16[:, None], np.repeat(ch, 8, axis=0)]
        n = np.where(has & ~gone & ~first.reshape(16, -1), o, ent); hn = n < M
        w = np.where(hn[None], inner(L, R, n), -2 ** 23)
        l = np.where(np.any(hn[:8], axis=0)[None], np.max(w[:, :8], axis=1) - temp, xl)
        r = np.where(np.any(hn[8:], axis=0)[None], temp - np.max(w[:, 8:], axis=1), xr)
        low = l < r; mid = (l + r) >> 1
        nL[:, c] = np.where(low, mid, l); nR[:, c] = np.where(low, mid, r); nO[:, c] = n
        L, R, O = nL, nR, nO
    return {"yl": back(L), "yr": back(R), "yo": back(O)}

@@ -1,0 +1,545 @@
+from concourse.bass import DstId, RemoteDMATransfer
+from concourse.mybir import AluOpType as A, ActivationFunctionType as AF
+
+EXW = ["0", "1", "2", "3"]
+EXO = ["i", "2", "3"]
+NREP = {"0": (2, 1), "1": (1, 1), "2": (1, 1), "3": (1, 1)}
+FREE = ["LW0", "LOi", "LW1", "LO2", "LO3"]
+BIG = 2.0 ** 23
+MATB = (["REP%d" % p for p in range(4)] + ["YM", "E8", "GT", "ENT0", "ENT1", "KEEPN", "ANY0", "ANY1", "KX0", "KX1", "KN0", "KN1", "IB",
+        "TMN", "TMP", "ONES", "PERM64", "PERM1", "OXH0", "OXH1", "OXL0", "OXL1"]
+        + ["ICO%d" % f for f in range(6)] + ["INV%d" % f for f in range(5)])
+MATF = ["REPF%d" % p for p in range(4)] + ["CH0", "CH1", "SW", "NSW", "ISW", "INVF"]
+SLID = ["OTH", "BKO"] + ["BD%d" % d for d in range(6)]
+DELTA = [1, -1, 2, -2, 3, -3]
+F, B16, I32, U16 = "float32", "bfloat16", "int32", "uint16"
+SCRATCH = {}
+for _n, _w, _d in (("W", 8200, F), ("OT", 8208, B16), ("MBF", 128 * len(MATB), B16), ("MFF", 128 * len(MATF), F), ("MSL", 144 * len(SLID) + 160, B16),
+                   ("CI", 16, I32), ("CF", 64, F), ("XI", 144, F), ("MI", 128, I32), ("MF", 768, I32), ("MKI", 1152, I32), ("MK", 1152, B16),
+                   ("RS", 640, F), ("ST", 256, I32), ("OI", 128, I32), ("FI", 896, I32), ("FB", 896, B16), ("HB", 128, B16), ("OF", 128, F),
+                   ("OL", 128, U16), ("XE0", 1024, F), ("XE1", 1024, F), ("GM", 1024, B16), ("KL", 128, U16), ("KC", 64, F), ("HAS", 64, F),
+                   ("U", 1024, F), ("VO", 1024, B16), ("VX", 1024, B16), ("C", 1024, B16), ("R1", 64, F), ("REV", 64, B16), ("ND", 64, F),
+                   ("NH", 64, F), ("FF", 64, F), ("FK", 64, F), ("KEEP", 64, B16), ("OK", 64, F), ("CL", 32, U16), ("E", 512, B16),
+                   ("OXA", 128, B16), ("HN", 64, B16), ("U5", 1024, F), ("MX", 1024, F), ("OWNW", 128, F), ("M1", 128, I32), ("M2", 128, I32),
+                   ("NF", 128, F), ("YW0", 128, F), ("YW1", 128, F), ("YI", 64, I32), ("YFI", 320, I32), ("YFB", 320, B16), ("YO0", 64, F),
+                   ("YO1", 64, F), ("LW0", 1024, F), ("LW1", 1024, F), ("LW2", 1024, F), ("LW3", 1024, F), ("LOi", 2048, B16), ("LO2", 1024, B16),
+                   ("LO3", 1024, B16)):
+    SCRATCH[_n] = ("sbuf", [128, _w], _d)
+for _n in ("K0", "K1", "RV", "DD", "YY", "NP", "UP"):
+    SCRATCH[_n] = ("psum", [128, 1024 if _n == "UP" else 512], F)
+SEMAPHORES = (["sV", "sS", "sP", "sG", "dOI", "dST"]
+              + [k + "W" + x for x in EXW for k in ("p", "m", "l", "f")] + [k + "O" + x for x in EXO for k in ("p", "m", "l", "f")]
+              + ["dW%s%d" % (x, h) for x in EXW for h in (0, 1)] + ["dY0", "dY1", "dO0", "dO1"])
+
+
+def rank_program(g, core, T, topo):
+    rank = T.rank_of(core)
+    if rank is None:
+        return
+    cores = list(T.cores)
+    side = [int(topo.die(c) != topo.die(cores[0])) for c in cores]
+    slot = [4 * side[r] + sum(1 for q in range(r) if side[q] == side[r]) for r in range(len(cores))]
+    assert slot == [4 * (r & 1) + (r >> 1) for r in range(len(cores))]
+    me, half = slot[rank], side[rank]
+    peers = [c for r, c in enumerate(cores) if side[r] == half and c != core]
+    mate = [c for c in cores if c != core and topo.chip(c) == topo.chip(core)][0]
+    eng = {"V": g.vector, "S": g.scalar, "P": g.tensor, "G": g, "Y": g.sync}
+    cnt, known, clk, wr, rd, bk, toks_all = {q: 0 for q in eng}, {q: {} for q in eng}, {}, {}, {}, {}, {}
+
+    def need(q, toks):
+        best = {}
+        for s, v in toks:
+            best[s] = max(best.get(s, 0), v)
+        todo = [(s, v) for s, v in best.items() if known[q].get(s, 0) < v]
+        todo = [t for t in todo if not any(o != t and clk[o].get(t[0], 0) >= t[1] for o in todo)]
+        for s, v in todo:
+            eng[q].wait_ge(T.sem[s], v)
+            for a, b in clk[(s, v)].items():
+                known[q][a] = max(known[q].get(a, 0), b)
+            known[q][s] = max(known[q].get(s, 0), v)
+
+    def pre(q, R, W, B=()):
+        toks = []
+        for r in R:
+            toks += wr.get(r, [])
+        for w in W:
+            toks += wr.get(w, []) + rd.get(w, [])
+        for b in B:
+            toks += [t for e, t in bk.get(b, {}).items() if e != q]
+        need(q, toks)
+
+    def post(q, tok, R, W, B=()):
+        clk[tok] = dict(known[q])
+        toks_all[tok[0]] = max(toks_all.get(tok[0], 0), tok[1])
+        for r in R:
+            rd[r] = [t for t in rd.get(r, []) if t[0] != tok[0]] + [tok]
+        for w in W:
+            wr[w], rd[w] = [tok], []
+        for b in B:
+            bk.setdefault(b, {})[q] = tok
+
+    def emit(q, calls, R=(), W=(), B=()):
+        pre(q, R, W, B)
+        for c in calls:
+            c().then_inc(T.sem["s" + q], 1)
+            cnt[q] += 1
+        post(q, ("s" + q, cnt[q]), R, W, B)
+
+    def dmas(q, pairs, sem, R=(), W=()):
+        pre(q, R, W)
+        for o, i in pairs:
+            eng[q].dma_start(out=o, in_=i).then_inc(T.sem[sem], 16)
+        post(q, (sem, 16 * len(pairs)), R, W)
+
+    def arrive(sem, val, W):
+        clk[(sem, val)] = {}
+        toks_all[sem] = val
+        for w in W:
+            wr[w] = wr.get(w, []) + [(sem, val)]
+
+    def ts(out, in0, s1, op0, s2=None, op1=None, R=(), W=(), B=()):
+        if op1 is None:
+            emit("V", [lambda: g.vector.tensor_scalar(out=out, in0=in0, scalar1=s1, scalar2=None, op0=op0)], R, W, B)
+        else:
+            emit("V", [lambda: g.vector.tensor_scalar(out=out, in0=in0, scalar1=s1, scalar2=s2, op0=op0, op1=op1)], R, W, B)
+
+    def tt(out, a, b, op, R=(), W=(), B=()):
+        emit("V", [lambda: g.vector.tensor_tensor(out=out, in0=a, in1=b, op=op)], R, W, B)
+
+    def cp(q, out, i, R=(), W=(), B=()):
+        if q == "V":
+            emit("V", [lambda: g.vector.tensor_copy(out=out, in_=i)], R, W, B)
+        else:
+            emit("S", [lambda: g.scalar.activation(out=out, in_=i, func=AF.Copy)], R, W, B)
+
+    def sc(dst, src, scale, R, W):
+        emit("S", [lambda: g.scalar.activation(out=dst, in_=src, func=AF.Copy, scale=float(scale))], R, W)
+
+    def mms(groups, R=(), W=(), B=()):
+        emit("P", [(lambda m=m: g.tensor.matmul(out=m[0], lhsT=m[1], rhs=m[2], start=m[3], stop=m[4])) for m in groups], R, W, B)
+
+    def MB(n):
+        j = MATB.index(n)
+        return T.MBF[:, 128 * j:128 * j + 128]
+
+    def MX(n):
+        j = MATF.index(n)
+        return T.MFF[:, 128 * j:128 * j + 128]
+
+    def SL(n, q=None):
+        j = 4 if n == "OWN" else 160 + 144 * SLID.index(n)
+        return T.MSL[:, j:j + 144] if q is None else T.MSL[:, j + 15 - q:j + 143 - q]
+
+    dmas("Y", [(T.OI[:], T.opts[:])], "dOI", (), ["OI"])
+    for q, r0, src in (("Y", 0, T.lw), ("S", 16, T.rw)):
+        for P in range(4):
+            for h in (0, 1):
+                eng[q].dma_start(out=T.ST[32 * P + r0:32 * P + r0 + 16, 128 * h:128 * h + 128],
+                                 in_=src[32 * P + 16 * h:32 * P + 16 * h + 16, :]).then_inc(T.sem.dST, 16)
+    arrive("dST", 16 * 16, ["ST"])
+    emit("G", [lambda: g.iota(T.CI[:, 0:1], [[0, 1]], 0, 1)], (), ["ci0"])
+    emit("G", [lambda: g.iota(T.XI[:], [[1, 144]], 0, 0, allow_small_or_imprecise_dtypes=True)], (), ["XI"])
+    emit("G", [lambda: g.iota(T.MI[:], [[1, 128]], 0, 0)], (), ["MI"])
+    emit("G", [lambda: g.iota(T.MKI[:], [[0, 9], [1, 8], [0, 16]], 0, 0)], (), ["MKI"])
+    ints = [("P", 5, 7), ("rho", 4, 1), ("grp", 4, 15), ("i", 0, 15), ("s", 0, 7), ("h3", 3, 1), ("blk", 3, 31), ("b0", 0, 1), ("b1", 1, 1)]
+    for j, (n, sh, m) in enumerate(ints):
+        ts(T.CI[:, j + 1:j + 2], T.CI[:, 0:1], sh, A.logical_shift_right, m, A.bitwise_and, ["ci0"], ["ci%d" % (j + 1)])
+    names = ["k"] + [x[0] for x in ints]
+    cp("V", T.CF[:, 0:10], T.CI[:, 0:10], ["ci%d" % j for j in range(10)], ["c_" + n for n in names])
+
+    def col(n):
+        j = names.index(n)
+        return T.CF[:, j:j + 1]
+
+    def lin(n, a, m, add, q="S"):
+        names.append(n)
+        d = add if not isinstance(add, str) else col(add)
+        R = ["c_" + a] + (["c_" + add] if isinstance(add, str) else [])
+        if q == "S":
+            emit("S", [lambda: g.scalar.activation(out=col(n), in_=col(a), func=AF.Identity, bias=d, scale=float(m))], R, ["c_" + n])
+        else:
+            ts(col(n), col(a), float(m), A.mult, d, A.add, R, ["c_" + n])
+
+    def mat(dst, name, f, fr, h, w, wn=None):
+        ts(dst, f, col(h), A.is_equal, w if wn is None else col(wn), A.mult, [fr, "c_" + h] + ([] if wn is None else ["c_" + wn]), [name])
+
+    Xm, Xs = T.XI[:, 0:128], T.XI[:]
+    lin("sgn", "rho", 2, -1.0, "V")
+    lin("ntemp", "i", -1024, 0.0, "V")
+    ico = [1.0, 63.0, 12.0, -8.0, -30.0, -1.0]
+    mat(MB("IB"), "IB", Xm, "XI", "k", 1.0)
+    for j in range(1, 6):
+        sc(MB("ICO%d" % j), MB("IB"), ico[j], ["IB"], ["ICO%d" % j])
+    lin("X0", "P", 32, "s", "V")
+    lin("OXn", "h3", 16, "X0", "V")
+    lin("n0", "rho", -1, 1.0, "V")
+    for h in (0, 1):
+        mat(MB("OXH%d" % h), "OXH%d" % h, Xm, "XI", "OXn", None, ["n0", "rho"][h])
+    fi = [(6, 255), (6, 1), (8, 3), (10, 1), (11, 3), (7, 1), (0, 63)]
+    for j, (sh, m) in enumerate(fi):
+        ts(T.FI[:, 128 * j:128 * j + 128], T.OI[:], sh, A.logical_shift_right, m, A.bitwise_and, ["OI"], ["FI%d" % j])
+
+    def own_walls(b):
+        for h in (0, 1):
+            ts(T["LW%d" % b][:, 128 * me + 64 * h:128 * me + 64 * h + 64], T.ST[:, 128 * h + 64 * b:128 * h + 64 * b + 64], col("sgn"), A.mult,
+               col("ntemp"), A.add, ["ST", "c_sgn", "c_ntemp"], ["LW%do%d" % (b, h)])
+
+    def send(x, kind, buf, w):
+        blk = T[buf][:, w * me:w * me + w]
+        pre("G", [kind + x + "o0", kind + x + "o1"], [])
+        tag = buf[1] + x
+        ids = [DstId(rid=topo.addr(c)[0], pnc=topo.addr(c)[1]) for c in peers]
+        g.remote_dma_fused([RemoteDMATransfer(dst_ids=ids, dma_engine_mask=topo.mask(core, peers[0]), remote_sem=T.sem["p" + tag], srcs=[blk],
+                                              dsts=[blk for c in peers])], local_sem=T.sem["l" + tag])
+        ne = len(topo.engines(core, peers[0]))
+        toks_all["l" + tag] = ne
+        arrive("p" + tag, len(peers) * ne, [kind + x + "p"])
+
+    def forward(x, kind, buf, w):
+        pre("G", [kind + x + "o0", kind + x + "o1", kind + x + "p"], [])
+        tag = buf[1] + x
+        blk = T[buf][:, 4 * w * half:4 * w * half + 4 * w]
+        es = topo.engines(core, mate)
+        if kind + x in FREE:
+            es = [e for e in es if e not in topo.engines(core, peers[0])]
+        g.remote_dma(blk, blk, T.sem["m" + tag], T.sem["f" + tag], topo.addr(mate)[1], topo.addr(mate)[0], sum(1 << e for e in es))
+        toks_all["f" + tag] = len(es)
+        arrive("m" + tag, len(es), [kind + x + "m"])
+
+    def have(kind, x, h):
+        return [kind + x + "o0", kind + x + "o1", kind + x + "p"] if h == half else [kind + x + "m"]
+
+    own_walls(0)
+    send("0", "LW", "LW0", 128)
+    flds = [("f8", 3, 31), ("f16", 4, 15), ("f31", 0, 31), ("f15", 0, 15), ("f119", 0, 119), ("f4", 2, 31)]
+
+    def fld(n):
+        j = [x[0] for x in flds].index(n)
+        return T.MF[:, 128 * j:128 * j + 128]
+
+    cp("V", T.FB[:, 0:768], T.FI[:, 0:768], ["FI%d" % j for j in range(6)], ["FB"])
+    mms([(T.K0[:, 0:128], MB("ICO%d" % j) if j else MB("IB"), T.FB[:, 128 * j:128 * j + 128], j == 0, j == 5) for j in range(6)],
+        ["FB", "IB"] + ["ICO%d" % j for j in range(1, 6)], ["K0.h"], ["K0"])
+    cp("V", T.FB[:, 768:896], T.FI[:, 768:896], ["FI6"], ["FB6"])
+    lin("OXl", "OXn", 1, 8.0, "V")
+    for h in (0, 1):
+        mat(MB("OXL%d" % h), "OXL%d" % h, Xm, "XI", "OXl", None, ["n0", "rho"][h])
+    cp("V", T.HB[:], T.K0[:, 0:128], ["K0.h"], ["HB"], ["K0"])
+    low = T.FB[:, 768:896]
+    for h, bank in ((0, "RV"), (1, "NP")):
+        mms([(T[bank][:, 0:128], MB("OXH%d" % h), T.HB[:], True, False), (T[bank][:, 0:128], MB("OXL%d" % h), low, False, True)],
+            ["HB", "FB6", "OXH%d" % h, "OXL%d" % h], [bank + ".x"], [bank])
+    for h, bank in ((0, "RV"), (1, "NP")):
+        for b in (0, 1):
+            c0 = 256 * me + 128 * b + 64 * h
+            cp("V" if h == 0 else "S", T.LOi[:, c0:c0 + 64], T[bank][:, 64 * b:64 * b + 64], [bank + ".x"], ["LOio%d" % h + ("b" if b else "")], [bank])
+    for h in (0, 1):
+        wr["LOio%d" % h] = wr["LOio%d" % h] + wr["LOio%db" % h]
+    own_walls(1)
+    send("i", "LO", "LOi", 256)
+    send("1", "LW", "LW1", 128)
+    forward("0", "LW", "LW0", 128)
+    forward("i", "LO", "LOi", 256)
+    forward("1", "LW", "LW1", 128)
+    lin("pa", "h3", -16, "X0")
+    lin("pb", "rho", 8, "pa")
+    lin("PERMh", "pb", 1, 16.0)
+    mat(MB("PERM1"), "PERM1", Xm, "XI", "PERMh", 1.0)
+    sc(MB("PERM64"), MB("PERM1"), 64.0, ["PERM1"], ["PERM64"])
+    mms([(T.K1[:, 0:128], MB("PERM64"), T.HB[:], True, False), (T.K1[:, 0:128], MB("PERM1"), low, False, True)],
+        ["HB", "FB6", "PERM64", "PERM1"], ["K1.o"], ["K1"])
+    cp("V", T.OF[:], T.K1[:, 0:128], ["K1.o"], ["OF0", "OF1"], ["K1"])
+    cp("V", T.OL[:], T.OF[:], ["OF0", "OF1"], ["OL0", "OL1"])
+    for j, (n, sh, m) in enumerate(flds):
+        ts(fld(n), T.MI[:], sh, A.logical_shift_right, m, A.bitwise_and, ["MI"], [n])
+    for p in range(4):
+        lin("kr%d" % p, "k", 1, -32.0 * p)
+        mat(MB("REP%d" % p), "REP%d" % p, fld("f31"), "f31", "kr%d" % p, 1.0)
+        if p >= 2:
+            sc(MX("REPF%d" % p), MB("REP%d" % p), 1.0, ["REP%d" % p], ["REPF%d" % p])
+    emit("V", [lambda: g.vector.memset(T.W[:, 8192:8200], -BIG)], (), ["Wz"])
+    lin("sent", "h3", -128, 128.0)
+    emit("V", [lambda: g.vector.memset(MB("ONES"), 1.0)], (), ["ONES"])
+    ones = 128 * MATB.index("ONES")
+    ts(T.OT[:, 8192:8208], T.MBF[:, ones:ones + 16], col("sent"), A.mult, None, None, ["ONES", "c_sent"], ["OTz"])
+    ts(T.MK[:], T.MKI[:], col("s"), A.is_equal, None, None, ["MKI", "c_s"], ["MK"])
+    lin("own15", "grp", 16, 15.0)
+    lin("w64", "h3", -63, 64.0)
+    mat(SL("BKO"), "BKO", Xs, "XI", "own15", None, "w64")
+    lin("sa", "rho", -32, "k")
+    lin("SWh", "sa", 1, 16.0)
+    mat(MX("SW"), "SW", Xm, "XI", "SWh", 1.0)
+
+    def late():
+        emit("V", [lambda: g.vector.memset(T.MSL[:, 0:4], 0.0), lambda: g.vector.memset(T.MSL[:, 148:160], 0.0)], (), ["GUARD"])
+        mat(SL("OWN"), "OWN", Xs, "XI", "own15", 1.0)
+        lin("ot", "rho", -32, "own15")
+        lin("oth15", "ot", 1, 16.0)
+        mat(SL("OTH"), "OTH", Xs, "XI", "oth15", 1.0)
+        sc(T.MX[:, 0:152], T.MSL[:, 0:152], 32.0, ["OWN", "GUARD"], ["MX0"])
+        for j, d in enumerate(DELTA):
+            k0 = 160 + 144 * SLID.index("BD%d" % j)
+            tt(T.MSL[:, k0:k0 + 144], T.MX[:, 4:148], T.MSL[:, 4 - d:148 - d], A.subtract, ["MX0", "OWN", "GUARD"], ["BD%d" % j])
+        lin("thr1", "b0", 1, -0.5)
+        lin("thr2", "b1", 1, -0.5)
+        mat(MB("E8"), "E8", fld("f8"), "f8", "blk", -2.0)
+        ts(MB("GT"), Xm, col("k"), A.is_gt, None, None, ["XI", "c_k"], ["GT"])
+        tt(MB("E8"), MB("E8"), MB("GT"), A.mult, ["GT"], ["E8"])
+        tt(MB("YM"), MB("E8"), MB("IB"), A.add, ["E8", "IB"], ["YM"])
+        lin("bf", "rho", -4, "blk")
+        lin("blkf", "bf", 1, 2.0)
+        lin("bl2", "blkf", 2, 0.0)
+        lin("bl3", "blkf", 2, 1.0)
+        mat(MX("CH0"), "CH0", fld("f4"), "f4", "bl2", 1.0)
+        mat(MX("CH1"), "CH1", fld("f4"), "f4", "bl3", 1.0)
+        lin("ta", "rho", -16, "X0")
+        lin("T0", "ta", 1, 16.0)
+        lin("T8", "ta", 1, 24.0)
+        lin("g0", "h3", -1, 1.0)
+        lin("a0", "g0", -BIG, 0.0)
+        lin("a1", "h3", -BIG, 0.0)
+        lin("temp", "i", 1024, 0.0)
+        mat(MB("ENT0"), "ENT0", Xm, "XI", "T0", None, "w64")
+        mat(MB("ENT1"), "ENT1", Xm, "XI", "T8", None, "w64")
+        for h, gn in ((0, "g0"), (1, "h3")):
+            mat(MB("ANY%d" % h), "ANY%d" % h, fld("f16"), "f16", "grp", None, "a%d" % h)
+            mat(MB("KX%d" % h), "KX%d" % h, fld("f119"), "f119", "T0", None, gn)
+
+    def late2():
+        tt(MX("ISW"), MX("SW"), MB("IB"), A.add, ["SW", "IB"], ["ISW"])
+        names.append("kz")
+        ts(col("kz"), col("k"), 0.0, A.is_equal, -1024.0, A.mult, ["c_k"], ["c_kz"])
+        ts(MB("TMN"), fld("f15"), col("kz"), A.mult, None, None, ["f15", "c_kz"], ["TMN"])
+        emit("V", [lambda: g.vector.memset(T.RS[:], 0.0)], (), ["RS"])
+        emit("V", [lambda: g.vector.memset(T.RS[:, 0::8], -BIG)], (), ["RS"])
+
+    def late2s():
+        sc(MB("KEEPN"), MB("IB"), -16384.0, ["IB"], ["KEEPN"])
+        for h in (0, 1):
+            sc(MB("KN%d" % h), MB("KX%d" % h), -256.0, ["KX%d" % h], ["KN%d" % h])
+        sc(MX("NSW"), MX("SW"), -1.0, ["SW"], ["NSW"])
+        sc(MB("TMP"), MB("TMN"), -1.0, ["TMN"], ["TMP"])
+
+    def late3():
+        lin("iv", "rho", -8, "OXn")
+        lin("INVh", "iv", 1, 8.0)
+        mat(MX("INVF"), "INVF", Xm, "XI", "INVh", 1.0)
+        for j, c in enumerate([-4032.0, -768.0, 512.0, 1920.0, 64.0]):
+            sc(MB("INV%d" % j), MX("INVF"), c, ["INVF"], ["INV%d" % j])
+
+    OTALL = ["OTz"] + ["OT%d%d%d" % (b, p, h) for b in (0, 1) for p in range(4) for h in (0, 1)]
+    WALL = ["Wz"] + ["W%d%d%d" % (b, p, h) + z for b in (0, 1) for p in range(4) for h in (0, 1) for z in ("", "s")]
+    rb = [("UP", 0, "UPa"), ("UP", 512, "UPb"), ("YY", 0, "YY"), ("DD", 0, "DD")]
+    nb = [0]
+
+    def rep_o(x, b, h, qs):
+        for p in range(4):
+            buf, c0, bank = rb[nb[0] % 4]
+            nb[0] += 1
+            out = T[buf][:, c0:c0 + 512]
+            if x == "i":
+                ms = [(T[buf][:, c0 + 128 * j:c0 + 128 * j + 128], MB("REP%d" % p),
+                       T.LOi[:, 256 * (4 * h + j) + 128 * b:256 * (4 * h + j) + 128 * b + 128], True, True) for j in range(4)]
+            else:
+                ms = [(out, MB("REP%d" % p), T["LO" + x][:, 512 * h:512 * h + 512], True, True)]
+            mms(ms, have("LO", x, h) + ["REP%d" % p], [bank + ".r"], [bank])
+            d0 = 4096 * b + 1024 * p + 512 * h
+            cp(qs[p % len(qs)], T.OT[:, d0:d0 + 512], out, [bank + ".r"], ["OT%d%d%d" % (b, p, h)], [bank])
+
+    def rep_w_dma(x, b, h):
+        n = 4 - NREP[x][h != half]
+        dmas("Y", [(T.W[32 * pp:32 * pp + 32, 4096 * b + 1024 * p + 512 * h:4096 * b + 1024 * p + 512 * h + 512],
+                    T["LW" + x][32 * p:32 * p + 32, 512 * h:512 * h + 512]) for p in range(n) for pp in range(4) if pp != p],
+             "dW%s%d" % (x, h), have("LW", x, h) + (have("LO", "i", half) if x == "0" else []), ["W%d%d%d" % (b, p, h) for p in range(n)])
+
+    def rep_w_same(x, b, h, q):
+        for p in range(4 - NREP[x][h != half]):
+            d0 = 4096 * b + 1024 * p + 512 * h
+            cp(q, T.W[32 * p:32 * p + 32, d0:d0 + 512], T["LW" + x][32 * p:32 * p + 32, 512 * h:512 * h + 512], have("LW", x, h), ["W%d%d%ds" % (b, p, h)])
+
+    def rep_w_pe(x, b, h, q):
+        for p in range(4 - NREP[x][h != half], 4):
+            buf, c0, bank = rb[nb[0] % 4]
+            nb[0] += 1
+            out = T[buf][:, c0:c0 + 512]
+            mms([(out, MX("REPF%d" % p), T["LW" + x][:, 512 * h:512 * h + 512], True, True)], have("LW", x, h) + ["REPF%d" % p], [bank + ".r"], [bank])
+            d0 = 4096 * b + 1024 * p + 512 * h
+            cp(q, T.W[:, d0:d0 + 512], out, [bank + ".r"], ["W%d%d%d" % (b, p, h)], [bank])
+
+    def expand(x, b):
+        for q in range(16):
+            hh = q >> 3
+            cp("S", T["XE%d" % b][:, q::16], T["LW" + x][:, 128 * me + 64 * hh:128 * me + 64 * hh + 64], ["LW%so%d" % (x, hh)], ["XE%d.%d" % (b, q)])
+
+    def lists_gather(t):
+        b = t & 1
+        tt(T.GM[:], T.OT[:].indirect(T.OL[:, 64 * b:64 * b + 64]), T.MK[:, 16 * t:16 * t + 1024], A.mult, OTALL + ["OL%d" % b, "MK"], ["GM"])
+
+    def lists(t):
+        b = t & 1
+        mms([(T.K0[:, 0:64], SL("BKO", q), T.GM[:, q::16], q == 0, q == 15) for q in range(16)], ["GM", "BKO"], ["K0.k"], ["K0"])
+        ts(T.KC[:], T.K0[:, 0:64], -8192.0, A.add, None, None, ["K0.k"], ["KC"], ["K0"])
+        mms([(T.K1[:, 0:64], MX("SW"), T.KC[:], True, True)], ["KC", "SW"], ["K1.k"], ["K1"])
+        cp("V", T.KL[:, 0:64], T.K0[:, 0:64], ["K0.k"], ["KL0"], ["K0"])
+        ts(T.HAS[:], T.OF[:, 64 * b:64 * b + 64], 8191.5, A.is_lt, None, None, ["OF%d" % b], ["HAS"])
+        ts(T.KL[:, 64:128], T.K1[:, 0:64], 8192.0, A.add, None, None, ["K1.k"], ["KL1"], ["K1"])
+
+    def fields(b):
+        cp("V", T.YI[:], T.OF[:, 64 * b:64 * b + 64], ["OF%d" % b], ["YI"])
+        for j, (sh, m) in enumerate([(12, 1), (10, 3), (9, 1), (7, 3), (6, 1)]):
+            ts(T.YFI[:, 64 * j:64 * j + 64], T.YI[:], sh, A.logical_shift_right, m, A.bitwise_and, ["YI"], ["YFI%d" % j])
+        cp("V", T.YFB[:], T.YFI[:], ["YFI%d" % j for j in range(5)], ["YFB"])
+
+    def natural(b):
+        mms([(T.YY[:, 128:192], MX("INVF"), T.OF[:, 64 * b:64 * b + 64], True, False)]
+            + [(T.YY[:, 128:192], MB("INV%d" % j), T.YFB[:, 64 * j:64 * j + 64], False, j == 4) for j in range(5)],
+            ["OF%d" % b, "YFB", "INVF"] + ["INV%d" % j for j in range(5)], ["YY.n"], ["YY"])
+        cp("S", T["YO%d" % b][:], T.YY[:, 128:192], ["YY.n"], ["YO%d" % b], ["YY"])
+        dmas("Y", [(T.yo[:, 64 * b:64 * b + 64], T["YO%d" % b][:])], "dO%d" % b, ["YO%d" % b], [])
+
+    def round_(t):
+        b, m = t & 1, 1 + t
+        x = {0: "0", 1: "1", 2: "2"}[t]
+        nx = {0: "2", 1: "3", 2: None}[t]
+        xe = ["XE%d.%d" % (b, q) for q in range(16)]
+        Wt = T.W[:]
+        mine = "LW%so" % x
+        ol = T.OL[:, 64 * b:64 * b + 64]
+        emit("S", [lambda: g.scalar.activation(out=T.U[:], in_=Wt.indirect(ol), func=AF.Copy)], WALL + ["OL%d" % b], ["U"])
+        cp("S", T.UP[:], T.U[:], ["U"], ["UPa.r", "UPb.r"], ["UPa", "UPb"])
+        if t == 0:
+            late2s()
+        XE = T["XE%d" % b]
+        tt(T.VO[:], Wt.indirect(T.KL[:, 0:64]), XE[:], A.is_gt, WALL + ["KL0"] + xe, ["VO"])
+        mms([(T.RV[:, 0:64], SL("OWN", q), T.VO[:, q::16], q == 0, False) for q in range(16)], ["VO", "OWN"], ["RV.v"], ["RV"])
+        tt(T.VX[:], Wt.indirect(T.KL[:, 64:128]), XE[:], A.is_lt, WALL + ["KL1"] + xe, ["VX"])
+        mms([(T.RV[:, 0:64], SL("OTH", q), T.VX[:, q::16], False, q == 15) for q in range(16)], ["VX", "OTH"], ["RV.v2"], ["RV"])
+        st = {1: [(0, 1, 2)], 2: [(0, 2, 4), (1, 3, 4)], 3: [(0, 3, 4), (1, 2, 4)]}[m]
+        thr = "thr1" if m == 1 else "thr2"
+        nq = 0
+        for u, v, s in st:
+            for y, z in ((u, v), (v, u)):
+                tt(T.C[:, y::s], T.U[:, y::s], T.UP[:, z::s], A.is_gt, ["U", "UPa.r", "UPb.r"], ["C%d" % y], ["UPa", "UPb"])
+                qs = range(y, 16, s)
+                mms([(T.DD[:, 0:64], SL("BD%d" % DELTA.index((q ^ m) - q), q), T.C[:, q::16], nq + j == 0, nq + j == 15) for j, q in enumerate(qs)],
+                    ["C%d" % y] + ["BD%d" % j for j in range(6)], ["DD.d%d" % y], ["DD"])
+                nq += len(qs)
+        dd = ["DD.d%d" % y for u, v, s in st for y in (u, v)]
+        ts(T.R1[:], T.RV[:, 0:64], 1024.0, A.mult, col(thr), A.add, ["RV.v", "RV.v2", "c_" + thr], ["R1"], ["RV"])
+        tt(T.REV[:], T.DD[:, 0:64], T.R1[:], A.is_ge, dd + ["R1"], ["REV"], ["DD"])
+        mms([(T.YY[:, 0:64], MB("YM"), T.REV[:], True, True)], ["REV", "YM"], ["YY.y"], ["YY"])
+        ts(T.ND[:], T.DD[:, 0:64], col(thr), A.is_ge, None, None, dd + ["c_" + thr], ["ND"], ["DD"])
+        tt(T.NH[:], T.ND[:], T.HAS[:], A.mult, ["ND", "HAS"], ["NH"])
+        ts(T.FF[:], T.YY[:, 0:64], 0.5, A.is_gt, None, None, ["YY.y"], ["FF"], ["YY"])
+        tt(T.FK[:], T.FF[:], T.KC[:], A.mult, ["FF", "KC"], ["FK"])
+        mms([(T.YY[:, 64:96], MX("CH%d" % e), T.FK[:, 32 * e:32 * e + 32], e == 0, e == 1) for e in (0, 1)], ["FK", "CH0", "CH1"], ["YY.c"], ["YY"])
+        tt(T.KEEP[:], T.NH[:], T.FF[:], A.subtract, ["NH", "FF"], ["KEEP"])
+        tt(T.OK[:], T.OF[:, 64 * b:64 * b + 64], T.KEEP[:], A.mult, ["OF%d" % b, "KEEP"], ["OK"])
+        mms([(T.NP[:, 0:64], MB("KEEPN"), T.KEEP[:], True, False)], ["KEEP", "KEEPN"], ["NP.n"], ["NP"])
+        ts(T.CL[:], T.YY[:, 64:96], 8192.0, A.add, None, None, ["YY.c"], ["CL"], ["YY"])
+        if nx:
+            mms([(T.RV[:, 64 * h + 128:64 * h + 192], MB("KX%d" % h), T.KEEP[:], True, True) for h in (0, 1)], ["KEEP", "KX0", "KX1"], ["RV.k"], ["RV"])
+        emit("V", [lambda: g.vector.tensor_copy(out=T.E[:, 0:256], in_=T.OT[:].indirect(T.CL[:, 0:16]))], OTALL + ["CL"], ["E0"])
+        emit("S", [lambda: g.scalar.activation(out=T.E[:, 256:512], in_=T.OT[:].indirect(T.CL[:, 16:32]), func=AF.Copy)], OTALL + ["CL"], ["E1"])
+        mms([(T.NP[:, 32 * e:32 * e + 32], MB("ENT%d" % h), T.E[:, 8 * h + 4 * e::16], False, h == 1 and e == 1) for e in (0, 1) for h in (0, 1)],
+            ["E0", "E1", "ENT0", "ENT1"], ["NP.n2"], ["NP"])
+        if nx:
+            old = T.LOi[:, 256 * me + 128 * b:256 * me + 128 * b + 128]
+            tt(T.OXA[:], T.RV[:, 128:256], old, A.mult, ["RV.k", "LOio0", "LOio1"], ["OXA"], ["RV"])
+            for h in (0, 1):
+                mms([(T.DD[:, 128 + 64 * h:192 + 64 * h], MB("KN%d" % h), T.KEEP[:], True, False)]
+                    + [(T.DD[:, 128 + 64 * h + 32 * e:160 + 64 * h + 32 * e], MB("IB"), T.E[:, 8 * h + 4 * e::16], False, e == 1) for e in (0, 1)],
+                    ["KEEP", "E0", "E1", "IB", "KN%d" % h], ["DD.x%d" % h], ["DD"])
+        n = T.OF[:, 64 * b:64 * b + 64]
+        tt(n, T.NP[:, 0:64], T.OK[:], A.max, ["NP.n", "NP.n2", "OK"], ["OF%d" % b], ["NP"])
+        cp("V", ol, n, ["OF%d" % b], ["OL%d" % b])
+        for h, bank in ((0, "K0"), (1, "K1")):
+            mms([(T[bank][:, 0:64], MX("NSW"), T["LW" + x][:, 128 * me + 64 * h:128 * me + 64 * h + 64], True, False),
+                 (T[bank][:, 0:64], MB("TMN"), T.MBF[:, ones:ones + 64], False, False)], [mine + "0", mine + "1", "NSW", "TMN", "ONES"], [bank + ".a"], [bank])
+        emit("S", [lambda: g.scalar.activation(out=T.U5[:, 384:1024], in_=Wt.indirect(T.OL[:, 64 * b + 24:64 * b + 64]), func=AF.Copy)],
+             WALL + ["OL%d" % b], ["U51"])
+        if nx:
+            for h in (0, 1):
+                tt(T["LO" + nx][:, 128 * me + 64 * h:128 * me + 64 * h + 64], T.DD[:, 128 + 64 * h:192 + 64 * h], T.OXA[:, 64 * h:64 * h + 64], A.max,
+                   ["DD.x%d" % h, "OXA"], ["LO%so%d" % (nx, h)], ["DD"])
+            send(nx, "LO", "LO" + nx, 128)
+        emit("V", [lambda: g.vector.tensor_copy(out=T.U5[:, 0:384], in_=Wt.indirect(T.OL[:, 64 * b:64 * b + 24]))], WALL + ["OL%d" % b], ["U50"])
+        ts(T.HN[:], n, 8191.5, A.is_lt, None, None, ["OF%d" % b], ["HN"])
+        for h, bank in ((0, "K0"), (1, "K1")):
+            mms([(T[bank][:, 0:64], MB("ANY%d" % h), T.HN[:], False, True)], ["HN", "ANY%d" % h], [bank + ".b"], [bank])
+        for h, c0, c1 in ((0, 0, 384), (1, 384, 1024)):
+            emit("V", [lambda: g.vector.tensor_tensor_scan(out=T.MX[:, c0:c1], data0=T.RS[:, 0:c1 - c0], data1=T.U5[:, c0:c1],
+                                                           initial=-2.0 * BIG, op0=A.add, op1=A.max)], ["RS", "U5%d" % h], ["MX%d" % h])
+        for h, bank in ((0, "K0"), (1, "K1")):
+            tt(T.OWNW[:, 64 * h:64 * h + 64], T.MX[:, 7 + 8 * h::16], T[bank][:, 0:64], A.max, ["MX0", "MX1", bank + ".a", bank + ".b"], ["OWN%d" % h], [bank])
+        mms([(T.NP[:, 256:384], MB("TMP"), MB("ONES"), True, False)], ["TMP", "ONES"], ["NP.t"], ["NP"])
+        mms([(T.RV[:, 256:384], MX("ISW"), T.OWNW[:], True, True)], ["OWN0", "OWN1", "ISW"], ["RV.s"], ["RV"])
+        mms([(T.NP[:, 256:384], MX("SW"), T.OWNW[:], False, True)], ["OWN0", "OWN1", "SW"], ["NP.t2"], ["NP"])
+        if not nx:
+            fields(b)
+            natural(b)
+        ts(T.M1[:], T.RV[:, 256:384], 0.0, A.min, col("n0"), A.add, ["RV.s", "c_n0"], ["M1"], ["RV"])
+        ts(T.M2[:], T.M1[:], 1, A.arith_shift_right, None, None, ["M1"], ["M2"])
+        if nx:
+            tt(T["LW" + nx][:, 128 * me:128 * me + 128], T.M2[:], T.NP[:, 256:384], A.subtract, ["M2", "NP.t", "NP.t2"], ["LW%so0" % nx, "LW%so1" % nx], ["NP"])
+            send(nx, "LW", "LW" + nx, 128)
+            forward(nx, "LO", "LO" + nx, 128)
+            forward(nx, "LW", "LW" + nx, 128)
+            src, sr = T["LW" + nx][:, 128 * me:128 * me + 128], ["LW%so0" % nx, "LW%so1" % nx]
+        else:
+            tt(T.NF[:], T.M2[:], T.NP[:, 256:384], A.subtract, ["M2", "NP.t", "NP.t2"], ["NF"], ["NP"])
+            src, sr = T.NF[:], ["NF"]
+        if t > 0:
+            ts(T["YW%d" % b][:], src, col("temp"), A.add, col("sgn"), A.mult, sr + ["c_temp", "c_sgn"], ["YW%d" % b])
+            for q, y, r0 in (("Y", T.yl, 0), ("S", T.yr, 16)):
+                pre(q, ["YW%d" % b], [])
+                for P in range(4):
+                    for h in (0, 1):
+                        eng[q].dma_start(out=y[32 * P + 16 * h:32 * P + 16 * h + 16, 64 * b:64 * b + 64],
+                                         in_=T["YW%d" % b][32 * P + r0:32 * P + r0 + 16, 64 * h:64 * h + 64]).then_inc(T.sem["dY%d" % b], 16)
+            toks_all["dY%d" % b] = 16 * 16
+            if nx:
+                fields(b)
+                natural(b)
+
+    hs = [half, 1 - half]
+    expand("0", 0)
+    rep_w_pe("0", 0, hs[0], "S")
+    late()
+    for b in (0, 1):
+        rep_o("i", b, hs[0], "S")
+    for x, b in (("0", 0), ("1", 1)):
+        for h in hs:
+            rep_w_dma(x, b, h)
+    rep_w_same("0", 0, hs[0], "S")
+    for b in (0, 1):
+        rep_o("i", b, hs[1], "VS")
+    rep_w_same("0", 0, hs[1], "S")
+    lists_gather(0)
+    rep_w_same("1", 1, hs[0], "V")
+    rep_w_pe("0", 0, hs[1], "S")
+    rep_w_pe("1", 1, hs[0], "S")
+    lists(0)
+    rep_w_same("1", 1, hs[1], "V")
+    rep_w_pe("1", 1, hs[1], "S")
+    late2()
+    round_(0)
+    late3()
+    expand("1", 1)
+    for t, x, b in ((1, "2", 0), (2, "3", 1)):
+        for h in hs:
+            rep_w_dma(x, b, h)
+        for h in hs:
+            rep_o(x, b, h, "VS")
+        lists_gather(t)
+        rep_w_same(x, b, hs[0], "S")
+        rep_w_pe(x, b, hs[0], "S")
+        lists(t)
+        rep_w_same(x, b, hs[1], "S")
+        rep_w_pe(x, b, hs[1], "S")
+        round_(t)
+        if t == 1:
+            expand("2", 0)
+    for s in SEMAPHORES:
+        if toks_all.get(s, 0) > known["G"].get(s, 0):
+            g.wait_ge(T.sem[s], toks_all[s])

@@ -1,35 +1,36 @@
 from concourse.bass import DstId, RemoteDMATransfer
 from concourse.mybir import AluOpType as A, ActivationFunctionType as AF
 
-EXW = ["0", "1", "2", "3"]
-EXO = ["i", "2", "3"]
-NREP = {"0": (2, 1), "1": (1, 1), "2": (1, 1), "3": (1, 1)}
-FREE = ["LW0", "LOi", "LW1", "LO2", "LO3"]
+EX = {"LOi": (256, "relay", False), "LW0": (256, "relay", False), "LW1": (256, "relay", True), "LO2": (128, "relay", True),
+      "LW2": (256, "relay", True), "LO3": (128, "relay", True), "LW3": (256, "relay", True)}
 BIG = 2.0 ** 23
-MATB = (["REP%d" % p for p in range(4)] + ["YM", "E8", "GT", "ENT0", "ENT1", "KEEPN", "ANY0", "ANY1", "KX0", "KX1", "KN0", "KN1", "IB",
-        "TMN", "TMP", "ONES", "PERM64", "PERM1", "OXH0", "OXH1", "OXL0", "OXL1"]
-        + ["ICO%d" % f for f in range(6)] + ["INV%d" % f for f in range(5)])
-MATF = ["REPF%d" % p for p in range(4)] + ["CH0", "CH1", "SW", "NSW", "ISW", "INVF"]
+MAGIC = 1.5 * 2.0 ** 17
+EMPTY = 4096.0
+MATB = (["REP%d" % p for p in range(4)] + ["YM", "ENT0", "ENT1", "KEEPN", "ANY0", "ANY1", "KX0", "KX1", "KN0", "KN1", "IB",
+        "TMN", "CM", "ONES", "PERM64", "PERM65", "PERM1", "OXH0", "OXH1", "OXB0", "OXB1", "OXL0", "OXL1", "INV0", "INV1"])
+MATF = ["CH0", "CH1", "SW", "NSW", "ISWH", "INVF", "INVF2"]
+MATH = ["RW0", "RW1", "KP00", "KP01", "KP10", "KP11"]
 SLID = ["OTH", "BKO"] + ["BD%d" % d for d in range(6)]
 DELTA = [1, -1, 2, -2, 3, -3]
-F, B16, I32, U16 = "float32", "bfloat16", "int32", "uint16"
+F, B16, H16, I32, U16 = "float32", "bfloat16", "float16", "int32", "uint16"
 SCRATCH = {}
-for _n, _w, _d in (("W", 8200, F), ("OT", 8208, B16), ("MBF", 128 * len(MATB), B16), ("MFF", 128 * len(MATF), F), ("MSL", 144 * len(SLID) + 160, B16),
-                   ("CI", 16, I32), ("CF", 64, F), ("XI", 144, F), ("MI", 128, I32), ("MF", 768, I32), ("MKI", 1152, I32), ("MK", 1152, B16),
-                   ("RS", 640, F), ("ST", 256, I32), ("OI", 128, I32), ("FI", 896, I32), ("FB", 896, B16), ("HB", 128, B16), ("OF", 128, F),
-                   ("OL", 128, U16), ("XE0", 1024, F), ("XE1", 1024, F), ("GM", 1024, B16), ("KL", 128, U16), ("KC", 64, F), ("HAS", 64, F),
-                   ("U", 1024, F), ("VO", 1024, B16), ("VX", 1024, B16), ("C", 1024, B16), ("R1", 64, F), ("REV", 64, B16), ("ND", 64, F),
-                   ("NH", 64, F), ("FF", 64, F), ("FK", 64, F), ("KEEP", 64, B16), ("OK", 64, F), ("CL", 32, U16), ("E", 512, B16),
-                   ("OXA", 128, B16), ("HN", 64, B16), ("U5", 1024, F), ("MX", 1024, F), ("OWNW", 128, F), ("M1", 128, I32), ("M2", 128, I32),
-                   ("NF", 128, F), ("YW0", 128, F), ("YW1", 128, F), ("YI", 64, I32), ("YFI", 320, I32), ("YFB", 320, B16), ("YO0", 64, F),
-                   ("YO1", 64, F), ("LW0", 1024, F), ("LW1", 1024, F), ("LW2", 1024, F), ("LW3", 1024, F), ("LOi", 2048, B16), ("LO2", 1024, B16),
-                   ("LO3", 1024, B16)):
+for _n, _w, _d in (("W", 8256, F), ("OT", 8256, B16), ("MBF", 128 * len(MATB), B16), ("MFF", 128 * len(MATF), F), ("MHF", 128 * len(MATH), H16),
+                   ("MSL", 144 * len(SLID) + 160, B16),
+                   ("CI", 16, I32), ("CF", 80, F), ("XI", 144, B16), ("MF", 768, B16), ("MKI", 1152, B16), ("MK", 1152, B16),
+                   ("RS", 640, B16), ("R32", 160, B16), ("ST", 256, I32), ("OI", 128, I32), ("FI", 384, I32), ("FB", 384, B16), ("OF", 128, F),
+                   ("OL", 128, U16), ("XL", 64, U16), ("XE0", 1024, F), ("XE1", 1024, F), ("GM", 1024, B16), ("KL", 128, U16), ("KC", 64, F),
+                   ("HAS", 64, F), ("U", 1024, F), ("VO", 1024, B16), ("VX", 1024, B16), ("C", 1024, B16), ("R1", 64, F), ("REV", 64, B16),
+                   ("ND", 64, F), ("NH", 64, F), ("FF", 64, F), ("FK", 64, F), ("KEEP", 64, B16), ("OK", 64, F), ("CL", 32, U16), ("E", 512, B16),
+                   ("OXA", 128, B16), ("HN", 64, B16), ("U5", 1024, F), ("MX", 1024, F), ("OWNW", 128, F), ("M1", 128, F),
+                   ("HI", 256, H16), ("LO", 256, H16), ("YW0", 128, F), ("YW1", 128, F), ("YI", 64, I32), ("YFI", 64, I32), ("YFB", 128, B16),
+                   ("YO0", 64, F), ("YO1", 64, F), ("LW0", 2048, H16), ("LW1", 2048, H16), ("LW2", 2048, H16), ("LW3", 2048, H16),
+                   ("LOi", 2048, B16), ("LO2", 1024, B16), ("LO3", 1024, B16)):
     SCRATCH[_n] = ("sbuf", [128, _w], _d)
 for _n in ("K0", "K1", "RV", "DD", "YY", "NP", "UP"):
     SCRATCH[_n] = ("psum", [128, 1024 if _n == "UP" else 512], F)
 SEMAPHORES = (["sV", "sS", "sP", "sG", "dOI", "dST"]
-              + [k + "W" + x for x in EXW for k in ("p", "m", "l", "f")] + [k + "O" + x for x in EXO for k in ("p", "m", "l", "f")]
-              + ["dW%s%d" % (x, h) for x in EXW for h in (0, 1)] + ["dY0", "dY1", "dO0", "dO1"])
+              + [k + x for x in EX for k in ("p0", "p1", "p2", "p3", "q0", "q1", "q2", "q3", "m", "n", "l", "f")]
+              + ["dY0", "dY1", "dO0", "dO1"])
 
 
 def rank_program(g, core, T, topo):
@@ -37,12 +38,12 @@ def rank_program(g, core, T, topo):
     if rank is None:
         return
     cores = list(T.cores)
-    side = [int(topo.die(c) != topo.die(cores[0])) for c in cores]
-    slot = [4 * side[r] + sum(1 for q in range(r) if side[q] == side[r]) for r in range(len(cores))]
-    assert slot == [4 * (r & 1) + (r >> 1) for r in range(len(cores))]
-    me, half = slot[rank], side[rank]
-    peers = [c for r, c in enumerate(cores) if side[r] == half and c != core]
-    mate = [c for c in cores if c != core and topo.chip(c) == topo.chip(core)][0]
+    same = [r for r in range(len(cores)) if topo.die(cores[r]) == topo.die(core)]
+    other = [r for r in range(len(cores)) if topo.die(cores[r]) != topo.die(core)]
+    idx = same.index(rank)
+    mate = cores[other[idx]]
+    assert topo.chip(mate) == topo.chip(core) and len(same) == len(other) == 4
+    at = [same[(idx - j) % 4] for j in range(4)] + [other[(idx - j) % 4] for j in range(4)]
     eng = {"V": g.vector, "S": g.scalar, "P": g.tensor, "G": g, "Y": g.sync}
     cnt, known, clk, wr, rd, bk, toks_all = {q: 0 for q in eng}, {q: {} for q in eng}, {}, {}, {}, {}, {}
 
@@ -112,6 +113,9 @@ def rank_program(g, core, T, topo):
         else:
             emit("S", [lambda: g.scalar.activation(out=out, in_=i, func=AF.Copy)], R, W, B)
 
+    def act(out, i, scale, bias, R=(), W=(), B=()):
+        emit("S", [lambda: g.scalar.activation(out=out, in_=i, func=AF.Identity, bias=bias, scale=scale)], R, W, B)
+
     def sc(dst, src, scale, R, W):
         emit("S", [lambda: g.scalar.activation(out=dst, in_=src, func=AF.Copy, scale=float(scale))], R, W)
 
@@ -126,12 +130,19 @@ def rank_program(g, core, T, topo):
         j = MATF.index(n)
         return T.MFF[:, 128 * j:128 * j + 128]
 
+    def MH(n):
+        j = MATH.index(n)
+        return T.MHF[:, 128 * j:128 * j + 128]
+
     def SL(n, q=None):
         j = 4 if n == "OWN" else 160 + 144 * SLID.index(n)
         return T.MSL[:, j:j + 144] if q is None else T.MSL[:, j + 15 - q:j + 143 - q]
 
+    def place(r, b):
+        return 64 * (8 * r + 65 * b)
+
     dmas("Y", [(T.OI[:], T.opts[:])], "dOI", (), ["OI"])
-    for q, r0, src in (("Y", 0, T.lw), ("S", 16, T.rw)):
+    for q, r0, src in (("Y", 16, T.lw), ("S", 0, T.rw)):
         for P in range(4):
             for h in (0, 1):
                 eng[q].dma_start(out=T.ST[32 * P + r0:32 * P + r0 + 16, 128 * h:128 * h + 128],
@@ -139,13 +150,25 @@ def rank_program(g, core, T, topo):
     arrive("dST", 16 * 16, ["ST"])
     emit("G", [lambda: g.iota(T.CI[:, 0:1], [[0, 1]], 0, 1)], (), ["ci0"])
     emit("G", [lambda: g.iota(T.XI[:], [[1, 144]], 0, 0, allow_small_or_imprecise_dtypes=True)], (), ["XI"])
-    emit("G", [lambda: g.iota(T.MI[:], [[1, 128]], 0, 0)], (), ["MI"])
-    emit("G", [lambda: g.iota(T.MKI[:], [[0, 9], [1, 8], [0, 16]], 0, 0)], (), ["MKI"])
-    ints = [("P", 5, 7), ("rho", 4, 1), ("grp", 4, 15), ("i", 0, 15), ("s", 0, 7), ("h3", 3, 1), ("blk", 3, 31), ("b0", 0, 1), ("b1", 1, 1)]
-    for j, (n, sh, m) in enumerate(ints):
-        ts(T.CI[:, j + 1:j + 2], T.CI[:, 0:1], sh, A.logical_shift_right, m, A.bitwise_and, ["ci0"], ["ci%d" % (j + 1)])
+    flds = [("f31", [[0, 4], [1, 32]]), ("f8", [[1, 16], [0, 8]]), ("f16", [[1, 8], [0, 16]]), ("f119", [[16, 8], [0, 2], [1, 8]]),
+            ("f4", [[1, 32], [0, 4]]), ("f111", [[32, 4], [0, 2], [1, 16]])]
+
+    def fld(n):
+        j = [x[0] for x in flds].index(n)
+        return T.MF[:, 128 * j:128 * j + 128]
+
+    for n, pat in flds:
+        emit("G", [lambda: g.iota(fld(n), pat, 0, 0, allow_small_or_imprecise_dtypes=True)], (), [n])
+    ints = [("P", 5, 7), ("rho", 4, 1), ("s", 0, 7), ("h3", 3, 1), ("i", 0, 15), ("k6", 6, 1), ("grp", 4, 15), ("blk", 3, 31), ("b0", 0, 1),
+            ("b1", 1, 1), ("k31", 0, 31), ("b5", 5, 1)]
     names = ["k"] + [x[0] for x in ints]
-    cp("V", T.CF[:, 0:10], T.CI[:, 0:10], ["ci%d" % j for j in range(10)], ["c_" + n for n in names])
+
+    def colints(lo, hi):
+        for j in range(lo, hi):
+            n, sh, m = ints[j]
+            ts(T.CI[:, j + 1:j + 2], T.CI[:, 0:1], sh, A.logical_shift_right, m, A.bitwise_and, ["ci0"], ["ci%d" % (j + 1)])
+        a = lo + 1 if lo else 0
+        cp("V", T.CF[:, a:hi + 1], T.CI[:, a:hi + 1], ["ci%d" % j for j in range(a, hi + 1)], ["c_" + n for n in names[a:hi + 1]])
 
     def col(n):
         j = names.index(n)
@@ -156,7 +179,7 @@ def rank_program(g, core, T, topo):
         d = add if not isinstance(add, str) else col(add)
         R = ["c_" + a] + (["c_" + add] if isinstance(add, str) else [])
         if q == "S":
-            emit("S", [lambda: g.scalar.activation(out=col(n), in_=col(a), func=AF.Identity, bias=d, scale=float(m))], R, ["c_" + n])
+            act(col(n), col(a), float(m), d, R, ["c_" + n])
         else:
             ts(col(n), col(a), float(m), A.mult, d, A.add, R, ["c_" + n])
 
@@ -164,212 +187,208 @@ def rank_program(g, core, T, topo):
         ts(dst, f, col(h), A.is_equal, w if wn is None else col(wn), A.mult, [fr, "c_" + h] + ([] if wn is None else ["c_" + wn]), [name])
 
     Xm, Xs = T.XI[:, 0:128], T.XI[:]
-    lin("sgn", "rho", 2, -1.0, "V")
-    lin("ntemp", "i", -1024, 0.0, "V")
-    ico = [1.0, 63.0, 12.0, -8.0, -30.0, -1.0]
-    mat(MB("IB"), "IB", Xm, "XI", "k", 1.0)
-    for j in range(1, 6):
-        sc(MB("ICO%d" % j), MB("IB"), ico[j], ["IB"], ["ICO%d" % j])
+    colints(0, 6)
     lin("X0", "P", 32, "s", "V")
-    lin("OXn", "h3", 16, "X0", "V")
     lin("n0", "rho", -1, 1.0, "V")
-    for h in (0, 1):
-        mat(MB("OXH%d" % h), "OXH%d" % h, Xm, "XI", "OXn", None, ["n0", "rho"][h])
-    fi = [(6, 255), (6, 1), (8, 3), (10, 1), (11, 3), (7, 1), (0, 63)]
-    for j, (sh, m) in enumerate(fi):
-        ts(T.FI[:, 128 * j:128 * j + 128], T.OI[:], sh, A.logical_shift_right, m, A.bitwise_and, ["OI"], ["FI%d" % j])
-
-    def own_walls(b):
-        for h in (0, 1):
-            ts(T["LW%d" % b][:, 128 * me + 64 * h:128 * me + 64 * h + 64], T.ST[:, 128 * h + 64 * b:128 * h + 64 * b + 64], col("sgn"), A.mult,
-               col("ntemp"), A.add, ["ST", "c_sgn", "c_ntemp"], ["LW%do%d" % (b, h)])
-
-    def send(x, kind, buf, w):
-        blk = T[buf][:, w * me:w * me + w]
-        pre("G", [kind + x + "o0", kind + x + "o1"], [])
-        tag = buf[1] + x
-        ids = [DstId(rid=topo.addr(c)[0], pnc=topo.addr(c)[1]) for c in peers]
-        g.remote_dma_fused([RemoteDMATransfer(dst_ids=ids, dma_engine_mask=topo.mask(core, peers[0]), remote_sem=T.sem["p" + tag], srcs=[blk],
-                                              dsts=[blk for c in peers])], local_sem=T.sem["l" + tag])
-        ne = len(topo.engines(core, peers[0]))
-        toks_all["l" + tag] = ne
-        arrive("p" + tag, len(peers) * ne, [kind + x + "p"])
-
-    def forward(x, kind, buf, w):
-        pre("G", [kind + x + "o0", kind + x + "o1", kind + x + "p"], [])
-        tag = buf[1] + x
-        blk = T[buf][:, 4 * w * half:4 * w * half + 4 * w]
-        es = topo.engines(core, mate)
-        if kind + x in FREE:
-            es = [e for e in es if e not in topo.engines(core, peers[0])]
-        g.remote_dma(blk, blk, T.sem["m" + tag], T.sem["f" + tag], topo.addr(mate)[1], topo.addr(mate)[0], sum(1 << e for e in es))
-        toks_all["f" + tag] = len(es)
-        arrive("m" + tag, len(es), [kind + x + "m"])
-
-    def have(kind, x, h):
-        return [kind + x + "o0", kind + x + "o1", kind + x + "p"] if h == half else [kind + x + "m"]
-
-    own_walls(0)
-    send("0", "LW", "LW0", 128)
-    flds = [("f8", 3, 31), ("f16", 4, 15), ("f31", 0, 31), ("f15", 0, 15), ("f119", 0, 119), ("f4", 2, 31)]
-
-    def fld(n):
-        j = [x[0] for x in flds].index(n)
-        return T.MF[:, 128 * j:128 * j + 128]
-
-    cp("V", T.FB[:, 0:768], T.FI[:, 0:768], ["FI%d" % j for j in range(6)], ["FB"])
-    mms([(T.K0[:, 0:128], MB("ICO%d" % j) if j else MB("IB"), T.FB[:, 128 * j:128 * j + 128], j == 0, j == 5) for j in range(6)],
-        ["FB", "IB"] + ["ICO%d" % j for j in range(1, 6)], ["K0.h"], ["K0"])
-    cp("V", T.FB[:, 768:896], T.FI[:, 768:896], ["FI6"], ["FB6"])
-    lin("OXl", "OXn", 1, 8.0, "V")
-    for h in (0, 1):
-        mat(MB("OXL%d" % h), "OXL%d" % h, Xm, "XI", "OXl", None, ["n0", "rho"][h])
-    cp("V", T.HB[:], T.K0[:, 0:128], ["K0.h"], ["HB"], ["K0"])
-    low = T.FB[:, 768:896]
-    for h, bank in ((0, "RV"), (1, "NP")):
-        mms([(T[bank][:, 0:128], MB("OXH%d" % h), T.HB[:], True, False), (T[bank][:, 0:128], MB("OXL%d" % h), low, False, True)],
-            ["HB", "FB6", "OXH%d" % h, "OXL%d" % h], [bank + ".x"], [bank])
-    for h, bank in ((0, "RV"), (1, "NP")):
-        for b in (0, 1):
-            c0 = 256 * me + 128 * b + 64 * h
-            cp("V" if h == 0 else "S", T.LOi[:, c0:c0 + 64], T[bank][:, 64 * b:64 * b + 64], [bank + ".x"], ["LOio%d" % h + ("b" if b else "")], [bank])
-    for h in (0, 1):
-        wr["LOio%d" % h] = wr["LOio%d" % h] + wr["LOio%db" % h]
-    own_walls(1)
-    send("i", "LO", "LOi", 256)
-    send("1", "LW", "LW1", 128)
-    forward("0", "LW", "LW0", 128)
-    forward("i", "LO", "LOi", 256)
-    forward("1", "LW", "LW1", 128)
-    lin("pa", "h3", -16, "X0")
-    lin("pb", "rho", 8, "pa")
-    lin("PERMh", "pb", 1, 16.0)
-    mat(MB("PERM1"), "PERM1", Xm, "XI", "PERMh", 1.0)
-    sc(MB("PERM64"), MB("PERM1"), 64.0, ["PERM1"], ["PERM64"])
-    mms([(T.K1[:, 0:128], MB("PERM64"), T.HB[:], True, False), (T.K1[:, 0:128], MB("PERM1"), low, False, True)],
-        ["HB", "FB6", "PERM64", "PERM1"], ["K1.o"], ["K1"])
-    cp("V", T.OF[:], T.K1[:, 0:128], ["K1.o"], ["OF0", "OF1"], ["K1"])
-    cp("V", T.OL[:], T.OF[:], ["OF0", "OF1"], ["OL0", "OL1"])
-    for j, (n, sh, m) in enumerate(flds):
-        ts(fld(n), T.MI[:], sh, A.logical_shift_right, m, A.bitwise_and, ["MI"], [n])
-    for p in range(4):
-        lin("kr%d" % p, "k", 1, -32.0 * p)
-        mat(MB("REP%d" % p), "REP%d" % p, fld("f31"), "f31", "kr%d" % p, 1.0)
-        if p >= 2:
-            sc(MX("REPF%d" % p), MB("REP%d" % p), 1.0, ["REP%d" % p], ["REPF%d" % p])
-    emit("V", [lambda: g.vector.memset(T.W[:, 8192:8200], -BIG)], (), ["Wz"])
-    lin("sent", "h3", -128, 128.0)
-    emit("V", [lambda: g.vector.memset(MB("ONES"), 1.0)], (), ["ONES"])
-    ones = 128 * MATB.index("ONES")
-    ts(T.OT[:, 8192:8208], T.MBF[:, ones:ones + 16], col("sent"), A.mult, None, None, ["ONES", "c_sent"], ["OTz"])
-    ts(T.MK[:], T.MKI[:], col("s"), A.is_equal, None, None, ["MKI", "c_s"], ["MK"])
-    lin("own15", "grp", 16, 15.0)
-    lin("w64", "h3", -63, 64.0)
-    mat(SL("BKO"), "BKO", Xs, "XI", "own15", None, "w64")
+    lin("OXn", "h3", 16, "X0", "V")
     lin("sa", "rho", -32, "k")
     lin("SWh", "sa", 1, 16.0)
-    mat(MX("SW"), "SW", Xm, "XI", "SWh", 1.0)
+    lin("KP0", "k6", -64, "SWh")
+    lin("KP1", "KP0", 1, 64.0)
+    lin("wa0", "k6", 1, -1.0)
+    lin("wa1", "k6", -1, 0.0)
+    lin("sg64", "rho", 2.0 / 64, -1.0 / 64)
+    lin("t64", "i", 16, 0.0)
+    lin("OXl", "OXn", 1, 8.0, "V")
+    colints(6, len(ints))
+    for h in (0, 1):
+        mat(MB("OXH%d" % h), "OXH%d" % h, Xm, "XI", "OXn", None, ["n0", "rho"][h])
+        sc(MB("OXB%d" % h), MB("OXH%d" % h), 65.0, ["OXH%d" % h], ["OXB%d" % h])
+    for h in (0, 1):
+        mat(MB("OXL%d" % h), "OXL%d" % h, Xm, "XI", "OXl", None, ["n0", "rho"][h])
+    for a in (0, 1):
+        for hl in (0, 1):
+            mat(MH("KP%d%d" % (a, hl)), "KP%d%d" % (a, hl), Xm, "XI", "KP%d" % hl, None, "wa%d" % a)
+    for p in range(4):
+        lin("kr%d" % p, "k", 1, -32.0 * p)
+    for n, a, m, add in (("nb5", "b5", -1, 1.0), ("pa", "h3", -16, "X0"), ("pb", "rho", 8, "pa"), ("PERMh", "pb", 1, 16.0), ("xa", "P", 128, 0.0),
+                         ("xb", "h3", 64, "xa"), ("sent", "h3", -64, 64.0), ("own15", "grp", 16, 15.0), ("w64", "h3", -63, 64.0)):
+        lin(n, a, m, add)
+    for j, (sh, m) in enumerate([(7, 127), (6, 1), (0, 63)]):
+        ts(T.FI[:, 128 * j:128 * j + 128], T.OI[:], sh, A.logical_shift_right, m, A.bitwise_and, ["OI"], ["FI%d" % j])
+    cp("V", T.FB[:], T.FI[:], ["FI0", "FI1", "FI2"], ["FB"])
 
-    def late():
-        emit("V", [lambda: g.vector.memset(T.MSL[:, 0:4], 0.0), lambda: g.vector.memset(T.MSL[:, 148:160], 0.0)], (), ["GUARD"])
-        mat(SL("OWN"), "OWN", Xs, "XI", "own15", 1.0)
-        lin("ot", "rho", -32, "own15")
-        lin("oth15", "ot", 1, 16.0)
-        mat(SL("OTH"), "OTH", Xs, "XI", "oth15", 1.0)
-        sc(T.MX[:, 0:152], T.MSL[:, 0:152], 32.0, ["OWN", "GUARD"], ["MX0"])
-        for j, d in enumerate(DELTA):
-            k0 = 160 + 144 * SLID.index("BD%d" % j)
-            tt(T.MSL[:, k0:k0 + 144], T.MX[:, 4:148], T.MSL[:, 4 - d:148 - d], A.subtract, ["MX0", "OWN", "GUARD"], ["BD%d" % j])
-        lin("thr1", "b0", 1, -0.5)
-        lin("thr2", "b1", 1, -0.5)
-        mat(MB("E8"), "E8", fld("f8"), "f8", "blk", -2.0)
-        ts(MB("GT"), Xm, col("k"), A.is_gt, None, None, ["XI", "c_k"], ["GT"])
-        tt(MB("E8"), MB("E8"), MB("GT"), A.mult, ["GT"], ["E8"])
-        tt(MB("YM"), MB("E8"), MB("IB"), A.add, ["E8", "IB"], ["YM"])
-        lin("bf", "rho", -4, "blk")
-        lin("blkf", "bf", 1, 2.0)
-        lin("bl2", "blkf", 2, 0.0)
-        lin("bl3", "blkf", 2, 1.0)
-        mat(MX("CH0"), "CH0", fld("f4"), "f4", "bl2", 1.0)
-        mat(MX("CH1"), "CH1", fld("f4"), "f4", "bl3", 1.0)
-        lin("ta", "rho", -16, "X0")
-        lin("T0", "ta", 1, 16.0)
-        lin("T8", "ta", 1, 24.0)
-        lin("g0", "h3", -1, 1.0)
-        lin("a0", "g0", -BIG, 0.0)
-        lin("a1", "h3", -BIG, 0.0)
-        lin("temp", "i", 1024, 0.0)
-        mat(MB("ENT0"), "ENT0", Xm, "XI", "T0", None, "w64")
-        mat(MB("ENT1"), "ENT1", Xm, "XI", "T8", None, "w64")
-        for h, gn in ((0, "g0"), (1, "h3")):
-            mat(MB("ANY%d" % h), "ANY%d" % h, fld("f16"), "f16", "grp", None, "a%d" % h)
-            mat(MB("KX%d" % h), "KX%d" % h, fld("f119"), "f119", "T0", None, gn)
+    def dst(cs):
+        return [DstId(rid=topo.addr(c)[0], pnc=topo.addr(c)[1]) for c in cs]
+
+    eo = topo.engines(core, cores[same[(idx + 1) % 4]])
+    es = [e for e in topo.engines(core, mate) if e not in eo]
+
+    def blocks(x, j0, j1):
+        return T[x][:, EX[x][0] * j0:EX[x][0] * j1]
+
+    def send(x):
+        w, mode, apart = EX[x]
+        pre("G", [x + "s0"], [])
+        to = [cores[same[(idx + j) % 4]] for j in (1, 2, 3)]
+        trs = [RemoteDMATransfer(dst_ids=dst(to), dma_engine_mask=topo.mask(core, to[0]), remote_sem=T.sem["p%d%s" % (idx, x)],
+                                 srcs=[blocks(x, 0, 1)], dsts=[blocks(x, j, j + 1) for j in (1, 2, 3)])]
+        if apart:
+            trs.append(RemoteDMATransfer(dst_ids=dst([mate]), dma_engine_mask=sum(1 << e for e in es), remote_sem=T.sem["m" + x],
+                                         srcs=[blocks(x, 0, 1)], dsts=[blocks(x, 4, 5)]))
+            arrive("m" + x, len(es), [x + "s4"])
+        g.remote_dma_fused(trs, local_sem=T.sem["l" + x])
+        toks_all["l" + x] = len(eo) + (len(es) if apart else 0)
+        for j in (1, 2, 3):
+            arrive("p%d%s" % ((idx - j) % 4, x), len(eo), [x + "s%d" % j])
+        if mode == "direct":
+            to = [cores[other[(idx + j) % 4]] for j in (1, 2, 3)]
+            g.remote_dma_fused([RemoteDMATransfer(dst_ids=dst(to), dma_engine_mask=topo.mask(core, to[0]), remote_sem=T.sem["q%d%s" % (idx, x)],
+                                                  srcs=[blocks(x, 0, 1)], dsts=[blocks(x, 4 + j, 5 + j) for j in (1, 2, 3)])], local_sem=T.sem["f" + x])
+            toks_all["f" + x] = len(eo)
+            for j in (1, 2, 3):
+                arrive("q%d%s" % ((idx - j) % 4, x), len(eo), [x + "s%d" % (4 + j)])
+
+    def forward(x, free):
+        w, mode, apart = EX[x]
+        if mode == "direct":
+            return
+        j0 = 1 if apart else 0
+        pre("G", [x + "s%d" % j for j in range(j0, 4)], [])
+        e = es if free else topo.engines(core, mate)
+        g.remote_dma(blocks(x, 4 + j0, 8), blocks(x, j0, 4), T.sem["n" + x], T.sem["f" + x], topo.addr(mate)[1], topo.addr(mate)[0], sum(1 << k for k in e))
+        toks_all["f" + x] = len(e)
+        arrive("n" + x, len(e), [x + "s%d" % j for j in range(4 + j0, 8)])
+
+    fa, fb, low = T.FB[:, 0:128], T.FB[:, 128:256], T.FB[:, 256:384]
+    for h, bank in ((0, "RV"), (1, "NP")):
+        mms([(T[bank][:, 0:128], MB("OXH%d" % h), fa, True, False), (T[bank][:, 0:128], MB("OXB%d" % h), fb, False, False),
+             (T[bank][:, 0:128], MB("OXL%d" % h), low, False, True)], ["FB", "OXH%d" % h, "OXB%d" % h, "OXL%d" % h], [bank + ".x"], [bank])
+    for h, bank in ((0, "RV"), (1, "NP")):
+        for b in (0, 1):
+            c0 = 128 * b + 64 * h
+            cp("V" if h == 0 else "S", T.LOi[:, c0:c0 + 64], T[bank][:, 64 * b:64 * b + 64], [bank + ".x"], ["LOio%d%d" % (h, b)], [bank])
+    wr["LOis0"] = sum((wr["LOio%d%d" % (h, b)] for h in (0, 1) for b in (0, 1)), [])
+    send("LOi")
+
+    def pack(x, cols):
+        ms = []
+        for a in (0, 1):
+            for o, i, n in cols:
+                ms += [(T.UP[:, 128 * a + o:128 * a + o + n], MH("KP%d0" % a), T.HI[:, i:i + n], True, False),
+                       (T.UP[:, 128 * a + o:128 * a + o + n], MH("KP%d1" % a), T.LO[:, i:i + n], False, True)]
+        mms(ms, ["HI", "LO", "KP00", "KP01", "KP10", "KP11"], ["UPa.r"], ["UPa"])
+        cp("V", blocks(x, 0, 1), T.UP[:, 0:256], ["UPa.r"], [x + "s0"], ["UPa"])
+
+    ts(T.HI[:], T.ST[:], col("sg64"), A.mult, col("t64"), A.add, ["ST", "c_sg64", "c_t64"], ["HI"])
+    ts(T.K0[:, 256:512], T.ST[:], col("sg64"), A.mult, col("t64"), A.add, ["ST", "c_sg64", "c_t64"], ["K0.y"], ["K0"])
+    tt(T.LO[:], T.K0[:, 256:512], T.HI[:], A.subtract, ["K0.y", "HI"], ["LO"], ["K0"])
+    for b in (0, 1):
+        pack("LW%d" % b, [(64 * h, 128 * h + 64 * b, 64) for h in (0, 1)])
+        send("LW%d" % b)
+    emit("G", [lambda: g.iota(T.MKI[:], [[0, 9], [1, 8], [0, 16]], 0, 0, allow_small_or_imprecise_dtypes=True)], (), ["MKI"])
+    forward("LOi", True)
+    forward("LW0", True)
+    forward("LW1", False)
+    for n, a, m, add in (("ot", "rho", -32, "own15"), ("oth15", "ot", 1, 16.0), ("thr1", "b0", 1, -0.5), ("thr2", "b1", 1, -0.5), ("bf", "rho", -4, "blk"),
+                         ("blkf", "bf", 1, 2.0), ("bl2", "blkf", 2, 0.0), ("bl3", "blkf", 2, 1.0), ("ta", "rho", -16, "X0"), ("T0", "ta", 1, 16.0),
+                         ("T8", "ta", 1, 24.0), ("g0", "h3", -1, 1.0), ("a0", "g0", -BIG, 0.0), ("a1", "h3", -BIG, 0.0), ("k111", "rho", -16, "k")):
+        lin(n, a, m, add)
+    for p in range(4):
+        mat(MB("REP%d" % p), "REP%d" % p, fld("f31"), "f31", "kr%d" % p, 1.0)
+    for p in (0, 1):
+        mat(MH("RW%d" % p), "RW%d" % p, fld("f31"), "f31", "k31", None, ["nb5", "b5"][p])
+
+    OTALL = ["OTz"] + ["OT%d%d" % (b, r) for b in (0, 1) for r in range(8)]
+    WALL = ["Wz"] + ["W%d%d" % (b, r) for b in (0, 1) for r in range(8)]
+    rb = [("UP", 0, "UPa"), ("UP", 512, "UPb"), ("YY", 0, "YY"), ("DD", 0, "DD"), ("RV", 0, "RV"), ("NP", 0, "NP")]
+    nb = [0]
+
+    def rep(x, j, b, q):
+        buf, c0, bank = rb[nb[0] % len(rb)]
+        nb[0] += 1
+        w, d0 = EX[x][0], place(at[j], b)
+        if x[1] == "O":
+            s0 = w * j + (128 * b if x == "LOi" else 0)
+            ms = [(T[buf][:, c0 + 128 * p:c0 + 128 * p + 128], MB("REP%d" % p), T[x][:, s0:s0 + 128], True, True) for p in range(4)]
+            mr, tab, reg = ["REP%d" % p for p in range(4)], T.OT, "OT"
+        else:
+            ms = [(T[buf][:, c0 + 128 * p:c0 + 128 * p + 128], MH("RW%d" % (p & 1)), T[x][:, w * j + 128 * (p >> 1):w * j + 128 * (p >> 1) + 128], True, True)
+                  for p in range(4)]
+            mr, tab, reg = ["RW0", "RW1"], T.W, "W"
+        mms(ms, [x + "s%d" % j] + mr, [bank + ".r"], [bank])
+        cp(q, tab[:, d0:d0 + 512], T[buf][:, c0:c0 + 512], [bank + ".r"], ["%s%d%d" % (reg, b, at[j])], [bank])
+
+    def expand(b):
+        d0 = place(rank, b)
+        emit("S", [lambda: g.scalar.activation(out=T["XE%d" % b][:], in_=T.W[:, d0:d0 + 512].indirect(T.XL[:]), func=AF.Copy)],
+             ["W%d%d" % (b, rank), "XL"], ["XE%d" % b])
+
+    mat(MB("PERM1"), "PERM1", Xm, "XI", "PERMh", 1.0)
+    mat(MB("PERM64"), "PERM64", Xm, "XI", "PERMh", 64.0)
+    mat(MB("PERM65"), "PERM65", Xm, "XI", "PERMh", 64.0 * 65)
+    rep("LW0", 0, 0, "S")
+    mms([(T.K1[:, 0:128], MB("PERM64"), fa, True, False), (T.K1[:, 0:128], MB("PERM65"), fb, False, False), (T.K1[:, 0:128], MB("PERM1"), low, False, True)],
+        ["FB", "PERM64", "PERM65", "PERM1"], ["K1.o"], ["K1"])
+    ts(T.XL[:], T.XI[:, 0:64], col("xb"), A.add, None, None, ["XI", "c_xb"], ["XL"])
+    expand(0)
+    rep("LW1", 0, 1, "S")
+    for b in (0, 1):
+        rep("LOi", 0, b, "S")
+    mat(MB("IB"), "IB", Xm, "XI", "k", 1.0)
+    emit("V", [lambda: g.vector.memset(T.W[:, 4096:4160], -BIG)], (), ["Wz"])
+    emit("V", [lambda: g.vector.memset(MB("ONES"), 1.0)], (), ["ONES"])
+    emit("V", [lambda: g.vector.memset(T.MSL[:, 0:4], 0.0), lambda: g.vector.memset(T.MSL[:, 148:160], 0.0)], (), ["GUARD"])
+    emit("V", [lambda: g.vector.memset(T.RS[:], 0.0)], (), ["RS"])
+    ones = 128 * MATB.index("ONES")
+    ts(T.OT[:, 4096:4160], T.MBF[:, ones:ones + 64], col("sent"), A.mult, None, None, ["ONES", "c_sent"], ["OTz"])
+    cp("V", T.OF[:], T.K1[:, 0:128], ["K1.o"], ["OF0", "OF1"], ["K1"])
+    emit("V", [lambda: g.vector.memset(T.RS[:, 0::8], -BIG)], (), ["RS"])
+    mat(SL("BKO"), "BKO", Xs, "XI", "own15", None, "w64")
+    cp("V", T.OL[:], T.OF[:], ["OF0", "OF1"], ["OL0", "OL1"])
+    mat(SL("OWN"), "OWN", Xs, "XI", "own15", 1.0)
+    mat(T.R32[:, 4:148], "R32", Xs, "XI", "own15", 32.0)
+    mat(SL("OTH"), "OTH", Xs, "XI", "oth15", 1.0)
+    mat(MX("SW"), "SW", Xm, "XI", "SWh", 1.0)
+    mat(MX("NSW"), "NSW", Xm, "XI", "SWh", -1.0)
+    mat(MB("YM"), "YM", fld("f8"), "f8", "blk", -2.0)
+    emit("G", [lambda: g.affine_select(MB("YM"), MB("YM"), [[1, 128]], A.is_gt, 0.0, 0, -1)], ["YM"], ["YM"])
+    emit("G", [lambda: g.affine_select(MB("YM"), MB("YM"), [[1, 128]], A.not_equal, 1.0, 0, -1)], ["YM"], ["YM"])
+
+    def partners(js):
+        for j in js:
+            k0, d = 160 + 144 * SLID.index("BD%d" % j), DELTA[j]
+            tt(T.MSL[:, k0:k0 + 144], T.R32[:, 4:148], T.MSL[:, 4 - d:148 - d], A.subtract, ["R32", "OWN", "GUARD"], ["BD%d" % j])
+
+    partners((0, 1))
+    mat(MX("CH0"), "CH0", fld("f4"), "f4", "bl2", 1.0)
+    mat(MX("CH1"), "CH1", fld("f4"), "f4", "bl3", 1.0)
+    mat(MB("ENT0"), "ENT0", Xm, "XI", "T0", None, "w64")
+    mat(MB("ENT1"), "ENT1", Xm, "XI", "T8", None, "w64")
+    for h, gn in ((0, "g0"), (1, "h3")):
+        mat(MB("ANY%d" % h), "ANY%d" % h, fld("f16"), "f16", "grp", None, "a%d" % h)
+        mat(MB("KX%d" % h), "KX%d" % h, fld("f119"), "f119", "T0", None, gn)
+    mat(MX("ISWH"), "ISWH", fld("f111"), "f111", "k111", 0.5)
+    mat(MB("KEEPN"), "KEEPN", Xm, "XI", "k", -16384.0)
+    ts(T.MK[:], T.MKI[:], col("s"), A.is_equal, None, None, ["MKI", "c_s"], ["MK"])
 
     def late2():
-        tt(MX("ISW"), MX("SW"), MB("IB"), A.add, ["SW", "IB"], ["ISW"])
-        names.append("kz")
-        ts(col("kz"), col("k"), 0.0, A.is_equal, -1024.0, A.mult, ["c_k"], ["c_kz"])
-        ts(MB("TMN"), fld("f15"), col("kz"), A.mult, None, None, ["f15", "c_kz"], ["TMN"])
-        emit("V", [lambda: g.vector.memset(T.RS[:], 0.0)], (), ["RS"])
-        emit("V", [lambda: g.vector.memset(T.RS[:, 0::8], -BIG)], (), ["RS"])
-
-    def late2s():
-        sc(MB("KEEPN"), MB("IB"), -16384.0, ["IB"], ["KEEPN"])
         for h in (0, 1):
             sc(MB("KN%d" % h), MB("KX%d" % h), -256.0, ["KX%d" % h], ["KN%d" % h])
-        sc(MX("NSW"), MX("SW"), -1.0, ["SW"], ["NSW"])
-        sc(MB("TMP"), MB("TMN"), -1.0, ["TMN"], ["TMP"])
+        lin("nt64", "i", -16, 0.0)
+        lin("c8", "rho", 2.0 / 256, -1.0 / 256)
+        lin("tm", "i", 16, MAGIC)
+        lin("s64", "rho", 128, -64.0)
+        act(MB("TMN"), MB("IB"), col("nt64"), 0.0, ["IB", "c_nt64"], ["TMN"])
+        act(MB("CM"), MB("IB"), col("c8"), 0.0, ["IB", "c_c8"], ["CM"])
 
     def late3():
         lin("iv", "rho", -8, "OXn")
         lin("INVh", "iv", 1, 8.0)
         mat(MX("INVF"), "INVF", Xm, "XI", "INVh", 1.0)
-        for j, c in enumerate([-4032.0, -768.0, 512.0, 1920.0, 64.0]):
+        sc(MX("INVF2"), MX("INVF"), 2.0, ["INVF"], ["INVF2"])
+        for j, c in enumerate([-1.0, -8256.0]):
             sc(MB("INV%d" % j), MX("INVF"), c, ["INVF"], ["INV%d" % j])
-
-    OTALL = ["OTz"] + ["OT%d%d%d" % (b, p, h) for b in (0, 1) for p in range(4) for h in (0, 1)]
-    WALL = ["Wz"] + ["W%d%d%d" % (b, p, h) + z for b in (0, 1) for p in range(4) for h in (0, 1) for z in ("", "s")]
-    rb = [("UP", 0, "UPa"), ("UP", 512, "UPb"), ("YY", 0, "YY"), ("DD", 0, "DD")]
-    nb = [0]
-
-    def rep_o(x, b, h, qs):
-        for p in range(4):
-            buf, c0, bank = rb[nb[0] % 4]
-            nb[0] += 1
-            out = T[buf][:, c0:c0 + 512]
-            if x == "i":
-                ms = [(T[buf][:, c0 + 128 * j:c0 + 128 * j + 128], MB("REP%d" % p),
-                       T.LOi[:, 256 * (4 * h + j) + 128 * b:256 * (4 * h + j) + 128 * b + 128], True, True) for j in range(4)]
-            else:
-                ms = [(out, MB("REP%d" % p), T["LO" + x][:, 512 * h:512 * h + 512], True, True)]
-            mms(ms, have("LO", x, h) + ["REP%d" % p], [bank + ".r"], [bank])
-            d0 = 4096 * b + 1024 * p + 512 * h
-            cp(qs[p % len(qs)], T.OT[:, d0:d0 + 512], out, [bank + ".r"], ["OT%d%d%d" % (b, p, h)], [bank])
-
-    def rep_w_dma(x, b, h):
-        n = 4 - NREP[x][h != half]
-        dmas("Y", [(T.W[32 * pp:32 * pp + 32, 4096 * b + 1024 * p + 512 * h:4096 * b + 1024 * p + 512 * h + 512],
-                    T["LW" + x][32 * p:32 * p + 32, 512 * h:512 * h + 512]) for p in range(n) for pp in range(4) if pp != p],
-             "dW%s%d" % (x, h), have("LW", x, h) + (have("LO", "i", half) if x == "0" else []), ["W%d%d%d" % (b, p, h) for p in range(n)])
-
-    def rep_w_same(x, b, h, q):
-        for p in range(4 - NREP[x][h != half]):
-            d0 = 4096 * b + 1024 * p + 512 * h
-            cp(q, T.W[32 * p:32 * p + 32, d0:d0 + 512], T["LW" + x][32 * p:32 * p + 32, 512 * h:512 * h + 512], have("LW", x, h), ["W%d%d%ds" % (b, p, h)])
-
-    def rep_w_pe(x, b, h, q):
-        for p in range(4 - NREP[x][h != half], 4):
-            buf, c0, bank = rb[nb[0] % 4]
-            nb[0] += 1
-            out = T[buf][:, c0:c0 + 512]
-            mms([(out, MX("REPF%d" % p), T["LW" + x][:, 512 * h:512 * h + 512], True, True)], have("LW", x, h) + ["REPF%d" % p], [bank + ".r"], [bank])
-            d0 = 4096 * b + 1024 * p + 512 * h
-            cp(q, T.W[:, d0:d0 + 512], out, [bank + ".r"], ["W%d%d%d" % (b, p, h)], [bank])
-
-    def expand(x, b):
-        for q in range(16):
-            hh = q >> 3
-            cp("S", T["XE%d" % b][:, q::16], T["LW" + x][:, 128 * me + 64 * hh:128 * me + 64 * hh + 64], ["LW%so%d" % (x, hh)], ["XE%d.%d" % (b, q)])
 
     def lists_gather(t):
         b = t & 1
@@ -378,40 +397,44 @@ def rank_program(g, core, T, topo):
     def lists(t):
         b = t & 1
         mms([(T.K0[:, 0:64], SL("BKO", q), T.GM[:, q::16], q == 0, q == 15) for q in range(16)], ["GM", "BKO"], ["K0.k"], ["K0"])
-        ts(T.KC[:], T.K0[:, 0:64], -8192.0, A.add, None, None, ["K0.k"], ["KC"], ["K0"])
+        ts(T.HAS[:], T.OF[:, 64 * b:64 * b + 64], EMPTY, A.not_equal, None, None, ["OF%d" % b], ["HAS"])
+        ts(T.KC[:], T.K0[:, 0:64], -EMPTY, A.add, None, None, ["K0.k"], ["KC"], ["K0"])
         mms([(T.K1[:, 0:64], MX("SW"), T.KC[:], True, True)], ["KC", "SW"], ["K1.k"], ["K1"])
         cp("V", T.KL[:, 0:64], T.K0[:, 0:64], ["K0.k"], ["KL0"], ["K0"])
-        ts(T.HAS[:], T.OF[:, 64 * b:64 * b + 64], 8191.5, A.is_lt, None, None, ["OF%d" % b], ["HAS"])
-        ts(T.KL[:, 64:128], T.K1[:, 0:64], 8192.0, A.add, None, None, ["K1.k"], ["KL1"], ["K1"])
+
+    def lists2(t):
+        ts(T.KL[:, 64:128], T.K1[:, 0:64], EMPTY, A.add, None, None, ["K1.k"], ["KL1"], ["K1"])
 
     def fields(b):
-        cp("V", T.YI[:], T.OF[:, 64 * b:64 * b + 64], ["OF%d" % b], ["YI"])
-        for j, (sh, m) in enumerate([(12, 1), (10, 3), (9, 1), (7, 3), (6, 1)]):
-            ts(T.YFI[:, 64 * j:64 * j + 64], T.YI[:], sh, A.logical_shift_right, m, A.bitwise_and, ["YI"], ["YFI%d" % j])
-        cp("V", T.YFB[:], T.YFI[:], ["YFI%d" % j for j in range(5)], ["YFB"])
+        n = T.OF[:, 64 * b:64 * b + 64]
+        cp("V", T.YI[:], n, ["OF%d" % b], ["YI"])
+        ts(T.YFB[:, 64:128], n, EMPTY + 63.5, A.is_gt, None, None, ["OF%d" % b], ["YFB1"])
+        ts(T.YFI[:], T.YI[:], 63, A.bitwise_and, None, None, ["YI"], ["YFI"])
+        cp("V", T.YFB[:, 0:64], T.YFI[:], ["YFI"], ["YFB0"])
 
     def natural(b):
-        mms([(T.YY[:, 128:192], MX("INVF"), T.OF[:, 64 * b:64 * b + 64], True, False)]
-            + [(T.YY[:, 128:192], MB("INV%d" % j), T.YFB[:, 64 * j:64 * j + 64], False, j == 4) for j in range(5)],
-            ["OF%d" % b, "YFB", "INVF"] + ["INV%d" % j for j in range(5)], ["YY.n"], ["YY"])
+        mms([(T.YY[:, 128:192], MX("INVF2"), T.OF[:, 64 * b:64 * b + 64], True, False)]
+            + [(T.YY[:, 128:192], MB("INV%d" % j), T.YFB[:, 64 * j:64 * j + 64], False, j == 1) for j in range(2)],
+            ["OF%d" % b, "YFB0", "YFB1", "INVF2", "INV0", "INV1"], ["YY.n"], ["YY"])
         cp("S", T["YO%d" % b][:], T.YY[:, 128:192], ["YY.n"], ["YO%d" % b], ["YY"])
         dmas("Y", [(T.yo[:, 64 * b:64 * b + 64], T["YO%d" % b][:])], "dO%d" % b, ["YO%d" % b], [])
 
     def round_(t):
         b, m = t & 1, 1 + t
-        x = {0: "0", 1: "1", 2: "2"}[t]
         nx = {0: "2", 1: "3", 2: None}[t]
-        xe = ["XE%d.%d" % (b, q) for q in range(16)]
+        xe = ["XE%d" % b]
         Wt = T.W[:]
-        mine = "LW%so" % x
         ol = T.OL[:, 64 * b:64 * b + 64]
         emit("S", [lambda: g.scalar.activation(out=T.U[:], in_=Wt.indirect(ol), func=AF.Copy)], WALL + ["OL%d" % b], ["U"])
         cp("S", T.UP[:], T.U[:], ["U"], ["UPa.r", "UPb.r"], ["UPa", "UPb"])
         if t == 0:
-            late2s()
+            late2()
+        if t == 1:
+            expand(0)
         XE = T["XE%d" % b]
         tt(T.VO[:], Wt.indirect(T.KL[:, 0:64]), XE[:], A.is_gt, WALL + ["KL0"] + xe, ["VO"])
         mms([(T.RV[:, 0:64], SL("OWN", q), T.VO[:, q::16], q == 0, False) for q in range(16)], ["VO", "OWN"], ["RV.v"], ["RV"])
+        lists2(t)
         tt(T.VX[:], Wt.indirect(T.KL[:, 64:128]), XE[:], A.is_lt, WALL + ["KL1"] + xe, ["VX"])
         mms([(T.RV[:, 0:64], SL("OTH", q), T.VX[:, q::16], False, q == 15) for q in range(16)], ["VX", "OTH"], ["RV.v2"], ["RV"])
         st = {1: [(0, 1, 2)], 2: [(0, 2, 4), (1, 3, 4)], 3: [(0, 3, 4), (1, 2, 4)]}[m]
@@ -436,7 +459,7 @@ def rank_program(g, core, T, topo):
         tt(T.KEEP[:], T.NH[:], T.FF[:], A.subtract, ["NH", "FF"], ["KEEP"])
         tt(T.OK[:], T.OF[:, 64 * b:64 * b + 64], T.KEEP[:], A.mult, ["OF%d" % b, "KEEP"], ["OK"])
         mms([(T.NP[:, 0:64], MB("KEEPN"), T.KEEP[:], True, False)], ["KEEP", "KEEPN"], ["NP.n"], ["NP"])
-        ts(T.CL[:], T.YY[:, 64:96], 8192.0, A.add, None, None, ["YY.c"], ["CL"], ["YY"])
+        ts(T.CL[:], T.YY[:, 64:96], EMPTY, A.add, None, None, ["YY.c"], ["CL"], ["YY"])
         if nx:
             mms([(T.RV[:, 64 * h + 128:64 * h + 192], MB("KX%d" % h), T.KEEP[:], True, True) for h in (0, 1)], ["KEEP", "KX0", "KX1"], ["RV.k"], ["RV"])
         emit("V", [lambda: g.vector.tensor_copy(out=T.E[:, 0:256], in_=T.OT[:].indirect(T.CL[:, 0:16]))], OTALL + ["CL"], ["E0"])
@@ -444,8 +467,8 @@ def rank_program(g, core, T, topo):
         mms([(T.NP[:, 32 * e:32 * e + 32], MB("ENT%d" % h), T.E[:, 8 * h + 4 * e::16], False, h == 1 and e == 1) for e in (0, 1) for h in (0, 1)],
             ["E0", "E1", "ENT0", "ENT1"], ["NP.n2"], ["NP"])
         if nx:
-            old = T.LOi[:, 256 * me + 128 * b:256 * me + 128 * b + 128]
-            tt(T.OXA[:], T.RV[:, 128:256], old, A.mult, ["RV.k", "LOio0", "LOio1"], ["OXA"], ["RV"])
+            old = T.LOi[:, 128 * b:128 * b + 128]
+            tt(T.OXA[:], T.RV[:, 128:256], old, A.mult, ["RV.k", "LOis0"], ["OXA"], ["RV"])
             for h in (0, 1):
                 mms([(T.DD[:, 128 + 64 * h:192 + 64 * h], MB("KN%d" % h), T.KEEP[:], True, False)]
                     + [(T.DD[:, 128 + 64 * h + 32 * e:160 + 64 * h + 32 * e], MB("IB"), T.E[:, 8 * h + 4 * e::16], False, e == 1) for e in (0, 1)],
@@ -454,92 +477,87 @@ def rank_program(g, core, T, topo):
         tt(n, T.NP[:, 0:64], T.OK[:], A.max, ["NP.n", "NP.n2", "OK"], ["OF%d" % b], ["NP"])
         cp("V", ol, n, ["OF%d" % b], ["OL%d" % b])
         for h, bank in ((0, "K0"), (1, "K1")):
-            mms([(T[bank][:, 0:64], MX("NSW"), T["LW" + x][:, 128 * me + 64 * h:128 * me + 64 * h + 64], True, False),
-                 (T[bank][:, 0:64], MB("TMN"), T.MBF[:, ones:ones + 64], False, False)], [mine + "0", mine + "1", "NSW", "TMN", "ONES"], [bank + ".a"], [bank])
+            mms([(T[bank][:, 0:64], MX("NSW"), XE[:, 8 * h::16], True, False),
+                 (T[bank][:, 0:64], MB("TMN"), T.MBF[:, ones:ones + 64], False, False)], xe + ["NSW", "TMN", "ONES"], [bank + ".a"], [bank])
         emit("S", [lambda: g.scalar.activation(out=T.U5[:, 384:1024], in_=Wt.indirect(T.OL[:, 64 * b + 24:64 * b + 64]), func=AF.Copy)],
              WALL + ["OL%d" % b], ["U51"])
         if nx:
-            for h in (0, 1):
-                tt(T["LO" + nx][:, 128 * me + 64 * h:128 * me + 64 * h + 64], T.DD[:, 128 + 64 * h:192 + 64 * h], T.OXA[:, 64 * h:64 * h + 64], A.max,
-                   ["DD.x%d" % h, "OXA"], ["LO%so%d" % (nx, h)], ["DD"])
-            send(nx, "LO", "LO" + nx, 128)
+            tt(blocks("LO" + nx, 0, 1), T.DD[:, 128:256], T.OXA[:], A.max, ["DD.x0", "DD.x1", "OXA"], ["LO%ss0" % nx], ["DD"])
+            send("LO" + nx)
         emit("V", [lambda: g.vector.tensor_copy(out=T.U5[:, 0:384], in_=Wt.indirect(T.OL[:, 64 * b:64 * b + 24]))], WALL + ["OL%d" % b], ["U50"])
-        ts(T.HN[:], n, 8191.5, A.is_lt, None, None, ["OF%d" % b], ["HN"])
+        ts(T.HN[:], n, EMPTY, A.not_equal, None, None, ["OF%d" % b], ["HN"])
         for h, bank in ((0, "K0"), (1, "K1")):
             mms([(T[bank][:, 0:64], MB("ANY%d" % h), T.HN[:], False, True)], ["HN", "ANY%d" % h], [bank + ".b"], [bank])
+        mms([(T.RV[:, 256:384], MB("CM"), MB("ONES"), True, False)], ["CM", "ONES"], ["RV.t"], ["RV"])
         for h, c0, c1 in ((0, 0, 384), (1, 384, 1024)):
             emit("V", [lambda: g.vector.tensor_tensor_scan(out=T.MX[:, c0:c1], data0=T.RS[:, 0:c1 - c0], data1=T.U5[:, c0:c1],
                                                            initial=-2.0 * BIG, op0=A.add, op1=A.max)], ["RS", "U5%d" % h], ["MX%d" % h])
         for h, bank in ((0, "K0"), (1, "K1")):
             tt(T.OWNW[:, 64 * h:64 * h + 64], T.MX[:, 7 + 8 * h::16], T[bank][:, 0:64], A.max, ["MX0", "MX1", bank + ".a", bank + ".b"], ["OWN%d" % h], [bank])
-        mms([(T.NP[:, 256:384], MB("TMP"), MB("ONES"), True, False)], ["TMP", "ONES"], ["NP.t"], ["NP"])
-        mms([(T.RV[:, 256:384], MX("ISW"), T.OWNW[:], True, True)], ["OWN0", "OWN1", "ISW"], ["RV.s"], ["RV"])
-        mms([(T.NP[:, 256:384], MX("SW"), T.OWNW[:], False, True)], ["OWN0", "OWN1", "SW"], ["NP.t2"], ["NP"])
+        mms([(T.RV[:, 256:384], MX("ISWH"), T.OWNW[:], False, True)], ["OWN0", "OWN1", "ISWH"], ["RV.s"], ["RV"])
+        act(T.NP[:, 256:384], T.OWNW[:], 1.0, col("tm"), ["OWN0", "OWN1", "c_tm"], ["NP.t"], ["NP"])
         if not nx:
             fields(b)
             natural(b)
-        ts(T.M1[:], T.RV[:, 256:384], 0.0, A.min, col("n0"), A.add, ["RV.s", "c_n0"], ["M1"], ["RV"])
-        ts(T.M2[:], T.M1[:], 1, A.arith_shift_right, None, None, ["M1"], ["M2"])
+        ts(T.M1[:], T.RV[:, 256:384], 0.0, A.min, MAGIC, A.add, ["RV.s", "RV.t"], ["M1"], ["RV"])
+        Y = T.K0[:, 256:384]
         if nx:
-            tt(T["LW" + nx][:, 128 * me:128 * me + 128], T.M2[:], T.NP[:, 256:384], A.subtract, ["M2", "NP.t", "NP.t2"], ["LW%so0" % nx, "LW%so1" % nx], ["NP"])
-            send(nx, "LW", "LW" + nx, 128)
-            forward(nx, "LO", "LO" + nx, 128)
-            forward(nx, "LW", "LW" + nx, 128)
-            src, sr = T["LW" + nx][:, 128 * me:128 * me + 128], ["LW%so0" % nx, "LW%so1" % nx]
-        else:
-            tt(T.NF[:], T.M2[:], T.NP[:, 256:384], A.subtract, ["M2", "NP.t", "NP.t2"], ["NF"], ["NP"])
-            src, sr = T.NF[:], ["NF"]
+            tt(T.HI[:, 0:128], T.NP[:, 256:384], T.M1[:], A.subtract, ["M1", "NP.t"], ["HI"], ["NP"])
+        tt(Y, T.NP[:, 256:384], T.M1[:], A.subtract, ["M1", "NP.t"], ["K0.y"], ["NP", "K0"])
+        if nx:
+            tt(T.LO[:, 0:128], Y, T.HI[:, 0:128], A.subtract, ["K0.y", "HI"], ["LO"], ["K0"])
+            pack("LW" + nx, [(0, 0, 128)])
+            forward("LO" + nx, True)
+            send("LW" + nx)
+            forward("LW" + nx, False)
         if t > 0:
-            ts(T["YW%d" % b][:], src, col("temp"), A.add, col("sgn"), A.mult, sr + ["c_temp", "c_sgn"], ["YW%d" % b])
-            for q, y, r0 in (("Y", T.yl, 0), ("S", T.yr, 16)):
+            ts(T["YW%d" % b][:], Y, col("t64"), A.subtract, col("s64"), A.mult, ["K0.y", "c_t64", "c_s64"], ["YW%d" % b], ["K0"])
+            for q, y, r0 in (("Y", T.yl, 16), ("Y" if nx else "S", T.yr, 0)):
                 pre(q, ["YW%d" % b], [])
                 for P in range(4):
                     for h in (0, 1):
                         eng[q].dma_start(out=y[32 * P + 16 * h:32 * P + 16 * h + 16, 64 * b:64 * b + 64],
                                          in_=T["YW%d" % b][32 * P + r0:32 * P + r0 + 16, 64 * h:64 * h + 64]).then_inc(T.sem["dY%d" % b], 16)
             toks_all["dY%d" % b] = 16 * 16
-            if nx:
-                fields(b)
-                natural(b)
 
-    hs = [half, 1 - half]
-    expand("0", 0)
-    rep_w_pe("0", 0, hs[0], "S")
-    late()
-    for b in (0, 1):
-        rep_o("i", b, hs[0], "S")
-    for x, b in (("0", 0), ("1", 1)):
-        for h in hs:
-            rep_w_dma(x, b, h)
-    rep_w_same("0", 0, hs[0], "S")
-    for b in (0, 1):
-        rep_o("i", b, hs[1], "VS")
-    rep_w_same("0", 0, hs[1], "S")
+    for j in (1, 2, 3):
+        rep("LOi", j, 0, "V")
+        rep("LOi", j, 1, "S")
+    for j in (1, 2, 3):
+        rep("LW0", j, 0, "VS"[j & 1])
+    rep("LW1", 4, 1, "V")
+    for j in (4, 5, 6, 7):
+        rep("LOi", j, 0, "V")
+        rep("LOi", j, 1, "S")
     lists_gather(0)
-    rep_w_same("1", 1, hs[0], "V")
-    rep_w_pe("0", 0, hs[1], "S")
-    rep_w_pe("1", 1, hs[0], "S")
+    for j in (1, 2, 3):
+        rep("LW1", j, 1, "S")
+    rep("LW0", 4, 0, "S")
     lists(0)
-    rep_w_same("1", 1, hs[1], "V")
-    rep_w_pe("1", 1, hs[1], "S")
-    late2()
+    for j in (5, 6, 7):
+        rep("LW0", j, 0, "SV"[j & 1])
+    for j in (5, 6, 7):
+        rep("LW1", j, 1, "VS"[j & 1])
     round_(0)
+    expand(1)
+    partners((2, 3, 4, 5))
     late3()
-    expand("1", 1)
     for t, x, b in ((1, "2", 0), (2, "3", 1)):
-        for h in hs:
-            rep_w_dma(x, b, h)
-        for h in hs:
-            rep_o(x, b, h, "VS")
+        for j in (0, 4, 1, 2, 3):
+            rep("LO" + x, j, b, "SV"[j & 1])
+        rep("LW" + x, 0, b, "S")
+        for j in (5, 6, 7):
+            rep("LO" + x, j, b, "SV"[j & 1])
         lists_gather(t)
-        rep_w_same(x, b, hs[0], "S")
-        rep_w_pe(x, b, hs[0], "S")
+        for j in (4, 1, 2, 3):
+            rep("LW" + x, j, b, "S")
         lists(t)
-        rep_w_same(x, b, hs[1], "S")
-        rep_w_pe(x, b, hs[1], "S")
+        if t == 2:
+            fields(b)
+            natural(b)
+        for j in (5, 6, 7):
+            rep("LW" + x, j, b, "SV"[j & 1])
         round_(t)
-        if t == 1:
-            expand("2", 0)
     for s in SEMAPHORES:
         if toks_all.get(s, 0) > known["G"].get(s, 0):
             g.wait_ge(T.sem[s], toks_all[s])

@@ -1,12 +1,13 @@
 from concourse.bass import DstId, RemoteDMATransfer
 from concourse.mybir import AluOpType as A, ActivationFunctionType as AF
 
-EX = {"LOi": (256, "relay", False), "LW0": (256, "relay", False), "LW1": (256, "relay", True), "LO2": (128, "relay", True),
-      "LW2": (256, "relay", True), "LO3": (128, "relay", True), "LW3": (256, "relay", True)}
+EX = {"LOi": (256, 0, ()), "LW0": (256, 0, ("LOi", "LW0")), "LW1": (256, 2, ("LW1",)), "LO2": (128, 3, ("LO2",)),
+      "LW2": (256, 2, ("LW2",)), "LO3": (128, 3, ("LO3",)), "LW3": (256, 2, ("LW3",))}
 BIG = 2.0 ** 23
 MAGIC = 1.5 * 2.0 ** 17
 EMPTY = 4096.0
-MATB = (["REP%d" % p for p in range(4)] + ["YM", "ENT0", "ENT1", "KEEPN", "ANY0", "ANY1", "KX0", "KX1", "KN0", "KN1", "IB",
+KOFF = 20480.0
+MATB = (["REP%d" % p for p in range(4)] + ["YM", "ZC0", "ZC1", "ENT0", "ENT1", "KEEPN", "ANY0", "ANY1", "KX0", "KX1", "KN0", "KN1", "IB",
         "TMN", "CM", "ONES", "PERM64", "PERM65", "PERM1", "OXH0", "OXH1", "OXB0", "OXB1", "OXL0", "OXL1", "INV0", "INV1"])
 MATF = ["CH0", "CH1", "SW", "NSW", "ISWH", "INVF", "INVF2"]
 MATH = ["RW0", "RW1", "KP00", "KP01", "KP10", "KP11"]
@@ -14,10 +15,10 @@ SLID = ["OTH", "BKO"] + ["BD%d" % d for d in range(6)]
 DELTA = [1, -1, 2, -2, 3, -3]
 F, B16, H16, I32, U16 = "float32", "bfloat16", "float16", "int32", "uint16"
 SCRATCH = {}
-for _n, _w, _d in (("W", 8256, F), ("OT", 8256, B16), ("MBF", 128 * len(MATB), B16), ("MFF", 128 * len(MATF), F), ("MHF", 128 * len(MATH), H16),
+for _n, _w, _d in (("W", 8256, F), ("OT", 8272, B16), ("MBF", 128 * len(MATB), B16), ("MFF", 128 * len(MATF), F), ("MHF", 128 * len(MATH), H16),
                    ("MSL", 144 * len(SLID) + 160, B16),
                    ("CI", 16, I32), ("CF", 80, F), ("XI", 144, B16), ("MF", 768, B16), ("MKI", 1152, B16), ("MK", 1152, B16),
-                   ("RS", 640, B16), ("R32", 160, B16), ("ST", 256, I32), ("OI", 128, I32), ("FI", 384, I32), ("FB", 384, B16), ("OF", 128, F),
+                   ("RS", 256, B16), ("R32", 160, B16), ("ST", 256, I32), ("OI", 128, I32), ("FI", 384, I32), ("FB", 384, B16), ("OF", 128, F),
                    ("OL", 128, U16), ("XL", 64, U16), ("XE0", 1024, F), ("XE1", 1024, F), ("GM", 1024, B16), ("KL", 128, U16), ("KC", 64, F),
                    ("HAS", 64, F), ("U", 1024, F), ("VO", 1024, B16), ("VX", 1024, B16), ("C", 1024, B16), ("R1", 64, F), ("REV", 64, B16),
                    ("ND", 64, F), ("NH", 64, F), ("FF", 64, F), ("FK", 64, F), ("KEEP", 64, B16), ("OK", 64, F), ("CL", 32, U16), ("E", 512, B16),
@@ -29,7 +30,7 @@ for _n, _w, _d in (("W", 8256, F), ("OT", 8256, B16), ("MBF", 128 * len(MATB), B
 for _n in ("K0", "K1", "RV", "DD", "YY", "NP", "UP"):
     SCRATCH[_n] = ("psum", [128, 1024 if _n == "UP" else 512], F)
 SEMAPHORES = (["sV", "sS", "sP", "sG", "dOI", "dST"]
-              + [k + x for x in EX for k in ("p0", "p1", "p2", "p3", "q0", "q1", "q2", "q3", "m", "n", "l", "f")]
+              + [k + x for x in EX for k in ["r%d" % r for r in range(8)] + ["n", "l", "d", "f"]]
               + ["dY0", "dY1", "dO0", "dO1"])
 
 
@@ -211,8 +212,7 @@ def rank_program(g, core, T, topo):
             mat(MH("KP%d%d" % (a, hl)), "KP%d%d" % (a, hl), Xm, "XI", "KP%d" % hl, None, "wa%d" % a)
     for p in range(4):
         lin("kr%d" % p, "k", 1, -32.0 * p)
-    for n, a, m, add in (("nb5", "b5", -1, 1.0), ("pa", "h3", -16, "X0"), ("pb", "rho", 8, "pa"), ("PERMh", "pb", 1, 16.0), ("xa", "P", 128, 0.0),
-                         ("xb", "h3", 64, "xa"), ("sent", "h3", -64, 64.0), ("own15", "grp", 16, 15.0), ("w64", "h3", -63, 64.0)):
+    for n, a, m, add in (("nb5", "b5", -1, 1.0), ("pa", "h3", -16, "X0"), ("xa", "P", 128, 0.0), ("pb", "rho", 8, "pa")):
         lin(n, a, m, add)
     for j, (sh, m) in enumerate([(7, 127), (6, 1), (0, 63)]):
         ts(T.FI[:, 128 * j:128 * j + 128], T.OI[:], sh, A.logical_shift_right, m, A.bitwise_and, ["OI"], ["FI%d" % j])
@@ -228,37 +228,36 @@ def rank_program(g, core, T, topo):
         return T[x][:, EX[x][0] * j0:EX[x][0] * j1]
 
     def send(x):
-        w, mode, apart = EX[x]
+        w, k, near = EX[x]
         pre("G", [x + "s0"], [])
-        to = [cores[same[(idx + j) % 4]] for j in (1, 2, 3)]
-        trs = [RemoteDMATransfer(dst_ids=dst(to), dma_engine_mask=topo.mask(core, to[0]), remote_sem=T.sem["p%d%s" % (idx, x)],
-                                 srcs=[blocks(x, 0, 1)], dsts=[blocks(x, j, j + 1) for j in (1, 2, 3)])]
-        if apart:
-            trs.append(RemoteDMATransfer(dst_ids=dst([mate]), dma_engine_mask=sum(1 << e for e in es), remote_sem=T.sem["m" + x],
-                                         srcs=[blocks(x, 0, 1)], dsts=[blocks(x, 4, 5)]))
-            arrive("m" + x, len(es), [x + "s4"])
+        sem = T.sem["r%d%s" % (rank, x)]
+        one = [(same[(idx + j) % 4], j) for j in range(1, 4 - k)]
+        both = [(side[(idx + j) % 4], j + o) for j in range(4 - k, 4) for side, o in ((same, 0), (other, 4))]
+
+        def off(to):
+            return RemoteDMATransfer(dst_ids=dst([cores[r] for r, j in to]), dma_engine_mask=sum(1 << e for e in eo), remote_sem=sem,
+                                     srcs=[blocks(x, 0, 1)], dsts=[blocks(x, j, j + 1) for r, j in to])
+
+        trs = [off(one + both)]
+        n = len(es) // max(len(near), 1)
+        for i, y in enumerate(near):
+            trs.append(RemoteDMATransfer(dst_ids=dst([mate]), dma_engine_mask=sum(1 << e for e in es[n * i:n * i + n]),
+                                         remote_sem=T.sem["r%d%s" % (rank, y)], srcs=[blocks(y, 0, 1)], dsts=[blocks(y, 4, 5)]))
+            arrive("r%d%s" % (at[4], y), n, [y + "s4"])
         g.remote_dma_fused(trs, local_sem=T.sem["l" + x])
-        toks_all["l" + x] = len(eo) + (len(es) if apart else 0)
-        for j in (1, 2, 3):
-            arrive("p%d%s" % ((idx - j) % 4, x), len(eo), [x + "s%d" % j])
-        if mode == "direct":
-            to = [cores[other[(idx + j) % 4]] for j in (1, 2, 3)]
-            g.remote_dma_fused([RemoteDMATransfer(dst_ids=dst(to), dma_engine_mask=topo.mask(core, to[0]), remote_sem=T.sem["q%d%s" % (idx, x)],
-                                                  srcs=[blocks(x, 0, 1)], dsts=[blocks(x, 4 + j, 5 + j) for j in (1, 2, 3)])], local_sem=T.sem["f" + x])
-            toks_all["f" + x] = len(eo)
-            for j in (1, 2, 3):
-                arrive("q%d%s" % ((idx - j) % 4, x), len(eo), [x + "s%d" % (4 + j)])
+        toks_all["l" + x] = len(eo) + n * len(near)
+        for j in [1, 2, 3] + list(range(8 - k, 8)):
+            arrive("r%d%s" % (at[j], x), len(eo), [x + "s%d" % j])
 
     def forward(x, free):
-        w, mode, apart = EX[x]
-        if mode == "direct":
+        w, k, near = EX[x]
+        if k == 3:
             return
-        j0 = 1 if apart else 0
-        pre("G", [x + "s%d" % j for j in range(j0, 4)], [])
+        pre("G", [x + "s%d" % j for j in range(1, 4 - k)], [])
         e = es if free else topo.engines(core, mate)
-        g.remote_dma(blocks(x, 4 + j0, 8), blocks(x, j0, 4), T.sem["n" + x], T.sem["f" + x], topo.addr(mate)[1], topo.addr(mate)[0], sum(1 << k for k in e))
+        g.remote_dma(blocks(x, 5, 8 - k), blocks(x, 1, 4 - k), T.sem["n" + x], T.sem["f" + x], topo.addr(mate)[1], topo.addr(mate)[0], sum(1 << i for i in e))
         toks_all["f" + x] = len(e)
-        arrive("n" + x, len(e), [x + "s%d" % j for j in range(4 + j0, 8)])
+        arrive("n" + x, len(e), [x + "s%d" % j for j in range(5, 8 - k)])
 
     fa, fb, low = T.FB[:, 0:128], T.FB[:, 128:256], T.FB[:, 256:384]
     for h, bank in ((0, "RV"), (1, "NP")):
@@ -272,13 +271,11 @@ def rank_program(g, core, T, topo):
     send("LOi")
 
     def pack(x, cols):
-        ms = []
-        for a in (0, 1):
-            for o, i, n in cols:
-                ms += [(T.UP[:, 128 * a + o:128 * a + o + n], MH("KP%d0" % a), T.HI[:, i:i + n], True, False),
-                       (T.UP[:, 128 * a + o:128 * a + o + n], MH("KP%d1" % a), T.LO[:, i:i + n], False, True)]
-        mms(ms, ["HI", "LO", "KP00", "KP01", "KP10", "KP11"], ["UPa.r"], ["UPa"])
-        cp("V", blocks(x, 0, 1), T.UP[:, 0:256], ["UPa.r"], [x + "s0"], ["UPa"])
+        for o, i, n in cols:
+            for hl, src, name in ((0, T.HI, "HI"), (1, T.LO, "LO")):
+                mms([(T.UP[:, 384 + 128 * a + o:384 + 128 * a + o + n], MH("KP%d%d" % (a, hl)), src[:, i:i + n], hl == 0, hl == 1) for a in (0, 1)],
+                    [name, "KP0%d" % hl, "KP1%d" % hl], ["UPa.r", "UPb.r"] if hl == 0 and o == 0 else ["UP.%d.%d" % (hl, o)], ["UPa", "UPb"])
+        cp("V", blocks(x, 0, 1), T.UP[:, 384:640], ["UPa.r", "UPb.r", "UP.1.%d" % cols[-1][0]], [x + "s0"], ["UPa", "UPb"])
 
     ts(T.HI[:], T.ST[:], col("sg64"), A.mult, col("t64"), A.add, ["ST", "c_sg64", "c_t64"], ["HI"])
     ts(T.K0[:, 256:512], T.ST[:], col("sg64"), A.mult, col("t64"), A.add, ["ST", "c_sg64", "c_t64"], ["K0.y"], ["K0"])
@@ -289,40 +286,49 @@ def rank_program(g, core, T, topo):
     emit("G", [lambda: g.iota(T.MKI[:], [[0, 9], [1, 8], [0, 16]], 0, 0, allow_small_or_imprecise_dtypes=True)], (), ["MKI"])
     forward("LOi", True)
     forward("LW0", True)
-    forward("LW1", False)
-    for n, a, m, add in (("ot", "rho", -32, "own15"), ("oth15", "ot", 1, 16.0), ("thr1", "b0", 1, -0.5), ("thr2", "b1", 1, -0.5), ("bf", "rho", -4, "blk"),
-                         ("blkf", "bf", 1, 2.0), ("bl2", "blkf", 2, 0.0), ("bl3", "blkf", 2, 1.0), ("ta", "rho", -16, "X0"), ("T0", "ta", 1, 16.0),
-                         ("T8", "ta", 1, 24.0), ("g0", "h3", -1, 1.0), ("a0", "g0", -BIG, 0.0), ("a1", "h3", -BIG, 0.0), ("k111", "rho", -16, "k")):
+    forward("LW1", True)
+    for n, a, m, add in (("PERMh", "pb", 1, 16.0), ("xb", "h3", 64, "xa"), ("sent", "h3", -64, 64.0), ("own15", "grp", 16, 15.0), ("w64", "h3", -63, 64.0),
+                         ("bf", "rho", -4, "blk"), ("ot", "rho", -32, "own15"), ("ta", "rho", -16, "X0"), ("g0", "h3", -1, 1.0), ("blkf", "bf", 1, 2.0),
+                         ("oth15", "ot", 1, 16.0), ("T0", "ta", 1, 16.0), ("T8", "ta", 1, 24.0), ("bl2", "blkf", 2, 0.0), ("bl3", "blkf", 2, 1.0),
+                         ("a0", "h3", BIG, -BIG), ("a1", "h3", -BIG, 0.0), ("k111", "rho", -16, "k"), ("wz", "s", -65536, 13 * 32768.0),
+                         ("thr1", "b0", 1, -0.5), ("thr2", "b1", 1, -0.5)):
         lin(n, a, m, add)
     for p in range(4):
         mat(MB("REP%d" % p), "REP%d" % p, fld("f31"), "f31", "kr%d" % p, 1.0)
     for p in (0, 1):
         mat(MH("RW%d" % p), "RW%d" % p, fld("f31"), "f31", "k31", None, ["nb5", "b5"][p])
 
-    OTALL = ["OTz"] + ["OT%d%d" % (b, r) for b in (0, 1) for r in range(8)]
-    WALL = ["Wz"] + ["W%d%d" % (b, r) for b in (0, 1) for r in range(8)]
+    OTALL = ["OTz", "OTy"] + ["OT%d%d%s" % (b, r, z) for b in (0, 1) for r in range(8) for z in "ab"]
+    WALL = ["Wz"] + ["W%d%d%s" % (b, r, z) for b in (0, 1) for r in range(8) for z in "ab"]
     rb = [("UP", 0, "UPa"), ("UP", 512, "UPb"), ("YY", 0, "YY"), ("DD", 0, "DD"), ("RV", 0, "RV"), ("NP", 0, "NP")]
     nb = [0]
 
     def rep(x, j, b, q):
-        buf, c0, bank = rb[nb[0] % len(rb)]
-        nb[0] += 1
         w, d0 = EX[x][0], place(at[j], b)
-        if x[1] == "O":
-            s0 = w * j + (128 * b if x == "LOi" else 0)
-            ms = [(T[buf][:, c0 + 128 * p:c0 + 128 * p + 128], MB("REP%d" % p), T[x][:, s0:s0 + 128], True, True) for p in range(4)]
-            mr, tab, reg = ["REP%d" % p for p in range(4)], T.OT, "OT"
-        else:
-            ms = [(T[buf][:, c0 + 128 * p:c0 + 128 * p + 128], MH("RW%d" % (p & 1)), T[x][:, w * j + 128 * (p >> 1):w * j + 128 * (p >> 1) + 128], True, True)
-                  for p in range(4)]
-            mr, tab, reg = ["RW0", "RW1"], T.W, "W"
-        mms(ms, [x + "s%d" % j] + mr, [bank + ".r"], [bank])
-        cp(q, tab[:, d0:d0 + 512], T[buf][:, c0:c0 + 512], [bank + ".r"], ["%s%d%d" % (reg, b, at[j])], [bank])
+        n = 4 // len(q)
+        for i, qi in enumerate(q):
+            buf, c0, bank = rb[nb[0] % len(rb)]
+            nb[0] += 1
+            ps = range(n * i, n * i + n)
+            outs = [T[buf][:, c0 + 128 * (p - n * i):c0 + 128 * (p - n * i) + 128] for p in ps]
+            if x[1] == "O":
+                s0 = w * j + (128 * b if x == "LOi" else 0)
+                ms = [(o, MB("REP%d" % p), T[x][:, s0:s0 + 128], True, True) for o, p in zip(outs, ps)]
+                mr, tab, reg = ["REP%d" % p for p in range(4)], T.OT, "OT"
+            else:
+                ms = [(o, MH("RW%d" % (p & 1)), T[x][:, w * j + 128 * (p >> 1):w * j + 128 * (p >> 1) + 128], True, True) for o, p in zip(outs, ps)]
+                mr, tab, reg = ["RW0", "RW1"], T.W, "W"
+            mms(ms, [x + "s%d" % j] + mr, [bank + ".r"], [bank])
+            cp(qi, tab[:, d0 + 128 * n * i:d0 + 128 * n * (i + 1)], T[buf][:, c0:c0 + 128 * n], [bank + ".r"],
+               ["%s%d%d%s" % (reg, b, at[j], z) for z in ("ab" if n == 4 else "ab"[i])], [bank])
+
+    def order(x):
+        return [[0, 4, 1, 2, 3, 5, 6, 7], [0, 4, 1, 2, 3, 7, 5, 6], [0, 4, 1, 2, 6, 3, 5, 7], [0, 4, 1, 5, 2, 6, 3, 7]][EX[x][1]]
 
     def expand(b):
         d0 = place(rank, b)
         emit("S", [lambda: g.scalar.activation(out=T["XE%d" % b][:], in_=T.W[:, d0:d0 + 512].indirect(T.XL[:]), func=AF.Copy)],
-             ["W%d%d" % (b, rank), "XL"], ["XE%d" % b])
+             ["W%d%da" % (b, rank), "W%d%db" % (b, rank), "XL"], ["XE%d" % b])
 
     mat(MB("PERM1"), "PERM1", Xm, "XI", "PERMh", 1.0)
     mat(MB("PERM64"), "PERM64", Xm, "XI", "PERMh", 64.0)
@@ -342,6 +348,7 @@ def rank_program(g, core, T, topo):
     emit("V", [lambda: g.vector.memset(T.RS[:], 0.0)], (), ["RS"])
     ones = 128 * MATB.index("ONES")
     ts(T.OT[:, 4096:4160], T.MBF[:, ones:ones + 64], col("sent"), A.mult, None, None, ["ONES", "c_sent"], ["OTz"])
+    ts(T.OT[:, 8256:8272], T.MBF[:, ones:ones + 16], col("sent"), A.mult, None, None, ["ONES", "c_sent"], ["OTy"])
     cp("V", T.OF[:], T.K1[:, 0:128], ["K1.o"], ["OF0", "OF1"], ["K1"])
     emit("V", [lambda: g.vector.memset(T.RS[:, 0::8], -BIG)], (), ["RS"])
     mat(SL("BKO"), "BKO", Xs, "XI", "own15", None, "w64")
@@ -351,9 +358,9 @@ def rank_program(g, core, T, topo):
     mat(SL("OTH"), "OTH", Xs, "XI", "oth15", 1.0)
     mat(MX("SW"), "SW", Xm, "XI", "SWh", 1.0)
     mat(MX("NSW"), "NSW", Xm, "XI", "SWh", -1.0)
-    mat(MB("YM"), "YM", fld("f8"), "f8", "blk", -2.0)
+    mat(MB("YM"), "YM", fld("f8"), "f8", "blk", -65536.0)
     emit("G", [lambda: g.affine_select(MB("YM"), MB("YM"), [[1, 128]], A.is_gt, 0.0, 0, -1)], ["YM"], ["YM"])
-    emit("G", [lambda: g.affine_select(MB("YM"), MB("YM"), [[1, 128]], A.not_equal, 1.0, 0, -1)], ["YM"], ["YM"])
+    emit("G", [lambda: g.affine_select(MB("YM"), MB("YM"), [[1, 128]], A.not_equal, 32768.0, 0, -1)], ["YM"], ["YM"])
 
     def partners(js):
         for j in js:
@@ -363,6 +370,8 @@ def rank_program(g, core, T, topo):
     partners((0, 1))
     mat(MX("CH0"), "CH0", fld("f4"), "f4", "bl2", 1.0)
     mat(MX("CH1"), "CH1", fld("f4"), "f4", "bl3", 1.0)
+    mat(MB("ZC0"), "ZC0", fld("f4"), "f4", "bl2", None, "wz")
+    mat(MB("ZC1"), "ZC1", fld("f4"), "f4", "bl3", None, "wz")
     mat(MB("ENT0"), "ENT0", Xm, "XI", "T0", None, "w64")
     mat(MB("ENT1"), "ENT1", Xm, "XI", "T8", None, "w64")
     for h, gn in ((0, "g0"), (1, "h3")):
@@ -398,12 +407,17 @@ def rank_program(g, core, T, topo):
         b = t & 1
         mms([(T.K0[:, 0:64], SL("BKO", q), T.GM[:, q::16], q == 0, q == 15) for q in range(16)], ["GM", "BKO"], ["K0.k"], ["K0"])
         ts(T.HAS[:], T.OF[:, 64 * b:64 * b + 64], EMPTY, A.not_equal, None, None, ["OF%d" % b], ["HAS"])
-        ts(T.KC[:], T.K0[:, 0:64], -EMPTY, A.add, None, None, ["K0.k"], ["KC"], ["K0"])
-        mms([(T.K1[:, 0:64], MX("SW"), T.KC[:], True, True)], ["KC", "SW"], ["K1.k"], ["K1"])
+        ts(T.KC[:], T.K0[:, 0:64], KOFF, A.add, None, None, ["K0.k"], ["KC"], ["K0"])
         cp("V", T.KL[:, 0:64], T.K0[:, 0:64], ["K0.k"], ["KL0"], ["K0"])
 
-    def lists2(t):
-        ts(T.KL[:, 64:128], T.K1[:, 0:64], EMPTY, A.add, None, None, ["K1.k"], ["KL1"], ["K1"])
+    def tail(x, b):
+        js = order(x)[4:]
+        rep(x, js[0], b, "S")
+        rep(x, js[1], b, "V")
+        mms([(T.K1[:, 0:64], MX("SW"), T.KC[:], True, True)], ["KC", "SW"], ["K1.k"], ["K1"])
+        ts(T.KL[:, 64:128], T.K1[:, 0:64], -KOFF, A.add, None, None, ["K1.k"], ["KL1"], ["K1"])
+        for j in js[2:]:
+            rep(x, j, b, "VS")
 
     def fields(b):
         n = T.OF[:, 64 * b:64 * b + 64]
@@ -429,15 +443,14 @@ def rank_program(g, core, T, topo):
         cp("S", T.UP[:], T.U[:], ["U"], ["UPa.r", "UPb.r"], ["UPa", "UPb"])
         if t == 0:
             late2()
-        if t == 1:
-            expand(0)
+        if nx:
+            expand(1 - b)
         XE = T["XE%d" % b]
         tt(T.VO[:], Wt.indirect(T.KL[:, 0:64]), XE[:], A.is_gt, WALL + ["KL0"] + xe, ["VO"])
         mms([(T.RV[:, 0:64], SL("OWN", q), T.VO[:, q::16], q == 0, False) for q in range(16)], ["VO", "OWN"], ["RV.v"], ["RV"])
-        lists2(t)
         tt(T.VX[:], Wt.indirect(T.KL[:, 64:128]), XE[:], A.is_lt, WALL + ["KL1"] + xe, ["VX"])
         mms([(T.RV[:, 0:64], SL("OTH", q), T.VX[:, q::16], False, q == 15) for q in range(16)], ["VX", "OTH"], ["RV.v2"], ["RV"])
-        st = {1: [(0, 1, 2)], 2: [(0, 2, 4), (1, 3, 4)], 3: [(0, 3, 4), (1, 2, 4)]}[m]
+        st = {1: [(0, 1, 4), (2, 3, 4)], 2: [(0, 2, 4), (1, 3, 4)], 3: [(0, 3, 4), (1, 2, 4)]}[m]
         thr = "thr1" if m == 1 else "thr2"
         nq = 0
         for u, v, s in st:
@@ -451,21 +464,22 @@ def rank_program(g, core, T, topo):
         ts(T.R1[:], T.RV[:, 0:64], 1024.0, A.mult, col(thr), A.add, ["RV.v", "RV.v2", "c_" + thr], ["R1"], ["RV"])
         tt(T.REV[:], T.DD[:, 0:64], T.R1[:], A.is_ge, dd + ["R1"], ["REV"], ["DD"])
         mms([(T.YY[:, 0:64], MB("YM"), T.REV[:], True, True)], ["REV", "YM"], ["YY.y"], ["YY"])
+        mms([(T.K1[:, 64:96], MB("ZC%d" % e), T.REV[:, 32 * e:32 * e + 32], e == 0, False) for e in (0, 1)], ["REV", "ZC0", "ZC1"], ["K1.z"], ["K1"])
         ts(T.ND[:], T.DD[:, 0:64], col(thr), A.is_ge, None, None, dd + ["c_" + thr], ["ND"], ["DD"])
-        tt(T.NH[:], T.ND[:], T.HAS[:], A.mult, ["ND", "HAS"], ["NH"])
+        tt(T.FK[:], T.YY[:, 0:64], T.KC[:], A.min, ["YY.y", "KC"], ["FK"], ["YY"])
+        mms([(T.K1[:, 64:96], MX("CH%d" % e), T.FK[:, 32 * e:32 * e + 32], False, e == 1) for e in (0, 1)], ["FK", "CH0", "CH1"], ["K1.c"], ["K1"])
         ts(T.FF[:], T.YY[:, 0:64], 0.5, A.is_gt, None, None, ["YY.y"], ["FF"], ["YY"])
-        tt(T.FK[:], T.FF[:], T.KC[:], A.mult, ["FF", "KC"], ["FK"])
-        mms([(T.YY[:, 64:96], MX("CH%d" % e), T.FK[:, 32 * e:32 * e + 32], e == 0, e == 1) for e in (0, 1)], ["FK", "CH0", "CH1"], ["YY.c"], ["YY"])
+        tt(T.NH[:], T.ND[:], T.HAS[:], A.mult, ["ND", "HAS"], ["NH"])
         tt(T.KEEP[:], T.NH[:], T.FF[:], A.subtract, ["NH", "FF"], ["KEEP"])
-        tt(T.OK[:], T.OF[:, 64 * b:64 * b + 64], T.KEEP[:], A.mult, ["OF%d" % b, "KEEP"], ["OK"])
         mms([(T.NP[:, 0:64], MB("KEEPN"), T.KEEP[:], True, False)], ["KEEP", "KEEPN"], ["NP.n"], ["NP"])
-        ts(T.CL[:], T.YY[:, 64:96], EMPTY, A.add, None, None, ["YY.c"], ["CL"], ["YY"])
+        ts(T.CL[:], T.K1[:, 64:96], 32768.0 - KOFF, A.add, 8256.0, A.min, ["K1.z", "K1.c"], ["CL"], ["K1"])
         if nx:
             mms([(T.RV[:, 64 * h + 128:64 * h + 192], MB("KX%d" % h), T.KEEP[:], True, True) for h in (0, 1)], ["KEEP", "KX0", "KX1"], ["RV.k"], ["RV"])
         emit("V", [lambda: g.vector.tensor_copy(out=T.E[:, 0:256], in_=T.OT[:].indirect(T.CL[:, 0:16]))], OTALL + ["CL"], ["E0"])
         emit("S", [lambda: g.scalar.activation(out=T.E[:, 256:512], in_=T.OT[:].indirect(T.CL[:, 16:32]), func=AF.Copy)], OTALL + ["CL"], ["E1"])
         mms([(T.NP[:, 32 * e:32 * e + 32], MB("ENT%d" % h), T.E[:, 8 * h + 4 * e::16], False, h == 1 and e == 1) for e in (0, 1) for h in (0, 1)],
             ["E0", "E1", "ENT0", "ENT1"], ["NP.n2"], ["NP"])
+        tt(T.OK[:], T.OF[:, 64 * b:64 * b + 64], T.KEEP[:], A.mult, ["OF%d" % b, "KEEP"], ["OK"])
         if nx:
             old = T.LOi[:, 128 * b:128 * b + 128]
             tt(T.OXA[:], T.RV[:, 128:256], old, A.mult, ["RV.k", "LOis0"], ["OXA"], ["RV"])
@@ -479,21 +493,23 @@ def rank_program(g, core, T, topo):
         for h, bank in ((0, "K0"), (1, "K1")):
             mms([(T[bank][:, 0:64], MX("NSW"), XE[:, 8 * h::16], True, False),
                  (T[bank][:, 0:64], MB("TMN"), T.MBF[:, ones:ones + 64], False, False)], xe + ["NSW", "TMN", "ONES"], [bank + ".a"], [bank])
-        emit("S", [lambda: g.scalar.activation(out=T.U5[:, 384:1024], in_=Wt.indirect(T.OL[:, 64 * b + 24:64 * b + 64]), func=AF.Copy)],
-             WALL + ["OL%d" % b], ["U51"])
+        for h in (1, 2, 3):
+            emit("S", [lambda: g.scalar.activation(out=T.U5[:, 256 * h:256 * h + 256], in_=Wt.indirect(T.OL[:, 64 * b + 16 * h:64 * b + 16 * h + 16]),
+                                                   func=AF.Copy)], WALL + ["OL%d" % b], ["U5%d" % h])
         if nx:
             tt(blocks("LO" + nx, 0, 1), T.DD[:, 128:256], T.OXA[:], A.max, ["DD.x0", "DD.x1", "OXA"], ["LO%ss0" % nx], ["DD"])
             send("LO" + nx)
-        emit("V", [lambda: g.vector.tensor_copy(out=T.U5[:, 0:384], in_=Wt.indirect(T.OL[:, 64 * b:64 * b + 24]))], WALL + ["OL%d" % b], ["U50"])
+        emit("V", [lambda: g.vector.tensor_copy(out=T.U5[:, 0:256], in_=Wt.indirect(T.OL[:, 64 * b:64 * b + 16]))], WALL + ["OL%d" % b], ["U50"])
         ts(T.HN[:], n, EMPTY, A.not_equal, None, None, ["OF%d" % b], ["HN"])
         for h, bank in ((0, "K0"), (1, "K1")):
             mms([(T[bank][:, 0:64], MB("ANY%d" % h), T.HN[:], False, True)], ["HN", "ANY%d" % h], [bank + ".b"], [bank])
         mms([(T.RV[:, 256:384], MB("CM"), MB("ONES"), True, False)], ["CM", "ONES"], ["RV.t"], ["RV"])
-        for h, c0, c1 in ((0, 0, 384), (1, 384, 1024)):
-            emit("V", [lambda: g.vector.tensor_tensor_scan(out=T.MX[:, c0:c1], data0=T.RS[:, 0:c1 - c0], data1=T.U5[:, c0:c1],
+        for h in range(4):
+            emit("V", [lambda: g.vector.tensor_tensor_scan(out=T.MX[:, 256 * h:256 * h + 256], data0=T.RS[:], data1=T.U5[:, 256 * h:256 * h + 256],
                                                            initial=-2.0 * BIG, op0=A.add, op1=A.max)], ["RS", "U5%d" % h], ["MX%d" % h])
         for h, bank in ((0, "K0"), (1, "K1")):
-            tt(T.OWNW[:, 64 * h:64 * h + 64], T.MX[:, 7 + 8 * h::16], T[bank][:, 0:64], A.max, ["MX0", "MX1", bank + ".a", bank + ".b"], ["OWN%d" % h], [bank])
+            tt(T.OWNW[:, 64 * h:64 * h + 64], T.MX[:, 7 + 8 * h::16], T[bank][:, 0:64], A.max, ["MX0", "MX1", "MX2", "MX3", bank + ".a", bank + ".b"],
+               ["OWN%d" % h], [bank])
         mms([(T.RV[:, 256:384], MX("ISWH"), T.OWNW[:], False, True)], ["OWN0", "OWN1", "ISWH"], ["RV.s"], ["RV"])
         act(T.NP[:, 256:384], T.OWNW[:], 1.0, col("tm"), ["OWN0", "OWN1", "c_tm"], ["NP.t"], ["NP"])
         if not nx:
@@ -507,9 +523,9 @@ def rank_program(g, core, T, topo):
         if nx:
             tt(T.LO[:, 0:128], Y, T.HI[:, 0:128], A.subtract, ["K0.y", "HI"], ["LO"], ["K0"])
             pack("LW" + nx, [(0, 0, 128)])
-            forward("LO" + nx, True)
             send("LW" + nx)
-            forward("LW" + nx, False)
+            forward("LO" + nx, True)
+            forward("LW" + nx, True)
         if t > 0:
             ts(T["YW%d" % b][:], Y, col("t64"), A.subtract, col("s64"), A.mult, ["K0.y", "c_t64", "c_s64"], ["YW%d" % b], ["K0"])
             for q, y, r0 in (("Y", T.yl, 16), ("Y" if nx else "S", T.yr, 0)):
@@ -519,44 +535,41 @@ def rank_program(g, core, T, topo):
                         eng[q].dma_start(out=y[32 * P + 16 * h:32 * P + 16 * h + 16, 64 * b:64 * b + 64],
                                          in_=T["YW%d" % b][32 * P + r0:32 * P + r0 + 16, 64 * h:64 * h + 64]).then_inc(T.sem["dY%d" % b], 16)
             toks_all["dY%d" % b] = 16 * 16
+            if nx:
+                fields(b)
+                natural(b)
 
-    for j in (1, 2, 3):
+    for j in (4, 1, 2, 3):
         rep("LOi", j, 0, "V")
         rep("LOi", j, 1, "S")
-    for j in (1, 2, 3):
+    for j in (4, 1, 2, 3):
         rep("LW0", j, 0, "VS"[j & 1])
-    rep("LW1", 4, 1, "V")
-    for j in (4, 5, 6, 7):
+    rep("LW1", 4, 1, "S")
+    for j in (5, 6, 7):
         rep("LOi", j, 0, "V")
         rep("LOi", j, 1, "S")
     lists_gather(0)
-    for j in (1, 2, 3):
+    ow = order("LW1")
+    for j in ow[2:4]:
         rep("LW1", j, 1, "S")
-    rep("LW0", 4, 0, "S")
+    for j in (5, 6, 7):
+        rep("LW0", j, 0, "SSV"[j - 5])
     lists(0)
-    for j in (5, 6, 7):
-        rep("LW0", j, 0, "SV"[j & 1])
-    for j in (5, 6, 7):
-        rep("LW1", j, 1, "VS"[j & 1])
+    tail("LW1", 1)
     round_(0)
-    expand(1)
-    partners((2, 3, 4, 5))
-    late3()
     for t, x, b in ((1, "2", 0), (2, "3", 1)):
-        for j in (0, 4, 1, 2, 3):
-            rep("LO" + x, j, b, "SV"[j & 1])
-        rep("LW" + x, 0, b, "S")
-        for j in (5, 6, 7):
-            rep("LO" + x, j, b, "SV"[j & 1])
+        oo, ow = order("LO" + x), order("LW" + x)
+        for i, j in enumerate(oo):
+            rep("LO" + x, j, b, "SV"[i & 1])
         lists_gather(t)
-        for j in (4, 1, 2, 3):
+        for j in ow[:3]:
             rep("LW" + x, j, b, "S")
         lists(t)
-        if t == 2:
-            fields(b)
-            natural(b)
-        for j in (5, 6, 7):
-            rep("LW" + x, j, b, "SV"[j & 1])
+        partners((2 * t, 2 * t + 1))
+        if t == 1:
+            late3()
+        rep("LW" + x, ow[3], b, "S")
+        tail("LW" + x, b)
         round_(t)
     for s in SEMAPHORES:
         if toks_all.get(s, 0) > known["G"].get(s, 0):

@@ -3,34 +3,36 @@ from concourse.mybir import AluOpType as A, ActivationFunctionType as AF
 
 EX = {"LOi": (256, 0, ()), "LW0": (256, 0, ("LOi", "LW0")), "LW1": (256, 2, ("LW1",)), "LO2": (128, 3, ("LO2",)),
       "LW2": (256, 2, ("LW2",)), "LO3": (128, 3, ("LO3",)), "LW3": (256, 2, ("LW3",))}
+TWO = False
 BIG = 2.0 ** 23
 MAGIC = 1.5 * 2.0 ** 17
 EMPTY = 4096.0
-KOFF = 20480.0
-MATB = (["REP%d" % p for p in range(4)] + ["YM", "ZC0", "ZC1", "ENT0", "ENT1", "KEEPN", "ANY0", "ANY1", "KX0", "KX1", "KN0", "KN1", "IB",
-        "TMN", "CM", "ONES", "PERM64", "PERM65", "PERM1", "OXH0", "OXH1", "OXB0", "OXB1", "OXL0", "OXL1", "INV0", "INV1"])
-MATF = ["CH0", "CH1", "SW", "NSW", "ISWH", "INVF", "INVF2"]
-MATH = ["RW0", "RW1", "KP00", "KP01", "KP10", "KP11"]
-SLID = ["OTH", "BKO"] + ["BD%d" % d for d in range(6)]
+KOFF = 8192.0 * 3
+MATB = [("REP", 512), ("YM", 128), ("ZC", 136), ("ENT", 136), ("KEEPN", 128), ("ANY0", 128), ("ANY1", 128), ("KX0", 128), ("KX1", 128),
+        ("KN0", 128), ("KN1", 128), ("IB", 128), ("TMN", 128), ("CM", 128), ("ONES", 128), ("PERM64", 128), ("PERM1", 128), ("OX0", 136),
+        ("OX1", 136), ("INV1", 128), ("OWN", 152), ("R32", 144), ("OTH", 144), ("BKO", 144)] + [("BD%d" % d, 144) for d in range(6)]
+MATF = [("CH", 132), ("SW", 128), ("NSW", 128), ("ISWH", 128), ("INVF", 128)]
+MATH = [("RW", 256), ("KP", 320), ("RP", 512), ("INV0", 128)]
+FLD = [("f31", [[32, 4], [0, 4], [1, 32]], 0), ("f63", [[64, 3], [200, 2], [1, 64]], -216), ("f16", [[0, 3], [1, 8], [0, 16]], 0), ("f8", [[1, 16], [0, 8]], 0), ("f4", [[1, 34], [0, 4]], -5),
+       ("f119", [[16, 8], [0, 2], [1, 8]], -16), ("f111", [[32, 4], [0, 2], [1, 16]], 0)]
 DELTA = [1, -1, 2, -2, 3, -3]
 F, B16, H16, I32, U16 = "float32", "bfloat16", "float16", "int32", "uint16"
 SCRATCH = {}
-for _n, _w, _d in (("W", 8256, F), ("OT", 8272, B16), ("MBF", 128 * len(MATB), B16), ("MFF", 128 * len(MATF), F), ("MHF", 128 * len(MATH), H16),
-                   ("MSL", 144 * len(SLID) + 160, B16),
-                   ("CI", 16, I32), ("CF", 80, F), ("XI", 144, B16), ("MF", 768, B16), ("MKI", 1152, B16), ("MK", 1152, B16),
-                   ("RS", 256, B16), ("R32", 160, B16), ("ST", 256, I32), ("OI", 128, I32), ("FI", 384, I32), ("FB", 384, B16), ("OF", 128, F),
+for _n, _w, _d in (("W", 8256, F), ("OT", 8272, B16), ("MBF", sum(w for n, w in MATB), B16), ("MFF", sum(w for n, w in MATF), F),
+                   ("MHF", sum(w for n, w in MATH), H16), ("CI", 16, I32), ("CF", 64, F), ("XI", 208, B16), ("MF", 512 * len(FLD), B16),
+                   ("MK", 1056, B16), ("RS", 256, B16), ("ST", 256, I32), ("OI", 128, I32), ("FI", 384, I32), ("FB", 384, B16), ("OF", 128, F),
                    ("OL", 128, U16), ("XL", 64, U16), ("XE0", 1024, F), ("XE1", 1024, F), ("GM", 1024, B16), ("KL", 128, U16), ("KC", 64, F),
-                   ("HAS", 64, F), ("U", 1024, F), ("VO", 1024, B16), ("VX", 1024, B16), ("C", 1024, B16), ("R1", 64, F), ("REV", 64, B16),
-                   ("ND", 64, F), ("NH", 64, F), ("FF", 64, F), ("FK", 64, F), ("KEEP", 64, B16), ("OK", 64, F), ("CL", 32, U16), ("E", 512, B16),
+                   ("H1", 64, F), ("H2", 64, F), ("U", 1024, F), ("VO", 1024, B16), ("VX", 1024, B16), ("C", 1024, B16), ("R1", 64, F),
+                   ("REV", 64, B16), ("FK", 64, F), ("KEEP", 64, B16), ("OK", 64, F), ("CL", 32, U16), ("E", 512, B16),
                    ("OXA", 128, B16), ("HN", 64, B16), ("U5", 1024, F), ("MX", 1024, F), ("OWNW", 128, F), ("M1", 128, F),
-                   ("HI", 256, H16), ("LO", 256, H16), ("YW0", 128, F), ("YW1", 128, F), ("YI", 64, I32), ("YFI", 64, I32), ("YFB", 128, B16),
+                   ("HI", 256, H16), ("LO", 256, H16), ("YW0", 128, F), ("YW1", 128, F), ("YH", 64, H16), ("YB", 64, B16),
                    ("YO0", 64, F), ("YO1", 64, F), ("LW0", 2048, H16), ("LW1", 2048, H16), ("LW2", 2048, H16), ("LW3", 2048, H16),
                    ("LOi", 2048, B16), ("LO2", 1024, B16), ("LO3", 1024, B16)):
     SCRATCH[_n] = ("sbuf", [128, _w], _d)
 for _n in ("K0", "K1", "RV", "DD", "YY", "NP", "UP"):
     SCRATCH[_n] = ("psum", [128, 1024 if _n == "UP" else 512], F)
 SEMAPHORES = (["sV", "sS", "sP", "sG", "dOI", "dST"]
-              + [k + x for x in EX for k in ["r%d" % r for r in range(8)] + ["n", "l", "d", "f"]]
+              + [k + x for x in EX for k in ["r%d" % r for r in range(8)] + ["n1", "n2", "l", "f1", "f2"]]
               + ["dY0", "dY1", "dO0", "dO1"])
 
 
@@ -114,6 +116,9 @@ def rank_program(g, core, T, topo):
         else:
             emit("S", [lambda: g.scalar.activation(out=out, in_=i, func=AF.Copy)], R, W, B)
 
+    def fill(out, c, W):
+        emit("V", [lambda: g.vector.memset(out, c)], (), W)
+
     def act(out, i, scale, bias, R=(), W=(), B=()):
         emit("S", [lambda: g.scalar.activation(out=out, in_=i, func=AF.Identity, bias=bias, scale=scale)], R, W, B)
 
@@ -123,21 +128,16 @@ def rank_program(g, core, T, topo):
     def mms(groups, R=(), W=(), B=()):
         emit("P", [(lambda m=m: g.tensor.matmul(out=m[0], lhsT=m[1], rhs=m[2], start=m[3], stop=m[4])) for m in groups], R, W, B)
 
-    def MB(n):
-        j = MATB.index(n)
-        return T.MBF[:, 128 * j:128 * j + 128]
+    def M(n, a=None, w=128):
+        for buf, lst in ((T.MBF, MATB), (T.MFF, MATF), (T.MHF, MATH)):
+            j = 0
+            for name, width in lst:
+                if name == n:
+                    return buf[:, j:j + width] if a is None else buf[:, j + a:j + a + w]
+                j += width
 
-    def MX(n):
-        j = MATF.index(n)
-        return T.MFF[:, 128 * j:128 * j + 128]
-
-    def MH(n):
-        j = MATH.index(n)
-        return T.MHF[:, 128 * j:128 * j + 128]
-
-    def SL(n, q=None):
-        j = 4 if n == "OWN" else 160 + 144 * SLID.index(n)
-        return T.MSL[:, j:j + 144] if q is None else T.MSL[:, j + 15 - q:j + 143 - q]
+    def SL(n, q):
+        return M(n, (4 if n == "OWN" else 0) + 15 - q)
 
     def place(r, b):
         return 64 * (8 * r + 65 * b)
@@ -150,18 +150,25 @@ def rank_program(g, core, T, topo):
                                  in_=src[32 * P + 16 * h:32 * P + 16 * h + 16, :]).then_inc(T.sem.dST, 16)
     arrive("dST", 16 * 16, ["ST"])
     emit("G", [lambda: g.iota(T.CI[:, 0:1], [[0, 1]], 0, 1)], (), ["ci0"])
-    emit("G", [lambda: g.iota(T.XI[:], [[1, 144]], 0, 0, allow_small_or_imprecise_dtypes=True)], (), ["XI"])
-    flds = [("f31", [[0, 4], [1, 32]]), ("f8", [[1, 16], [0, 8]]), ("f16", [[1, 8], [0, 16]]), ("f119", [[16, 8], [0, 2], [1, 8]]),
-            ("f4", [[1, 32], [0, 4]]), ("f111", [[32, 4], [0, 2], [1, 16]])]
+    emit("G", [lambda: g.iota(T.XI[:], [[1, 208]], -48, 0, allow_small_or_imprecise_dtypes=True)], (), ["XI"])
 
-    def fld(n):
-        j = [x[0] for x in flds].index(n)
-        return T.MF[:, 128 * j:128 * j + 128]
+    def X(off, w):
+        return T.XI[:, 48 + off:48 + off + w]
 
-    for n, pat in flds:
-        emit("G", [lambda: g.iota(fld(n), pat, 0, 0, allow_small_or_imprecise_dtypes=True)], (), [n])
-    ints = [("P", 5, 7), ("rho", 4, 1), ("s", 0, 7), ("h3", 3, 1), ("i", 0, 15), ("k6", 6, 1), ("grp", 4, 15), ("blk", 3, 31), ("b0", 0, 1),
-            ("b1", 1, 1), ("k31", 0, 31), ("b5", 5, 1)]
+    def fld(n, w=128):
+        j = [x[0] for x in FLD].index(n)
+        return T.MF[:, 512 * j:512 * j + w]
+
+    def field(lo, hi):
+        for n, pat, base in FLD[lo:hi]:
+            w = 1
+            for st, c in pat:
+                w *= c
+            emit("G", [lambda: g.iota(fld(n, w), pat, base, 0, allow_small_or_imprecise_dtypes=True)], (), [n])
+
+    field(0, 3)
+    ints = [("rho", 4, 1), ("h3", 3, 1), ("X0", 0, 103), ("i", 0, 15), ("k63", 0, 63),
+            ("s", 0, 7), ("g16", 0, 112), ("k96", 0, 96), ("blk", 3, 31), ("blk2", 2, 30), ("k111", 0, 111), ("b0", 0, 1), ("b1", 1, 1)]
     names = ["k"] + [x[0] for x in ints]
 
     def colints(lo, hi):
@@ -184,39 +191,29 @@ def rank_program(g, core, T, topo):
         else:
             ts(col(n), col(a), float(m), A.mult, d, A.add, R, ["c_" + n])
 
-    def mat(dst, name, f, fr, h, w, wn=None):
-        ts(dst, f, col(h), A.is_equal, w if wn is None else col(wn), A.mult, [fr, "c_" + h] + ([] if wn is None else ["c_" + wn]), [name])
+    def mat(name, f, h, w):
+        dst = M(name)
+        n = dst.shape[1]
+        src, fr = (X(f, n), "XI") if isinstance(f, int) else (fld(f, n), f)
+        ts(dst, src, col(h), A.is_equal, col(w) if isinstance(w, str) else w, A.mult, [fr, "c_" + h] + (["c_" + w] if isinstance(w, str) else []), [name])
 
-    Xm, Xs = T.XI[:, 0:128], T.XI[:]
-    colints(0, 6)
-    lin("X0", "P", 32, "s", "V")
+    colints(0, 9)
     lin("n0", "rho", -1, 1.0, "V")
     lin("OXn", "h3", 16, "X0", "V")
-    lin("sa", "rho", -32, "k")
-    lin("SWh", "sa", 1, 16.0)
-    lin("KP0", "k6", -64, "SWh")
-    lin("KP1", "KP0", 1, 64.0)
-    lin("wa0", "k6", 1, -1.0)
-    lin("wa1", "k6", -1, 0.0)
-    lin("sg64", "rho", 2.0 / 64, -1.0 / 64)
-    lin("t64", "i", 16, 0.0)
-    lin("OXl", "OXn", 1, 8.0, "V")
-    colints(6, len(ints))
-    for h in (0, 1):
-        mat(MB("OXH%d" % h), "OXH%d" % h, Xm, "XI", "OXn", None, ["n0", "rho"][h])
-        sc(MB("OXB%d" % h), MB("OXH%d" % h), 65.0, ["OXH%d" % h], ["OXB%d" % h])
-    for h in (0, 1):
-        mat(MB("OXL%d" % h), "OXL%d" % h, Xm, "XI", "OXl", None, ["n0", "rho"][h])
-    for a in (0, 1):
-        for hl in (0, 1):
-            mat(MH("KP%d%d" % (a, hl)), "KP%d%d" % (a, hl), Xm, "XI", "KP%d" % hl, None, "wa%d" % a)
-    for p in range(4):
-        lin("kr%d" % p, "k", 1, -32.0 * p)
-    for n, a, m, add in (("nb5", "b5", -1, 1.0), ("pa", "h3", -16, "X0"), ("xa", "P", 128, 0.0), ("pb", "rho", 8, "pa")):
+    for n, a, m, add in (("sa", "rho", -32, "k"), ("sg64", "rho", 2.0 / 64, -1.0 / 64), ("t64", "i", 16, 0.0), ("pa", "h3", -16, "X0"),
+                         ("xa", "k96", 4, 0.0), ("PERMh", "rho", 8, "pa"), ("xb", "h3", 64, "xa"), ("sent", "h3", -64, 64.0), ("w64", "h3", -63, 64.0),
+                         ("ta", "rho", -16, "X0"), ("g0", "h3", -1, 1.0), ("ot", "rho", -32, "g16"), ("wz", "s", -65536, 13 * 32768.0),
+                         ("SWh", "sa", 1, 16.0)):
         lin(n, a, m, add)
-    for j, (sh, m) in enumerate([(7, 127), (6, 1), (0, 63)]):
+    mat("OX0", -8, "OXn", "n0")
+    mat("OX1", -8, "OXn", "rho")
+    fill(M("ONES"), 1.0, ["ONES"])
+    fill(T.W[:, 4096:4160], -BIG, ["Wz"])
+    mat("RW", "f31", "k63", 1.0)
+    for j, (sh, m) in enumerate([(6, 1), (7, 127), (0, 63)]):
         ts(T.FI[:, 128 * j:128 * j + 128], T.OI[:], sh, A.logical_shift_right, m, A.bitwise_and, ["OI"], ["FI%d" % j])
-    cp("V", T.FB[:], T.FI[:], ["FI0", "FI1", "FI2"], ["FB"])
+    ts(T.FB[:, 0:128], T.FI[:, 0:128], 65.0, A.mult, None, None, ["FI0"], ["FB0"])
+    cp("V", T.FB[:, 128:384], T.FI[:, 128:384], ["FI1", "FI2"], ["FB1"])
 
     def dst(cs):
         return [DstId(rid=topo.addr(c)[0], pnc=topo.addr(c)[1]) for c in cs]
@@ -229,16 +226,12 @@ def rank_program(g, core, T, topo):
 
     def send(x):
         w, k, near = EX[x]
-        pre("G", [x + "s0"], [])
-        sem = T.sem["r%d%s" % (rank, x)]
+        pre("G", [y + "s0" for y in (x,) + near], [])
         one = [(same[(idx + j) % 4], j) for j in range(1, 4 - k)]
         both = [(side[(idx + j) % 4], j + o) for j in range(4 - k, 4) for side, o in ((same, 0), (other, 4))]
-
-        def off(to):
-            return RemoteDMATransfer(dst_ids=dst([cores[r] for r, j in to]), dma_engine_mask=sum(1 << e for e in eo), remote_sem=sem,
-                                     srcs=[blocks(x, 0, 1)], dsts=[blocks(x, j, j + 1) for r, j in to])
-
-        trs = [off(one + both)]
+        to = one + both
+        trs = [RemoteDMATransfer(dst_ids=dst([cores[r] for r, j in to]), dma_engine_mask=sum(1 << e for e in eo), remote_sem=T.sem["r%d%s" % (rank, x)],
+                                 srcs=[blocks(x, 0, 1)], dsts=[blocks(x, j, j + 1) for r, j in to])]
         n = len(es) // max(len(near), 1)
         for i, y in enumerate(near):
             trs.append(RemoteDMATransfer(dst_ids=dst([mate]), dma_engine_mask=sum(1 << e for e in es[n * i:n * i + n]),
@@ -249,58 +242,31 @@ def rank_program(g, core, T, topo):
         for j in [1, 2, 3] + list(range(8 - k, 8)):
             arrive("r%d%s" % (at[j], x), len(eo), [x + "s%d" % j])
 
-    def forward(x, free):
+    def forward(x, j0=1, j1=0):
         w, k, near = EX[x]
-        if k == 3:
+        j1 = j1 or 4 - k
+        if j0 == j1:
             return
-        pre("G", [x + "s%d" % j for j in range(1, 4 - k)], [])
-        e = es if free else topo.engines(core, mate)
-        g.remote_dma(blocks(x, 5, 8 - k), blocks(x, 1, 4 - k), T.sem["n" + x], T.sem["f" + x], topo.addr(mate)[1], topo.addr(mate)[0], sum(1 << i for i in e))
-        toks_all["f" + x] = len(e)
-        arrive("n" + x, len(e), [x + "s%d" % j for j in range(5, 8 - k)])
+        n, f = "n%d%s" % (j0, x), "f%d%s" % (j0, x)
+        pre("G", [x + "s%d" % j for j in range(j0, j1)], [])
+        g.remote_dma(blocks(x, 4 + j0, 4 + j1), blocks(x, j0, j1), T.sem[n], T.sem[f], topo.addr(mate)[1], topo.addr(mate)[0], sum(1 << i for i in es))
+        toks_all[f] = len(es)
+        arrive(n, len(es), [x + "s%d" % j for j in range(4 + j0, 4 + j1)])
 
-    fa, fb, low = T.FB[:, 0:128], T.FB[:, 128:256], T.FB[:, 256:384]
-    for h, bank in ((0, "RV"), (1, "NP")):
-        mms([(T[bank][:, 0:128], MB("OXH%d" % h), fa, True, False), (T[bank][:, 0:128], MB("OXB%d" % h), fb, False, False),
-             (T[bank][:, 0:128], MB("OXL%d" % h), low, False, True)], ["FB", "OXH%d" % h, "OXB%d" % h, "OXL%d" % h], [bank + ".x"], [bank])
-    for h, bank in ((0, "RV"), (1, "NP")):
-        for b in (0, 1):
-            c0 = 128 * b + 64 * h
-            cp("V" if h == 0 else "S", T.LOi[:, c0:c0 + 64], T[bank][:, 64 * b:64 * b + 64], [bank + ".x"], ["LOio%d%d" % (h, b)], [bank])
-    wr["LOis0"] = sum((wr["LOio%d%d" % (h, b)] for h in (0, 1) for b in (0, 1)), [])
-    send("LOi")
+    fs = [T.FB[:, 128 * j:128 * j + 128] for j in range(3)]
+    mms([(T.RV[:, 128 * b + 64 * h:128 * b + 64 * h + 64], M("OX%d" % h, 0 if j == 2 else 8), fs[j][:, 64 * b:64 * b + 64], j == 0, j == 2)
+         for b in (0, 1) for h in (0, 1) for j in range(3)], ["FB0", "FB1", "OX0", "OX1"], ["RV.r"], ["RV"])
 
     def pack(x, cols):
         for o, i, n in cols:
             for hl, src, name in ((0, T.HI, "HI"), (1, T.LO, "LO")):
-                mms([(T.UP[:, 384 + 128 * a + o:384 + 128 * a + o + n], MH("KP%d%d" % (a, hl)), src[:, i:i + n], hl == 0, hl == 1) for a in (0, 1)],
-                    [name, "KP0%d" % hl, "KP1%d" % hl], ["UPa.r", "UPb.r"] if hl == 0 and o == 0 else ["UP.%d.%d" % (hl, o)], ["UPa", "UPb"])
+                mms([(T.UP[:, 384 + 128 * a + o:384 + 128 * a + o + n], M("KP", 128 * a + 64 - 64 * hl), src[:, i:i + n], hl == 0, hl == 1) for a in (0, 1)],
+                    [name, "KP"], ["UPa.r", "UPb.r"] if hl == 0 and o == 0 else ["UP.%d.%d" % (hl, o)], ["UPa", "UPb"])
         cp("V", blocks(x, 0, 1), T.UP[:, 384:640], ["UPa.r", "UPb.r", "UP.1.%d" % cols[-1][0]], [x + "s0"], ["UPa", "UPb"])
-
-    ts(T.HI[:], T.ST[:], col("sg64"), A.mult, col("t64"), A.add, ["ST", "c_sg64", "c_t64"], ["HI"])
-    ts(T.K0[:, 256:512], T.ST[:], col("sg64"), A.mult, col("t64"), A.add, ["ST", "c_sg64", "c_t64"], ["K0.y"], ["K0"])
-    tt(T.LO[:], T.K0[:, 256:512], T.HI[:], A.subtract, ["K0.y", "HI"], ["LO"], ["K0"])
-    for b in (0, 1):
-        pack("LW%d" % b, [(64 * h, 128 * h + 64 * b, 64) for h in (0, 1)])
-        send("LW%d" % b)
-    emit("G", [lambda: g.iota(T.MKI[:], [[0, 9], [1, 8], [0, 16]], 0, 0, allow_small_or_imprecise_dtypes=True)], (), ["MKI"])
-    forward("LOi", True)
-    forward("LW0", True)
-    forward("LW1", True)
-    for n, a, m, add in (("PERMh", "pb", 1, 16.0), ("xb", "h3", 64, "xa"), ("sent", "h3", -64, 64.0), ("own15", "grp", 16, 15.0), ("w64", "h3", -63, 64.0),
-                         ("bf", "rho", -4, "blk"), ("ot", "rho", -32, "own15"), ("ta", "rho", -16, "X0"), ("g0", "h3", -1, 1.0), ("blkf", "bf", 1, 2.0),
-                         ("oth15", "ot", 1, 16.0), ("T0", "ta", 1, 16.0), ("T8", "ta", 1, 24.0), ("bl2", "blkf", 2, 0.0), ("bl3", "blkf", 2, 1.0),
-                         ("a0", "h3", BIG, -BIG), ("a1", "h3", -BIG, 0.0), ("k111", "rho", -16, "k"), ("wz", "s", -65536, 13 * 32768.0),
-                         ("thr1", "b0", 1, -0.5), ("thr2", "b1", 1, -0.5)):
-        lin(n, a, m, add)
-    for p in range(4):
-        mat(MB("REP%d" % p), "REP%d" % p, fld("f31"), "f31", "kr%d" % p, 1.0)
-    for p in (0, 1):
-        mat(MH("RW%d" % p), "RW%d" % p, fld("f31"), "f31", "k31", None, ["nb5", "b5"][p])
 
     OTALL = ["OTz", "OTy"] + ["OT%d%d%s" % (b, r, z) for b in (0, 1) for r in range(8) for z in "ab"]
     WALL = ["Wz"] + ["W%d%d%s" % (b, r, z) for b in (0, 1) for r in range(8) for z in "ab"]
-    rb = [("UP", 0, "UPa"), ("UP", 512, "UPb"), ("YY", 0, "YY"), ("DD", 0, "DD"), ("RV", 0, "RV"), ("NP", 0, "NP")]
+    rb = [("YY", 0, "YY"), ("DD", 0, "DD"), ("UP", 0, "UPa"), ("UP", 512, "UPb"), ("RV", 0, "RV"), ("NP", 0, "NP")]
     nb = [0]
 
     def rep(x, j, b, q):
@@ -313,11 +279,14 @@ def rank_program(g, core, T, topo):
             outs = [T[buf][:, c0 + 128 * (p - n * i):c0 + 128 * (p - n * i) + 128] for p in ps]
             if x[1] == "O":
                 s0 = w * j + (128 * b if x == "LOi" else 0)
-                ms = [(o, MB("REP%d" % p), T[x][:, s0:s0 + 128], True, True) for o, p in zip(outs, ps)]
-                mr, tab, reg = ["REP%d" % p for p in range(4)], T.OT, "OT"
+                ms = [(o, M("REP", 128 * p), T[x][:, s0:s0 + 128], True, True) for o, p in zip(outs, ps)]
+                mr, tab, reg = ["REP"], T.OT, "OT"
+            elif TWO and x in ("LW2", "LW3"):
+                ms = [(o, M("RP", 128 * p), T[x][:, w * j + 128 * hl:w * j + 128 * hl + 128], hl == 0, hl == 1) for o, p in zip(outs, ps) for hl in (0, 1)]
+                mr, tab, reg = ["RP"], T.W, "W"
             else:
-                ms = [(o, MH("RW%d" % (p & 1)), T[x][:, w * j + 128 * (p >> 1):w * j + 128 * (p >> 1) + 128], True, True) for o, p in zip(outs, ps)]
-                mr, tab, reg = ["RW0", "RW1"], T.W, "W"
+                ms = [(o, M("RW", 128 * (p & 1)), T[x][:, w * j + 128 * (p >> 1):w * j + 128 * (p >> 1) + 128], True, True) for o, p in zip(outs, ps)]
+                mr, tab, reg = ["RW"], T.W, "W"
             mms(ms, [x + "s%d" % j] + mr, [bank + ".r"], [bank])
             cp(qi, tab[:, d0 + 128 * n * i:d0 + 128 * n * (i + 1)], T[buf][:, c0:c0 + 128 * n], [bank + ".r"],
                ["%s%d%d%s" % (reg, b, at[j], z) for z in ("ab" if n == 4 else "ab"[i])], [bank])
@@ -330,107 +299,114 @@ def rank_program(g, core, T, topo):
         emit("S", [lambda: g.scalar.activation(out=T["XE%d" % b][:], in_=T.W[:, d0:d0 + 512].indirect(T.XL[:]), func=AF.Copy)],
              ["W%d%da" % (b, rank), "W%d%db" % (b, rank), "XL"], ["XE%d" % b])
 
-    mat(MB("PERM1"), "PERM1", Xm, "XI", "PERMh", 1.0)
-    mat(MB("PERM64"), "PERM64", Xm, "XI", "PERMh", 64.0)
-    mat(MB("PERM65"), "PERM65", Xm, "XI", "PERMh", 64.0 * 65)
+    mat("KP", "f63", "sa", -1.0)
+    ts(T.HI[:], T.ST[:], col("sg64"), A.mult, col("t64"), A.add, ["ST", "c_sg64", "c_t64"], ["HI"])
+    cp("S", blocks("LOi", 0, 1), T.RV[:, 0:256], ["RV.r"], ["LOis0"], ["RV"])
+    send("LOi")
+    ts(T.K0[:, 256:512], T.ST[:], col("sg64"), A.mult, col("t64"), A.add, ["ST", "c_sg64", "c_t64"], ["K0.y"], ["K0"])
+    tt(T.LO[:], T.K0[:, 256:512], T.HI[:], A.subtract, ["K0.y", "HI"], ["LO"], ["K0"])
+    mat("REP", "f31", "k", 1.0)
+    mat("PERM64", -16, "PERMh", 64.0)
+    mat("PERM1", -16, "PERMh", 1.0)
+    pack("LW0", [(64 * h, 128 * h, 64) for h in (0, 1)])
+    send("LW0")
     rep("LW0", 0, 0, "S")
-    mms([(T.K1[:, 0:128], MB("PERM64"), fa, True, False), (T.K1[:, 0:128], MB("PERM65"), fb, False, False), (T.K1[:, 0:128], MB("PERM1"), low, False, True)],
-        ["FB", "PERM64", "PERM65", "PERM1"], ["K1.o"], ["K1"])
-    ts(T.XL[:], T.XI[:, 0:64], col("xb"), A.add, None, None, ["XI", "c_xb"], ["XL"])
+    ts(T.XL[:], X(0, 64), col("xb"), A.add, None, None, ["XI", "c_xb"], ["XL"])
+    colints(9, len(ints))
+    pack("LW1", [(64 * h, 128 * h + 64, 64) for h in (0, 1)])
+    lin("bl", "rho", -8, "blk2", "V")
+    send("LW1")
+    field(3, len(FLD))
+    forward("LOi", 1, 2)
+    forward("LOi", 2, 4)
+    forward("LW0")
+    forward("LW1")
     expand(0)
+    mms([(T.K1[:, 0:128], M("PERM1" if j == 2 else "PERM64"), fs[j], j == 0, j == 2) for j in range(3)], ["FB0", "FB1", "PERM64", "PERM1"], ["K1.o"], ["K1"])
     rep("LW1", 0, 1, "S")
     for b in (0, 1):
         rep("LOi", 0, b, "S")
-    mat(MB("IB"), "IB", Xm, "XI", "k", 1.0)
-    emit("V", [lambda: g.vector.memset(T.W[:, 4096:4160], -BIG)], (), ["Wz"])
-    emit("V", [lambda: g.vector.memset(MB("ONES"), 1.0)], (), ["ONES"])
-    emit("V", [lambda: g.vector.memset(T.MSL[:, 0:4], 0.0), lambda: g.vector.memset(T.MSL[:, 148:160], 0.0)], (), ["GUARD"])
-    emit("V", [lambda: g.vector.memset(T.RS[:], 0.0)], (), ["RS"])
-    ones = 128 * MATB.index("ONES")
-    ts(T.OT[:, 4096:4160], T.MBF[:, ones:ones + 64], col("sent"), A.mult, None, None, ["ONES", "c_sent"], ["OTz"])
-    ts(T.OT[:, 8256:8272], T.MBF[:, ones:ones + 16], col("sent"), A.mult, None, None, ["ONES", "c_sent"], ["OTy"])
+    ts(T.OT[:, 4096:4112], M("ONES", 0, 16), col("sent"), A.mult, None, None, ["ONES", "c_sent"], ["OTz"])
+    ts(T.OT[:, 8256:8272], M("ONES", 0, 16), col("sent"), A.mult, None, None, ["ONES", "c_sent"], ["OTy"])
+    fill(T.OT[:, 4112:4160], 0.0, ["OTx"])
+    OTALL.append("OTx")
+    fill(T.RS[:], 0.0, ["RS"])
     cp("V", T.OF[:], T.K1[:, 0:128], ["K1.o"], ["OF0", "OF1"], ["K1"])
-    emit("V", [lambda: g.vector.memset(T.RS[:, 0::8], -BIG)], (), ["RS"])
-    mat(SL("BKO"), "BKO", Xs, "XI", "own15", None, "w64")
+    mat("BKO", -15, "g16", "w64")
+    fill(T.RS[:, 0::8], -BIG, ["RS"])
     cp("V", T.OL[:], T.OF[:], ["OF0", "OF1"], ["OL0", "OL1"])
-    mat(SL("OWN"), "OWN", Xs, "XI", "own15", 1.0)
-    mat(T.R32[:, 4:148], "R32", Xs, "XI", "own15", 32.0)
-    mat(SL("OTH"), "OTH", Xs, "XI", "oth15", 1.0)
-    mat(MX("SW"), "SW", Xm, "XI", "SWh", 1.0)
-    mat(MX("NSW"), "NSW", Xm, "XI", "SWh", -1.0)
-    mat(MB("YM"), "YM", fld("f8"), "f8", "blk", -65536.0)
-    emit("G", [lambda: g.affine_select(MB("YM"), MB("YM"), [[1, 128]], A.is_gt, 0.0, 0, -1)], ["YM"], ["YM"])
-    emit("G", [lambda: g.affine_select(MB("YM"), MB("YM"), [[1, 128]], A.not_equal, 32768.0, 0, -1)], ["YM"], ["YM"])
+    ts(T.MK[:, 0:288], fld("f16", 288), col("s"), A.is_equal, None, None, ["f16", "c_s"], ["MK0"])
+    mat("OWN", -19, "g16", 1.0)
+    mat("R32", -15, "g16", 32.0)
+    cp("V", T.MK[:, 288:544], T.MK[:, 32:288], ["MK0"], ["MK1"])
+    mat("OTH", -31, "ot", 1.0)
+    mat("SW", -16, "sa", 1.0)
+    cp("V", T.MK[:, 544:1056], T.MK[:, 32:544], ["MK0", "MK1"], ["MK2"])
+    mat("YM", "f8", "blk", -65536.0)
+    emit("G", [lambda: g.affine_select(M("YM"), M("YM"), [[1, 128]], A.is_gt, 0.0, 0, -1)], ["YM"], ["YM"])
+    emit("G", [lambda: g.affine_select(M("YM"), M("YM"), [[1, 128]], A.not_equal, 32768.0, 0, -1)], ["YM"], ["YM"])
 
     def partners(js):
         for j in js:
-            k0, d = 160 + 144 * SLID.index("BD%d" % j), DELTA[j]
-            tt(T.MSL[:, k0:k0 + 144], T.R32[:, 4:148], T.MSL[:, 4 - d:148 - d], A.subtract, ["R32", "OWN", "GUARD"], ["BD%d" % j])
+            tt(M("BD%d" % j), M("R32"), M("OWN", 4 - DELTA[j], 144), A.subtract, ["R32", "OWN"], ["BD%d" % j])
 
     partners((0, 1))
-    mat(MX("CH0"), "CH0", fld("f4"), "f4", "bl2", 1.0)
-    mat(MX("CH1"), "CH1", fld("f4"), "f4", "bl3", 1.0)
-    mat(MB("ZC0"), "ZC0", fld("f4"), "f4", "bl2", None, "wz")
-    mat(MB("ZC1"), "ZC1", fld("f4"), "f4", "bl3", None, "wz")
-    mat(MB("ENT0"), "ENT0", Xm, "XI", "T0", None, "w64")
-    mat(MB("ENT1"), "ENT1", Xm, "XI", "T8", None, "w64")
+    mat("CH", "f4", "bl", 1.0)
+    mat("ZC", "f4", "bl", "wz")
+    mat("ENT", -24, "ta", "w64")
+    ts(M("ANY0"), fld("f16"), 16.0, A.mult, col("g16"), A.is_equal, ["f16", "c_g16"], ["ANY0"])
     for h, gn in ((0, "g0"), (1, "h3")):
-        mat(MB("ANY%d" % h), "ANY%d" % h, fld("f16"), "f16", "grp", None, "a%d" % h)
-        mat(MB("KX%d" % h), "KX%d" % h, fld("f119"), "f119", "T0", None, gn)
-    mat(MX("ISWH"), "ISWH", fld("f111"), "f111", "k111", 0.5)
-    mat(MB("KEEPN"), "KEEPN", Xm, "XI", "k", -16384.0)
-    ts(T.MK[:], T.MKI[:], col("s"), A.is_equal, None, None, ["MKI", "c_s"], ["MK"])
+        mat("KX%d" % h, "f119", "ta", gn)
+    mat("ISWH", "f111", "k111", 0.5)
+    mat("IB", 0, "k", 1.0)
+    if TWO:
+        mat("RP", "f31", "SWh", -1.0)
 
     def late2():
+        sc(M("KEEPN"), M("IB"), -16384.0, ["IB"], ["KEEPN"])
         for h in (0, 1):
-            sc(MB("KN%d" % h), MB("KX%d" % h), -256.0, ["KX%d" % h], ["KN%d" % h])
+            sc(M("KN%d" % h), M("KX%d" % h), -256.0, ["KX%d" % h], ["KN%d" % h])
+        sc(M("NSW"), M("SW"), -1.0, ["SW"], ["NSW"])
         lin("nt64", "i", -16, 0.0)
+        lin("a0", "h3", BIG, -BIG)
+        lin("a1", "h3", -BIG, 0.0)
         lin("c8", "rho", 2.0 / 256, -1.0 / 256)
+        act(M("TMN"), M("IB"), col("nt64"), 0.0, ["IB", "c_nt64"], ["TMN"])
+        act(M("ANY1"), M("ANY0"), col("a1"), 0.0, ["ANY0", "c_a1"], ["ANY1"])
+        act(M("ANY0"), M("ANY0"), col("a0"), 0.0, ["ANY0", "c_a0"], ["ANY0"])
+        act(M("CM"), M("IB"), col("c8"), 0.0, ["IB", "c_c8"], ["CM"])
         lin("tm", "i", 16, MAGIC)
-        lin("s64", "rho", 128, -64.0)
-        act(MB("TMN"), MB("IB"), col("nt64"), 0.0, ["IB", "c_nt64"], ["TMN"])
-        act(MB("CM"), MB("IB"), col("c8"), 0.0, ["IB", "c_c8"], ["CM"])
 
     def late3():
-        lin("iv", "rho", -8, "OXn")
-        lin("INVh", "iv", 1, 8.0)
-        mat(MX("INVF"), "INVF", Xm, "XI", "INVh", 1.0)
-        sc(MX("INVF2"), MX("INVF"), 2.0, ["INVF"], ["INVF2"])
-        for j, c in enumerate([-1.0, -8256.0]):
-            sc(MB("INV%d" % j), MX("INVF"), c, ["INVF"], ["INV%d" % j])
+        lin("iv", "rho", -8, "OXn", "V")
+        lin("s64", "rho", 128, -64.0, "V")
+        mat("INVF", -8, "iv", 1.0)
+        mat("INV0", -8, "iv", 64.0)
+        sc(M("INV1"), M("INVF"), -4128.0, ["INVF"], ["INV1"])
 
     def lists_gather(t):
         b = t & 1
-        tt(T.GM[:], T.OT[:].indirect(T.OL[:, 64 * b:64 * b + 64]), T.MK[:, 16 * t:16 * t + 1024], A.mult, OTALL + ["OL%d" % b, "MK"], ["GM"])
+        tt(T.GM[:], T.OT[:].indirect(T.OL[:, 64 * b:64 * b + 64]), T.MK[:, 16 * t:16 * t + 1024], A.mult, OTALL + ["OL%d" % b, "MK0", "MK1", "MK2"], ["GM"])
 
     def lists(t):
         b = t & 1
         mms([(T.K0[:, 0:64], SL("BKO", q), T.GM[:, q::16], q == 0, q == 15) for q in range(16)], ["GM", "BKO"], ["K0.k"], ["K0"])
-        ts(T.HAS[:], T.OF[:, 64 * b:64 * b + 64], EMPTY, A.not_equal, None, None, ["OF%d" % b], ["HAS"])
-        ts(T.KC[:], T.K0[:, 0:64], KOFF, A.add, None, None, ["K0.k"], ["KC"], ["K0"])
+        thr = "b0" if t == 0 else "b1"
+        ts(T.H1[:], T.OF[:, 64 * b:64 * b + 64], EMPTY, A.is_equal, col(thr), A.add, ["OF%d" % b, "c_" + thr], ["H1"])
+        ts(T.KC[:], T.K0[:, 0:64], 32768.0 - 8256.0, A.add, None, None, ["K0.k"], ["KC"], ["K0"])
         cp("V", T.KL[:, 0:64], T.K0[:, 0:64], ["K0.k"], ["KL0"], ["K0"])
 
-    def tail(x, b):
-        js = order(x)[4:]
-        rep(x, js[0], b, "S")
-        rep(x, js[1], b, "V")
-        mms([(T.K1[:, 0:64], MX("SW"), T.KC[:], True, True)], ["KC", "SW"], ["K1.k"], ["K1"])
-        ts(T.KL[:, 64:128], T.K1[:, 0:64], -KOFF, A.add, None, None, ["K1.k"], ["KL1"], ["K1"])
-        for j in js[2:]:
-            rep(x, j, b, "VS")
-
-    def fields(b):
-        n = T.OF[:, 64 * b:64 * b + 64]
-        cp("V", T.YI[:], n, ["OF%d" % b], ["YI"])
-        ts(T.YFB[:, 64:128], n, EMPTY + 63.5, A.is_gt, None, None, ["OF%d" % b], ["YFB1"])
-        ts(T.YFI[:], T.YI[:], 63, A.bitwise_and, None, None, ["YI"], ["YFI"])
-        cp("V", T.YFB[:, 0:64], T.YFI[:], ["YFI"], ["YFB0"])
+    def swapped():
+        mms([(T.K1[:, 0:64], M("SW"), T.KC[:], True, True)], ["KC", "SW"], ["K1.k"], ["K1"])
+        ts(T.KL[:, 64:128], T.K1[:, 0:64], 8256.0 - 32768.0, A.add, None, None, ["K1.k"], ["KL1"], ["K1"])
 
     def natural(b):
-        mms([(T.YY[:, 128:192], MX("INVF2"), T.OF[:, 64 * b:64 * b + 64], True, False)]
-            + [(T.YY[:, 128:192], MB("INV%d" % j), T.YFB[:, 64 * j:64 * j + 64], False, j == 1) for j in range(2)],
-            ["OF%d" % b, "YFB0", "YFB1", "INVF2", "INV0", "INV1"], ["YY.n"], ["YY"])
-        cp("S", T["YO%d" % b][:], T.YY[:, 128:192], ["YY.n"], ["YO%d" % b], ["YY"])
+        n = T.OF[:, 64 * b:64 * b + 64]
+        ts(T.YH[:], n, 1.0 / 64, A.mult, 1025.0 - 63.0 / 128, A.add, ["OF%d" % b], ["YH"])
+        emit("S", [lambda: g.scalar.activation(out=T.YB[:], in_=n, func=AF.Sign, bias=-(EMPTY + 63.5))], ["OF%d" % b], ["YB"])
+        mms([(T.YY[:, 128:192], M("INVF"), n, True, False), (T.YY[:, 128:192], M("INV0"), T.YH[:], False, False),
+             (T.YY[:, 128:192], M("INV1"), T.YB[:], False, True)], ["OF%d" % b, "YH", "YB", "INVF", "INV0", "INV1"], ["YY.n"], ["YY"])
+        act(T["YO%d" % b][:], T.YY[:, 128:192], 1.0, -65600.0 - 4128.0, ["YY.n"], ["YO%d" % b], ["YY"])
         dmas("Y", [(T.yo[:, 64 * b:64 * b + 64], T["YO%d" % b][:])], "dO%d" % b, ["YO%d" % b], [])
 
     def round_(t):
@@ -443,15 +419,15 @@ def rank_program(g, core, T, topo):
         cp("S", T.UP[:], T.U[:], ["U"], ["UPa.r", "UPb.r"], ["UPa", "UPb"])
         if t == 0:
             late2()
-        if nx:
-            expand(1 - b)
+        if t == 1:
+            expand(0)
         XE = T["XE%d" % b]
         tt(T.VO[:], Wt.indirect(T.KL[:, 0:64]), XE[:], A.is_gt, WALL + ["KL0"] + xe, ["VO"])
         mms([(T.RV[:, 0:64], SL("OWN", q), T.VO[:, q::16], q == 0, False) for q in range(16)], ["VO", "OWN"], ["RV.v"], ["RV"])
         tt(T.VX[:], Wt.indirect(T.KL[:, 64:128]), XE[:], A.is_lt, WALL + ["KL1"] + xe, ["VX"])
         mms([(T.RV[:, 0:64], SL("OTH", q), T.VX[:, q::16], False, q == 15) for q in range(16)], ["VX", "OTH"], ["RV.v2"], ["RV"])
         st = {1: [(0, 1, 4), (2, 3, 4)], 2: [(0, 2, 4), (1, 3, 4)], 3: [(0, 3, 4), (1, 2, 4)]}[m]
-        thr = "thr1" if m == 1 else "thr2"
+        thr = "b0" if m == 1 else "b1"
         nq = 0
         for u, v, s in st:
             for y, z in ((u, v), (v, u)):
@@ -463,36 +439,34 @@ def rank_program(g, core, T, topo):
         dd = ["DD.d%d" % y for u, v, s in st for y in (u, v)]
         ts(T.R1[:], T.RV[:, 0:64], 1024.0, A.mult, col(thr), A.add, ["RV.v", "RV.v2", "c_" + thr], ["R1"], ["RV"])
         tt(T.REV[:], T.DD[:, 0:64], T.R1[:], A.is_ge, dd + ["R1"], ["REV"], ["DD"])
-        mms([(T.YY[:, 0:64], MB("YM"), T.REV[:], True, True)], ["REV", "YM"], ["YY.y"], ["YY"])
-        mms([(T.K1[:, 64:96], MB("ZC%d" % e), T.REV[:, 32 * e:32 * e + 32], e == 0, False) for e in (0, 1)], ["REV", "ZC0", "ZC1"], ["K1.z"], ["K1"])
-        ts(T.ND[:], T.DD[:, 0:64], col(thr), A.is_ge, None, None, dd + ["c_" + thr], ["ND"], ["DD"])
+        mms([(T.YY[:, 0:64], M("YM"), T.REV[:], True, True)], ["REV", "YM"], ["YY.y"], ["YY"])
+        mms([(T.K1[:, 64:96], M("ZC", 4 - 4 * e), T.REV[:, 32 * e:32 * e + 32], e == 0, False) for e in (0, 1)], ["REV", "ZC"], ["K1.z"], ["K1"])
         tt(T.FK[:], T.YY[:, 0:64], T.KC[:], A.min, ["YY.y", "KC"], ["FK"], ["YY"])
-        mms([(T.K1[:, 64:96], MX("CH%d" % e), T.FK[:, 32 * e:32 * e + 32], False, e == 1) for e in (0, 1)], ["FK", "CH0", "CH1"], ["K1.c"], ["K1"])
-        ts(T.FF[:], T.YY[:, 0:64], 0.5, A.is_gt, None, None, ["YY.y"], ["FF"], ["YY"])
-        tt(T.NH[:], T.ND[:], T.HAS[:], A.mult, ["ND", "HAS"], ["NH"])
-        tt(T.KEEP[:], T.NH[:], T.FF[:], A.subtract, ["NH", "FF"], ["KEEP"])
-        mms([(T.NP[:, 0:64], MB("KEEPN"), T.KEEP[:], True, False)], ["KEEP", "KEEPN"], ["NP.n"], ["NP"])
-        ts(T.CL[:], T.K1[:, 64:96], 32768.0 - KOFF, A.add, 8256.0, A.min, ["K1.z", "K1.c"], ["CL"], ["K1"])
+        mms([(T.K1[:, 64:96], M("CH", 4 - 4 * e), T.FK[:, 32 * e:32 * e + 32], False, e == 1) for e in (0, 1)], ["FK", "CH"], ["K1.c"], ["K1"])
+        tt(T.H2[:], T.YY[:, 0:64], T.H1[:], A.max, ["YY.y", "H1"], ["H2"], ["YY"])
+        tt(T.KEEP[:], T.DD[:, 0:64], T.H2[:], A.is_ge, dd + ["H2"], ["KEEP"], ["DD"])
+        mms([(T.NP[:, 0:64], M("KEEPN"), T.KEEP[:], True, False)], ["KEEP", "KEEPN"], ["NP.n"], ["NP"])
+        ts(T.CL[:], T.K1[:, 64:96], 8256.0, A.add, None, None, ["K1.z", "K1.c"], ["CL"], ["K1"])
         if nx:
-            mms([(T.RV[:, 64 * h + 128:64 * h + 192], MB("KX%d" % h), T.KEEP[:], True, True) for h in (0, 1)], ["KEEP", "KX0", "KX1"], ["RV.k"], ["RV"])
+            mms([(T.RV[:, 64 * h + 128:64 * h + 192], M("KX%d" % h), T.KEEP[:], True, True) for h in (0, 1)], ["KEEP", "KX0", "KX1"], ["RV.k"], ["RV"])
         emit("V", [lambda: g.vector.tensor_copy(out=T.E[:, 0:256], in_=T.OT[:].indirect(T.CL[:, 0:16]))], OTALL + ["CL"], ["E0"])
         emit("S", [lambda: g.scalar.activation(out=T.E[:, 256:512], in_=T.OT[:].indirect(T.CL[:, 16:32]), func=AF.Copy)], OTALL + ["CL"], ["E1"])
-        mms([(T.NP[:, 32 * e:32 * e + 32], MB("ENT%d" % h), T.E[:, 8 * h + 4 * e::16], False, h == 1 and e == 1) for e in (0, 1) for h in (0, 1)],
-            ["E0", "E1", "ENT0", "ENT1"], ["NP.n2"], ["NP"])
+        mms([(T.NP[:, 32 * e:32 * e + 32], M("ENT", 8 - 8 * h), T.E[:, 8 * h + 4 * e::16], False, h == 1 and e == 1) for e in (0, 1) for h in (0, 1)],
+            ["E0", "E1", "ENT"], ["NP.n2"], ["NP"])
         tt(T.OK[:], T.OF[:, 64 * b:64 * b + 64], T.KEEP[:], A.mult, ["OF%d" % b, "KEEP"], ["OK"])
         if nx:
             old = T.LOi[:, 128 * b:128 * b + 128]
             tt(T.OXA[:], T.RV[:, 128:256], old, A.mult, ["RV.k", "LOis0"], ["OXA"], ["RV"])
             for h in (0, 1):
-                mms([(T.DD[:, 128 + 64 * h:192 + 64 * h], MB("KN%d" % h), T.KEEP[:], True, False)]
-                    + [(T.DD[:, 128 + 64 * h + 32 * e:160 + 64 * h + 32 * e], MB("IB"), T.E[:, 8 * h + 4 * e::16], False, e == 1) for e in (0, 1)],
+                mms([(T.DD[:, 128 + 64 * h:192 + 64 * h], M("KN%d" % h), T.KEEP[:], True, False)]
+                    + [(T.DD[:, 128 + 64 * h + 32 * e:160 + 64 * h + 32 * e], M("IB"), T.E[:, 8 * h + 4 * e::16], False, e == 1) for e in (0, 1)],
                     ["KEEP", "E0", "E1", "IB", "KN%d" % h], ["DD.x%d" % h], ["DD"])
         n = T.OF[:, 64 * b:64 * b + 64]
         tt(n, T.NP[:, 0:64], T.OK[:], A.max, ["NP.n", "NP.n2", "OK"], ["OF%d" % b], ["NP"])
         cp("V", ol, n, ["OF%d" % b], ["OL%d" % b])
         for h, bank in ((0, "K0"), (1, "K1")):
-            mms([(T[bank][:, 0:64], MX("NSW"), XE[:, 8 * h::16], True, False),
-                 (T[bank][:, 0:64], MB("TMN"), T.MBF[:, ones:ones + 64], False, False)], xe + ["NSW", "TMN", "ONES"], [bank + ".a"], [bank])
+            mms([(T[bank][:, 0:64], M("NSW"), XE[:, 8 * h::16], True, False),
+                 (T[bank][:, 0:64], M("TMN"), M("ONES", 0, 64), False, False)], xe + ["NSW", "TMN", "ONES"], [bank + ".a"], [bank])
         for h in (1, 2, 3):
             emit("S", [lambda: g.scalar.activation(out=T.U5[:, 256 * h:256 * h + 256], in_=Wt.indirect(T.OL[:, 64 * b + 16 * h:64 * b + 16 * h + 16]),
                                                    func=AF.Copy)], WALL + ["OL%d" % b], ["U5%d" % h])
@@ -502,30 +476,33 @@ def rank_program(g, core, T, topo):
         emit("V", [lambda: g.vector.tensor_copy(out=T.U5[:, 0:256], in_=Wt.indirect(T.OL[:, 64 * b:64 * b + 16]))], WALL + ["OL%d" % b], ["U50"])
         ts(T.HN[:], n, EMPTY, A.not_equal, None, None, ["OF%d" % b], ["HN"])
         for h, bank in ((0, "K0"), (1, "K1")):
-            mms([(T[bank][:, 0:64], MB("ANY%d" % h), T.HN[:], False, True)], ["HN", "ANY%d" % h], [bank + ".b"], [bank])
-        mms([(T.RV[:, 256:384], MB("CM"), MB("ONES"), True, False)], ["CM", "ONES"], ["RV.t"], ["RV"])
+            mms([(T[bank][:, 0:64], M("ANY%d" % h), T.HN[:], False, True)], ["HN", "ANY%d" % h], [bank + ".b"], [bank])
+        mms([(T.RV[:, 256:384], M("CM"), M("ONES"), True, False)], ["CM", "ONES"], ["RV.t"], ["RV"])
         for h in range(4):
             emit("V", [lambda: g.vector.tensor_tensor_scan(out=T.MX[:, 256 * h:256 * h + 256], data0=T.RS[:], data1=T.U5[:, 256 * h:256 * h + 256],
                                                            initial=-2.0 * BIG, op0=A.add, op1=A.max)], ["RS", "U5%d" % h], ["MX%d" % h])
         for h, bank in ((0, "K0"), (1, "K1")):
             tt(T.OWNW[:, 64 * h:64 * h + 64], T.MX[:, 7 + 8 * h::16], T[bank][:, 0:64], A.max, ["MX0", "MX1", "MX2", "MX3", bank + ".a", bank + ".b"],
                ["OWN%d" % h], [bank])
-        mms([(T.RV[:, 256:384], MX("ISWH"), T.OWNW[:], False, True)], ["OWN0", "OWN1", "ISWH"], ["RV.s"], ["RV"])
+        mms([(T.RV[:, 256:384], M("ISWH"), T.OWNW[:], False, True)], ["OWN0", "OWN1", "ISWH"], ["RV.s"], ["RV"])
         act(T.NP[:, 256:384], T.OWNW[:], 1.0, col("tm"), ["OWN0", "OWN1", "c_tm"], ["NP.t"], ["NP"])
+        if t == 0:
+            expand(1)
         if not nx:
-            fields(b)
             natural(b)
         ts(T.M1[:], T.RV[:, 256:384], 0.0, A.min, MAGIC, A.add, ["RV.s", "RV.t"], ["M1"], ["RV"])
         Y = T.K0[:, 256:384]
         if nx:
-            tt(T.HI[:, 0:128], T.NP[:, 256:384], T.M1[:], A.subtract, ["M1", "NP.t"], ["HI"], ["NP"])
+            hi, lo = (T["LW" + nx][:, 0:128], T["LW" + nx][:, 128:256]) if TWO else (T.HI[:, 0:128], T.LO[:, 0:128])
+            tt(hi, T.NP[:, 256:384], T.M1[:], A.subtract, ["M1", "NP.t"], ["HI"], ["NP"])
         tt(Y, T.NP[:, 256:384], T.M1[:], A.subtract, ["M1", "NP.t"], ["K0.y"], ["NP", "K0"])
         if nx:
-            tt(T.LO[:, 0:128], Y, T.HI[:, 0:128], A.subtract, ["K0.y", "HI"], ["LO"], ["K0"])
-            pack("LW" + nx, [(0, 0, 128)])
+            tt(lo, Y, hi, A.subtract, ["K0.y", "HI"], ["LW%ss0" % nx if TWO else "LO"], ["K0"])
+            if not TWO:
+                pack("LW" + nx, [(0, 0, 128)])
             send("LW" + nx)
-            forward("LO" + nx, True)
-            forward("LW" + nx, True)
+            forward("LO" + nx)
+            forward("LW" + nx)
         if t > 0:
             ts(T["YW%d" % b][:], Y, col("t64"), A.subtract, col("s64"), A.mult, ["K0.y", "c_t64", "c_s64"], ["YW%d" % b], ["K0"])
             for q, y, r0 in (("Y", T.yl, 16), ("Y" if nx else "S", T.yr, 0)):
@@ -536,7 +513,6 @@ def rank_program(g, core, T, topo):
                                          in_=T["YW%d" % b][32 * P + r0:32 * P + r0 + 16, 64 * h:64 * h + 64]).then_inc(T.sem["dY%d" % b], 16)
             toks_all["dY%d" % b] = 16 * 16
             if nx:
-                fields(b)
                 natural(b)
 
     for j in (4, 1, 2, 3):
@@ -544,32 +520,39 @@ def rank_program(g, core, T, topo):
         rep("LOi", j, 1, "S")
     for j in (4, 1, 2, 3):
         rep("LW0", j, 0, "VS"[j & 1])
-    rep("LW1", 4, 1, "S")
-    for j in (5, 6, 7):
-        rep("LOi", j, 0, "V")
-        rep("LOi", j, 1, "S")
-    lists_gather(0)
     ow = order("LW1")
-    for j in ow[2:4]:
+    for j in (5, 6, 7):
+        rep("LOi", j, 0, "S")
+        rep("LOi", j, 1, "V")
+        if j == 5:
+            rep("LW1", ow[1], 1, "S")
+            rep("LW1", ow[2], 1, "V")
+            rep("LW1", ow[3], 1, "VS")
+    lists_gather(0)
+    for j in ow[4:6]:
         rep("LW1", j, 1, "S")
     for j in (5, 6, 7):
-        rep("LW0", j, 0, "SSV"[j - 5])
+        rep("LW0", j, 0, "SVS"[j - 5])
+    rep("LW1", ow[7], 1, "S")
     lists(0)
-    tail("LW1", 1)
+    rep("LW1", ow[6], 1, "SV")
+    swapped()
     round_(0)
     for t, x, b in ((1, "2", 0), (2, "3", 1)):
         oo, ow = order("LO" + x), order("LW" + x)
         for i, j in enumerate(oo):
-            rep("LO" + x, j, b, "SV"[i & 1])
+            rep("LO" + x, j, b, "VS"[i & 1])
+        if t == 1:
+            late3()
         lists_gather(t)
+        partners((2 * t, 2 * t + 1))
         for j in ow[:3]:
             rep("LW" + x, j, b, "S")
         lists(t)
-        partners((2 * t, 2 * t + 1))
-        if t == 1:
-            late3()
         rep("LW" + x, ow[3], b, "S")
-        tail("LW" + x, b)
+        swapped()
+        for j in ow[4:]:
+            rep("LW" + x, j, b, "VS")
         round_(t)
     for s in SEMAPHORES:
         if toks_all.get(s, 0) > known["G"].get(s, 0):

@@ -3,28 +3,28 @@ from concourse.mybir import AluOpType as A, ActivationFunctionType as AF
 
 EX = {"LOi": (256, 0, ()), "LW0": (256, 0, ("LOi", "LW0")), "LW1": (256, 2, ("LW1",)), "LO2": (128, 3, ("LO2",)),
       "LW2": (256, 2, ("LW2",)), "LO3": (128, 3, ("LO3",)), "LW3": (256, 2, ("LW3",))}
-TWO = False
+CUT = [(0, 12, 32, 52, 64), (0, 16, 36, 52, 64)]
 BIG = 2.0 ** 23
 MAGIC = 1.5 * 2.0 ** 17
 EMPTY = 4096.0
 KOFF = 8192.0 * 3
-MATB = [("REP", 512), ("YM", 128), ("ZC", 136), ("ENT", 136), ("KEEPN", 128), ("ANY0", 128), ("ANY1", 128), ("KX0", 128), ("KX1", 128),
-        ("KN0", 128), ("KN1", 128), ("IB", 128), ("TMN", 128), ("CM", 128), ("ONES", 128), ("PERM64", 128), ("PERM1", 128), ("OX0", 136),
-        ("OX1", 136), ("INV1", 128), ("OWN", 152), ("R32", 144), ("OTH", 144), ("BKO", 144)] + [("BD%d" % d, 144) for d in range(6)]
-MATF = [("CH", 132), ("SW", 128), ("NSW", 128), ("ISWH", 128), ("INVF", 128)]
-MATH = [("RW", 256), ("KP", 320), ("RP", 512), ("INV0", 128)]
+MATB = [("REP", 512), ("YM", 128), ("ZC", 132), ("ENT", 136), ("KEEPN", 128), ("ANY", 128), ("KX0", 128), ("KX1", 128),
+        ("KN0", 128), ("KN1", 128), ("IB", 128), ("TMN", 128), ("CM", 128), ("CM64", 128), ("C2M", 128), ("ONES", 128),
+        ("OX", 272), ("INV1", 128), ("OWN", 152), ("R32", 144), ("OTH", 144), ("BKO", 144)] + [("BD%d" % d, 144) for d in range(6)]
+MATF = [("CH", 132), ("SW", 128), ("NSW", 128), ("ISM", 128), ("ISM64", 128), ("INVF", 128)]
+MATH = [("RW", 256), ("KP", 320), ("INV0", 128)]
 FLD = [("f31", [[32, 4], [0, 4], [1, 32]], 0), ("f63", [[64, 3], [200, 2], [1, 64]], -216), ("f16", [[0, 3], [1, 8], [0, 16]], 0), ("f8", [[1, 16], [0, 8]], 0), ("f4", [[1, 34], [0, 4]], -5),
-       ("f119", [[16, 8], [0, 2], [1, 8]], -16), ("f111", [[32, 4], [0, 2], [1, 16]], 0)]
+       ("f119", [[16, 8], [0, 2], [1, 8]], -16)]
 DELTA = [1, -1, 2, -2, 3, -3]
 F, B16, H16, I32, U16 = "float32", "bfloat16", "float16", "int32", "uint16"
 SCRATCH = {}
 for _n, _w, _d in (("W", 8256, F), ("OT", 8272, B16), ("MBF", sum(w for n, w in MATB), B16), ("MFF", sum(w for n, w in MATF), F),
-                   ("MHF", sum(w for n, w in MATH), H16), ("CI", 16, I32), ("CF", 64, F), ("XI", 208, B16), ("MF", 512 * len(FLD), B16),
-                   ("MK", 1056, B16), ("RS", 256, B16), ("ST", 256, I32), ("OI", 128, I32), ("FI", 384, I32), ("FB", 384, B16), ("OF", 128, F),
+                   ("MHF", sum(w for n, w in MATH), H16), ("CI", 16, I32), ("CF", 64, F), ("XI", 312, B16), ("MF", 512 * len(FLD), B16),
+                   ("MK", 1056, B16), ("RS", 384, B16), ("ST", 256, I32), ("OI", 128, I32), ("FI", 384, I32), ("FB", 384, B16), ("OF", 128, F),
                    ("OL", 128, U16), ("XL", 64, U16), ("XE0", 1024, F), ("XE1", 1024, F), ("GM", 1024, B16), ("KL", 128, U16), ("KC", 64, F),
                    ("H1", 64, F), ("H2", 64, F), ("U", 1024, F), ("VO", 1024, B16), ("VX", 1024, B16), ("C", 1024, B16), ("R1", 64, F),
                    ("REV", 64, B16), ("FK", 64, F), ("KEEP", 64, B16), ("OK", 64, F), ("CL", 32, U16), ("E", 512, B16),
-                   ("OXA", 128, B16), ("HN", 64, B16), ("U5", 1024, F), ("MX", 1024, F), ("OWNW", 128, F), ("M1", 128, F),
+                   ("OXA", 128, B16), ("HN", 128, B16), ("U5", 1024, F), ("MX", 1024, F), ("OWNW", 128, F), ("M1", 128, F), ("YI", 128, I32),
                    ("HI", 256, H16), ("LO", 256, H16), ("YW0", 128, F), ("YW1", 128, F), ("YH", 64, H16), ("YB", 64, B16),
                    ("YO0", 64, F), ("YO1", 64, F), ("LW0", 2048, H16), ("LW1", 2048, H16), ("LW2", 2048, H16), ("LW3", 2048, H16),
                    ("LOi", 2048, B16), ("LO2", 1024, B16), ("LO3", 1024, B16)):
@@ -150,7 +150,7 @@ def rank_program(g, core, T, topo):
                                  in_=src[32 * P + 16 * h:32 * P + 16 * h + 16, :]).then_inc(T.sem.dST, 16)
     arrive("dST", 16 * 16, ["ST"])
     emit("G", [lambda: g.iota(T.CI[:, 0:1], [[0, 1]], 0, 1)], (), ["ci0"])
-    emit("G", [lambda: g.iota(T.XI[:], [[1, 208]], -48, 0, allow_small_or_imprecise_dtypes=True)], (), ["XI"])
+    emit("G", [lambda: g.iota(T.XI[:], [[1, 312]], -48, 0, allow_small_or_imprecise_dtypes=True)], (), ["XI"])
 
     def X(off, w):
         return T.XI[:, 48 + off:48 + off + w]
@@ -168,7 +168,7 @@ def rank_program(g, core, T, topo):
 
     field(0, 3)
     ints = [("rho", 4, 1), ("h3", 3, 1), ("X0", 0, 103), ("i", 0, 15), ("k63", 0, 63),
-            ("s", 0, 7), ("g16", 0, 112), ("k96", 0, 96), ("blk", 3, 31), ("blk2", 2, 30), ("k111", 0, 111), ("b0", 0, 1), ("b1", 1, 1)]
+            ("s", 0, 7), ("g16", 0, 112), ("k96", 0, 96), ("blk", 3, 31), ("blk2", 2, 30), ("b0", 0, 1), ("b1", 1, 1)]
     names = ["k"] + [x[0] for x in ints]
 
     def colints(lo, hi):
@@ -198,18 +198,16 @@ def rank_program(g, core, T, topo):
         ts(dst, src, col(h), A.is_equal, col(w) if isinstance(w, str) else w, A.mult, [fr, "c_" + h] + (["c_" + w] if isinstance(w, str) else []), [name])
 
     colints(0, 9)
-    lin("n0", "rho", -1, 1.0, "V")
     lin("OXn", "h3", 16, "X0", "V")
-    for n, a, m, add in (("sa", "rho", -32, "k"), ("sg64", "rho", 2.0 / 64, -1.0 / 64), ("t64", "i", 16, 0.0), ("pa", "h3", -16, "X0"),
-                         ("xa", "k96", 4, 0.0), ("PERMh", "rho", 8, "pa"), ("xb", "h3", 64, "xa"), ("sent", "h3", -64, 64.0), ("w64", "h3", -63, 64.0),
-                         ("ta", "rho", -16, "X0"), ("g0", "h3", -1, 1.0), ("ot", "rho", -32, "g16"), ("wz", "s", -65536, 13 * 32768.0),
-                         ("SWh", "sa", 1, 16.0)):
+    lin("OXm", "rho", 136, "OXn", "V")
+    for n, a, m, add in (("sa", "rho", -32, "k"), ("sg64", "rho", 2.0 / 64, -1.0 / 64), ("cb", "i", -16, MAGIC), ("xa", "k96", 4, 0.0),
+                         ("xb", "h3", 64, "xa"), ("sent", "h3", -64, 64.0), ("w64", "h3", -63, 64.0),
+                         ("ta", "rho", -16, "X0"), ("g0", "h3", -1, 1.0), ("ot", "rho", -32, "g16"), ("wz", "s", -65536, 13 * 32768.0)):
         lin(n, a, m, add)
-    mat("OX0", -8, "OXn", "n0")
-    mat("OX1", -8, "OXn", "rho")
     fill(M("ONES"), 1.0, ["ONES"])
-    fill(T.W[:, 4096:4160], -BIG, ["Wz"])
-    mat("RW", "f31", "k63", 1.0)
+    mat("OX", -8, "OXm", 1.0)
+    mat("OWN", -19, "g16", 1.0)
+    mat("SW", -16, "sa", 1.0)
     for j, (sh, m) in enumerate([(6, 1), (7, 127), (0, 63)]):
         ts(T.FI[:, 128 * j:128 * j + 128], T.OI[:], sh, A.logical_shift_right, m, A.bitwise_and, ["OI"], ["FI%d" % j])
     ts(T.FB[:, 0:128], T.FI[:, 0:128], 65.0, A.mult, None, None, ["FI0"], ["FB0"])
@@ -253,9 +251,8 @@ def rank_program(g, core, T, topo):
         toks_all[f] = len(es)
         arrive(n, len(es), [x + "s%d" % j for j in range(4 + j0, 4 + j1)])
 
-    fs = [T.FB[:, 128 * j:128 * j + 128] for j in range(3)]
-    mms([(T.RV[:, 128 * b + 64 * h:128 * b + 64 * h + 64], M("OX%d" % h, 0 if j == 2 else 8), fs[j][:, 64 * b:64 * b + 64], j == 0, j == 2)
-         for b in (0, 1) for h in (0, 1) for j in range(3)], ["FB0", "FB1", "OX0", "OX1"], ["RV.r"], ["RV"])
+    mms([(T.RV[:, 128 * b + 64 * h:128 * b + 64 * h + 64], M("OX", 136 * h + (0 if j == 2 else 8)), T.FB[:, 128 * j + 64 * b:128 * j + 64 * b + 64], j == 0, j == 2)
+         for b in (0, 1) for h in (0, 1) for j in range(3)], ["FB0", "FB1", "OX"], ["RV.r"], ["RV"])
 
     def pack(x, cols):
         for o, i, n in cols:
@@ -264,9 +261,9 @@ def rank_program(g, core, T, topo):
                     [name, "KP"], ["UPa.r", "UPb.r"] if hl == 0 and o == 0 else ["UP.%d.%d" % (hl, o)], ["UPa", "UPb"])
         cp("V", blocks(x, 0, 1), T.UP[:, 384:640], ["UPa.r", "UPb.r", "UP.1.%d" % cols[-1][0]], [x + "s0"], ["UPa", "UPb"])
 
-    OTALL = ["OTz", "OTy"] + ["OT%d%d%s" % (b, r, z) for b in (0, 1) for r in range(8) for z in "ab"]
+    OTALL = ["OTx", "OTz", "OTy"] + ["OT%d%d%s" % (b, r, z) for b in (0, 1) for r in range(8) for z in "ab"]
     WALL = ["Wz"] + ["W%d%d%s" % (b, r, z) for b in (0, 1) for r in range(8) for z in "ab"]
-    rb = [("YY", 0, "YY"), ("DD", 0, "DD"), ("UP", 0, "UPa"), ("UP", 512, "UPb"), ("RV", 0, "RV"), ("NP", 0, "NP")]
+    rb = [("YY", 0, "YY"), ("NP", 0, "NP"), ("DD", 0, "DD"), ("RV", 0, "RV"), ("UP", 0, "UPa"), ("UP", 512, "UPb")]
     nb = [0]
 
     def rep(x, j, b, q):
@@ -281,15 +278,18 @@ def rank_program(g, core, T, topo):
                 s0 = w * j + (128 * b if x == "LOi" else 0)
                 ms = [(o, M("REP", 128 * p), T[x][:, s0:s0 + 128], True, True) for o, p in zip(outs, ps)]
                 mr, tab, reg = ["REP"], T.OT, "OT"
-            elif TWO and x in ("LW2", "LW3"):
-                ms = [(o, M("RP", 128 * p), T[x][:, w * j + 128 * hl:w * j + 128 * hl + 128], hl == 0, hl == 1) for o, p in zip(outs, ps) for hl in (0, 1)]
-                mr, tab, reg = ["RP"], T.W, "W"
             else:
                 ms = [(o, M("RW", 128 * (p & 1)), T[x][:, w * j + 128 * (p >> 1):w * j + 128 * (p >> 1) + 128], True, True) for o, p in zip(outs, ps)]
                 mr, tab, reg = ["RW"], T.W, "W"
             mms(ms, [x + "s%d" % j] + mr, [bank + ".r"], [bank])
-            cp(qi, tab[:, d0 + 128 * n * i:d0 + 128 * n * (i + 1)], T[buf][:, c0:c0 + 128 * n], [bank + ".r"],
-               ["%s%d%d%s" % (reg, b, at[j], z) for z in ("ab" if n == 4 else "ab"[i])], [bank])
+            o, src = tab[:, d0 + 128 * n * i:d0 + 128 * n * (i + 1)], T[buf][:, c0:c0 + 128 * n]
+            W = ["%s%d%d%s" % (reg, b, at[j], z) for z in ("ab" if n == 4 else "ab"[i])]
+            if reg == "OT":
+                cp(qi, o, src, [bank + ".r"], W, [bank])
+            elif qi == "V":
+                ts(o, src, col("cb"), A.add, None, None, [bank + ".r", "c_cb"], W, [bank])
+            else:
+                act(o, src, 1.0, col("cb"), [bank + ".r", "c_cb"], W, [bank])
 
     def order(x):
         return [[0, 4, 1, 2, 3, 5, 6, 7], [0, 4, 1, 2, 3, 7, 5, 6], [0, 4, 1, 2, 6, 3, 5, 7], [0, 4, 1, 5, 2, 6, 3, 7]][EX[x][1]]
@@ -300,89 +300,86 @@ def rank_program(g, core, T, topo):
              ["W%d%da" % (b, rank), "W%d%db" % (b, rank), "XL"], ["XE%d" % b])
 
     mat("KP", "f63", "sa", -1.0)
-    ts(T.HI[:], T.ST[:], col("sg64"), A.mult, col("t64"), A.add, ["ST", "c_sg64", "c_t64"], ["HI"])
+    ts(T.HI[:], T.ST[:], col("sg64"), A.mult, None, None, ["ST", "c_sg64"], ["HI"])
     cp("S", blocks("LOi", 0, 1), T.RV[:, 0:256], ["RV.r"], ["LOis0"], ["RV"])
     send("LOi")
-    ts(T.K0[:, 256:512], T.ST[:], col("sg64"), A.mult, col("t64"), A.add, ["ST", "c_sg64", "c_t64"], ["K0.y"], ["K0"])
+    ts(T.K0[:, 256:512], T.ST[:], col("sg64"), A.mult, None, None, ["ST", "c_sg64"], ["K0.y"], ["K0"])
     tt(T.LO[:], T.K0[:, 256:512], T.HI[:], A.subtract, ["K0.y", "HI"], ["LO"], ["K0"])
+    for c0, reg in ((4096, "OTz"), (8256, "OTy")):
+        act(T.OT[:, c0:c0 + 16], M("ONES", 0, 16), col("sent"), 0.0, ["ONES", "c_sent"], [reg])
+    sc(M("R32"), M("OWN", 4, 144), 32.0, ["OWN"], ["R32"])
+    act(M("BKO"), M("OWN", 4, 144), col("w64"), 0.0, ["OWN", "c_w64"], ["BKO"])
+    sc(M("NSW"), M("SW"), -1.0, ["SW"], ["NSW"])
+    sc(M("ISM"), M("SW"), -0.5, ["SW"], ["ISM"])
+    mat("RW", "f31", "k63", 1.0)
     mat("REP", "f31", "k", 1.0)
-    mat("PERM64", -16, "PERMh", 64.0)
-    mat("PERM1", -16, "PERMh", 1.0)
+    ts(T.XL[:], X(0, 64), col("xb"), A.add, None, None, ["XI", "c_xb"], ["XL"])
+    mat("ENT", -24, "ta", "w64")
     pack("LW0", [(64 * h, 128 * h, 64) for h in (0, 1)])
     send("LW0")
     rep("LW0", 0, 0, "S")
-    ts(T.XL[:], X(0, 64), col("xb"), A.add, None, None, ["XI", "c_xb"], ["XL"])
+    expand(0)
     colints(9, len(ints))
     pack("LW1", [(64 * h, 128 * h + 64, 64) for h in (0, 1)])
-    lin("bl", "rho", -8, "blk2", "V")
     send("LW1")
     field(3, len(FLD))
     forward("LOi", 1, 2)
     forward("LOi", 2, 4)
     forward("LW0")
     forward("LW1")
-    expand(0)
-    mms([(T.K1[:, 0:128], M("PERM1" if j == 2 else "PERM64"), fs[j], j == 0, j == 2) for j in range(3)], ["FB0", "FB1", "PERM64", "PERM1"], ["K1.o"], ["K1"])
-    rep("LW1", 0, 1, "S")
+    mms([(T.K0[:, 64 * b:64 * b + 64], M("ENT", 8 - 8 * h), T.LOi[:, 128 * b + 64 * h:128 * b + 64 * h + 64], h == 0, h == 1) for b in (0, 1) for h in (0, 1)],
+        ["LOis0", "ENT"], ["K0.o"], ["K0"])
     for b in (0, 1):
         rep("LOi", 0, b, "S")
-    ts(T.OT[:, 4096:4112], M("ONES", 0, 16), col("sent"), A.mult, None, None, ["ONES", "c_sent"], ["OTz"])
-    ts(T.OT[:, 8256:8272], M("ONES", 0, 16), col("sent"), A.mult, None, None, ["ONES", "c_sent"], ["OTy"])
-    fill(T.OT[:, 4112:4160], 0.0, ["OTx"])
-    OTALL.append("OTx")
-    fill(T.RS[:], 0.0, ["RS"])
-    cp("V", T.OF[:], T.K1[:, 0:128], ["K1.o"], ["OF0", "OF1"], ["K1"])
-    mat("BKO", -15, "g16", "w64")
-    fill(T.RS[:, 0::8], -BIG, ["RS"])
-    cp("V", T.OL[:], T.OF[:], ["OF0", "OF1"], ["OL0", "OL1"])
-    ts(T.MK[:, 0:288], fld("f16", 288), col("s"), A.is_equal, None, None, ["f16", "c_s"], ["MK0"])
-    mat("OWN", -19, "g16", 1.0)
-    mat("R32", -15, "g16", 32.0)
-    cp("V", T.MK[:, 288:544], T.MK[:, 32:288], ["MK0"], ["MK1"])
-    mat("OTH", -31, "ot", 1.0)
-    mat("SW", -16, "sa", 1.0)
-    cp("V", T.MK[:, 544:1056], T.MK[:, 32:544], ["MK0", "MK1"], ["MK2"])
-    mat("YM", "f8", "blk", -65536.0)
-    emit("G", [lambda: g.affine_select(M("YM"), M("YM"), [[1, 128]], A.is_gt, 0.0, 0, -1)], ["YM"], ["YM"])
-    emit("G", [lambda: g.affine_select(M("YM"), M("YM"), [[1, 128]], A.not_equal, 32768.0, 0, -1)], ["YM"], ["YM"])
 
     def partners(js):
         for j in js:
             tt(M("BD%d" % j), M("R32"), M("OWN", 4 - DELTA[j], 144), A.subtract, ["R32", "OWN"], ["BD%d" % j])
 
+    lin("bl", "rho", -8, "blk2", "V")
+    cp("V", T.OF[:], T.K0[:, 0:128], ["K0.o"], ["OF0", "OF1"], ["K0"])
+    rep("LW1", 0, 1, "V")
+    ts(T.MK[:, 0:288], fld("f16", 288), col("s"), A.is_equal, None, None, ["f16", "c_s"], ["MK0"])
+    cp("V", T.OL[:], T.K0[:, 0:128], ["K0.o"], ["OL0", "OL1"], ["K0"])
+    cp("V", T.MK[:, 288:544], T.MK[:, 32:288], ["MK0"], ["MK1"])
+    mat("OTH", -31, "ot", 1.0)
+    cp("V", T.MK[:, 544:1056], T.MK[:, 32:544], ["MK0", "MK1"], ["MK2"])
+    ts(M("ANY"), fld("f16"), 16.0, A.mult, col("g16"), A.is_equal, ["f16", "c_g16"], ["ANY"])
     partners((0, 1))
+    mat("YM", "f8", "blk", -65536.0)
     mat("CH", "f4", "bl", 1.0)
-    mat("ZC", "f4", "bl", "wz")
-    mat("ENT", -24, "ta", "w64")
-    ts(M("ANY0"), fld("f16"), 16.0, A.mult, col("g16"), A.is_equal, ["f16", "c_g16"], ["ANY0"])
     for h, gn in ((0, "g0"), (1, "h3")):
         mat("KX%d" % h, "f119", "ta", gn)
-    mat("ISWH", "f111", "k111", 0.5)
-    mat("IB", 0, "k", 1.0)
-    if TWO:
-        mat("RP", "f31", "SWh", -1.0)
+    emit("G", [lambda: g.iota(T.OT[:, 4112:4160], [[0, 48]], 0, 0, allow_small_or_imprecise_dtypes=True)], (), ["OTx"])
+    emit("G", [lambda: g.iota(T.W[:, 4096:4160], [[0, 64]], -int(BIG), 0, allow_small_or_imprecise_dtypes=True)], (), ["Wz"])
+    emit("G", [lambda: g.affine_select(M("IB"), M("ONES"), [[1, 128]], A.is_equal, 0.0, 0, -1)], ["ONES"], ["IB"])
+    emit("G", [lambda: g.affine_select(M("YM"), M("YM"), [[1, 128]], A.is_gt, 0.0, 0, -1)], ["YM"], ["YM"])
+    emit("G", [lambda: g.iota(T.RS[:], [[0, 384]], 0, 0, allow_small_or_imprecise_dtypes=True)], (), ["RS"])
+    emit("G", [lambda: g.affine_select(M("YM"), M("YM"), [[1, 128]], A.not_equal, 32768.0, 0, -1)], ["YM"], ["YM"])
+    emit("G", [lambda: g.affine_select(T.RS[:], T.RS[:], [[0, 48], [1, 8]], A.not_equal, -BIG, 0, 0)], ["RS"], ["RS"])
+    emit("G", [lambda: g.affine_select(M("ISM"), M("ISM"), [[1, 128]], A.not_equal, 0.5, 0, -1)], ["ISM"], ["ISM"])
 
     def late2():
+        act(M("ZC"), M("CH"), col("wz"), 0.0, ["CH", "c_wz"], ["ZC"])
         sc(M("KEEPN"), M("IB"), -16384.0, ["IB"], ["KEEPN"])
         for h in (0, 1):
             sc(M("KN%d" % h), M("KX%d" % h), -256.0, ["KX%d" % h], ["KN%d" % h])
-        sc(M("NSW"), M("SW"), -1.0, ["SW"], ["NSW"])
         lin("nt64", "i", -16, 0.0)
-        lin("a0", "h3", BIG, -BIG)
-        lin("a1", "h3", -BIG, 0.0)
-        lin("c8", "rho", 2.0 / 256, -1.0 / 256)
+        lin("eg0", "h3", EMPTY, -EMPTY)
+        lin("c8", "rho", -2.0 / 256, 1.0 / 256)
         act(M("TMN"), M("IB"), col("nt64"), 0.0, ["IB", "c_nt64"], ["TMN"])
-        act(M("ANY1"), M("ANY0"), col("a1"), 0.0, ["ANY0", "c_a1"], ["ANY1"])
-        act(M("ANY0"), M("ANY0"), col("a0"), 0.0, ["ANY0", "c_a0"], ["ANY0"])
-        act(M("CM"), M("IB"), col("c8"), 0.0, ["IB", "c_c8"], ["CM"])
-        lin("tm", "i", 16, MAGIC)
 
     def late3():
-        lin("iv", "rho", -8, "OXn", "V")
-        lin("s64", "rho", 128, -64.0, "V")
-        mat("INVF", -8, "iv", 1.0)
-        mat("INV0", -8, "iv", 64.0)
-        sc(M("INV1"), M("INVF"), -4128.0, ["INVF"], ["INV1"])
+        sc(M("C2M"), M("IB"), 2 * MAGIC, ["IB"], ["C2M"])
+        sc(M("ANY"), M("ANY"), -BIG, ["ANY"], ["ANY"])
+        act(M("CM"), M("IB"), col("c8"), 0.0, ["IB", "c_c8"], ["CM"])
+
+    def late4():
+        sc(M("ISM64"), M("ISM"), 64.0, ["ISM"], ["ISM64"])
+        sc(M("CM64"), M("CM"), 64.0, ["CM"], ["CM64"])
+        lin("sgn", "rho", 2, -1.0)
+        lin("s64", "rho", 128, -64.0)
+        lin("sm", "rho", -128 * MAGIC, 64 * MAGIC)
 
     def lists_gather(t):
         b = t & 1
@@ -391,13 +388,14 @@ def rank_program(g, core, T, topo):
     def lists(t):
         b = t & 1
         mms([(T.K0[:, 0:64], SL("BKO", q), T.GM[:, q::16], q == 0, q == 15) for q in range(16)], ["GM", "BKO"], ["K0.k"], ["K0"])
-        thr = "b0" if t == 0 else "b1"
-        ts(T.H1[:], T.OF[:, 64 * b:64 * b + 64], EMPTY, A.is_equal, col(thr), A.add, ["OF%d" % b, "c_" + thr], ["H1"])
         ts(T.KC[:], T.K0[:, 0:64], 32768.0 - 8256.0, A.add, None, None, ["K0.k"], ["KC"], ["K0"])
         cp("V", T.KL[:, 0:64], T.K0[:, 0:64], ["K0.k"], ["KL0"], ["K0"])
 
-    def swapped():
+    def swapped(t):
         mms([(T.K1[:, 0:64], M("SW"), T.KC[:], True, True)], ["KC", "SW"], ["K1.k"], ["K1"])
+        b = t & 1
+        thr = "b0" if t == 0 else "b1"
+        ts(T.H1[:], T.OF[:, 64 * b:64 * b + 64], EMPTY, A.is_equal, col(thr), A.add, ["OF%d" % b, "c_" + thr], ["H1"])
         ts(T.KL[:, 64:128], T.K1[:, 0:64], 8256.0 - 32768.0, A.add, None, None, ["K1.k"], ["KL1"], ["K1"])
 
     def natural(b):
@@ -420,7 +418,13 @@ def rank_program(g, core, T, topo):
         if t == 0:
             late2()
         if t == 1:
-            expand(0)
+            lin("iv", "rho", -8, "OXn")
+        if nx:
+            expand(1 - b)
+        if t == 1:
+            late4()
+        if t == 2:
+            outputs(1)
         XE = T["XE%d" % b]
         tt(T.VO[:], Wt.indirect(T.KL[:, 0:64]), XE[:], A.is_gt, WALL + ["KL0"] + xe, ["VO"])
         mms([(T.RV[:, 0:64], SL("OWN", q), T.VO[:, q::16], q == 0, False) for q in range(16)], ["VO", "OWN"], ["RV.v"], ["RV"])
@@ -438,8 +442,15 @@ def rank_program(g, core, T, topo):
                 nq += len(qs)
         dd = ["DD.d%d" % y for u, v, s in st for y in (u, v)]
         ts(T.R1[:], T.RV[:, 0:64], 1024.0, A.mult, col(thr), A.add, ["RV.v", "RV.v2", "c_" + thr], ["R1"], ["RV"])
+        if t == 2:
+            natural(1)
+        if t == 1:
+            mat("INVF", -8, "iv", 1.0)
+            sc(M("INV1"), M("INVF"), -4128.0, ["INVF"], ["INV1"])
         tt(T.REV[:], T.DD[:, 0:64], T.R1[:], A.is_ge, dd + ["R1"], ["REV"], ["DD"])
         mms([(T.YY[:, 0:64], M("YM"), T.REV[:], True, True)], ["REV", "YM"], ["YY.y"], ["YY"])
+        if t == 1:
+            mat("INV0", -8, "iv", 64.0)
         mms([(T.K1[:, 64:96], M("ZC", 4 - 4 * e), T.REV[:, 32 * e:32 * e + 32], e == 0, False) for e in (0, 1)], ["REV", "ZC"], ["K1.z"], ["K1"])
         tt(T.FK[:], T.YY[:, 0:64], T.KC[:], A.min, ["YY.y", "KC"], ["FK"], ["YY"])
         mms([(T.K1[:, 64:96], M("CH", 4 - 4 * e), T.FK[:, 32 * e:32 * e + 32], False, e == 1) for e in (0, 1)], ["FK", "CH"], ["K1.c"], ["K1"])
@@ -451,6 +462,8 @@ def rank_program(g, core, T, topo):
             mms([(T.RV[:, 64 * h + 128:64 * h + 192], M("KX%d" % h), T.KEEP[:], True, True) for h in (0, 1)], ["KEEP", "KX0", "KX1"], ["RV.k"], ["RV"])
         emit("V", [lambda: g.vector.tensor_copy(out=T.E[:, 0:256], in_=T.OT[:].indirect(T.CL[:, 0:16]))], OTALL + ["CL"], ["E0"])
         emit("S", [lambda: g.scalar.activation(out=T.E[:, 256:512], in_=T.OT[:].indirect(T.CL[:, 16:32]), func=AF.Copy)], OTALL + ["CL"], ["E1"])
+        if t == 0:
+            late3()
         mms([(T.NP[:, 32 * e:32 * e + 32], M("ENT", 8 - 8 * h), T.E[:, 8 * h + 4 * e::16], False, h == 1 and e == 1) for e in (0, 1) for h in (0, 1)],
             ["E0", "E1", "ENT"], ["NP.n2"], ["NP"])
         tt(T.OK[:], T.OF[:, 64 * b:64 * b + 64], T.KEEP[:], A.mult, ["OF%d" % b, "KEEP"], ["OK"])
@@ -464,56 +477,58 @@ def rank_program(g, core, T, topo):
         n = T.OF[:, 64 * b:64 * b + 64]
         tt(n, T.NP[:, 0:64], T.OK[:], A.max, ["NP.n", "NP.n2", "OK"], ["OF%d" % b], ["NP"])
         cp("V", ol, n, ["OF%d" % b], ["OL%d" % b])
-        for h, bank in ((0, "K0"), (1, "K1")):
-            mms([(T[bank][:, 0:64], M("NSW"), XE[:, 8 * h::16], True, False),
-                 (T[bank][:, 0:64], M("TMN"), M("ONES", 0, 64), False, False)], xe + ["NSW", "TMN", "ONES"], [bank + ".a"], [bank])
-        for h in (1, 2, 3):
-            emit("S", [lambda: g.scalar.activation(out=T.U5[:, 256 * h:256 * h + 256], in_=Wt.indirect(T.OL[:, 64 * b + 16 * h:64 * b + 16 * h + 16]),
-                                                   func=AF.Copy)], WALL + ["OL%d" % b], ["U5%d" % h])
         if nx:
             tt(blocks("LO" + nx, 0, 1), T.DD[:, 128:256], T.OXA[:], A.max, ["DD.x0", "DD.x1", "OXA"], ["LO%ss0" % nx], ["DD"])
             send("LO" + nx)
-        emit("V", [lambda: g.vector.tensor_copy(out=T.U5[:, 0:256], in_=Wt.indirect(T.OL[:, 64 * b:64 * b + 16]))], WALL + ["OL%d" % b], ["U50"])
-        ts(T.HN[:], n, EMPTY, A.not_equal, None, None, ["OF%d" % b], ["HN"])
-        for h, bank in ((0, "K0"), (1, "K1")):
-            mms([(T[bank][:, 0:64], M("ANY%d" % h), T.HN[:], False, True)], ["HN", "ANY%d" % h], [bank + ".b"], [bank])
-        mms([(T.RV[:, 256:384], M("CM"), M("ONES"), True, False)], ["CM", "ONES"], ["RV.t"], ["RV"])
+        mms([(T.K0[:, 0:128], M("NSW"), XE[:, 0::8], True, False), (T.K0[:, 0:128], M("TMN"), M("ONES"), False, False),
+             (T.K0[:, 0:128], M("C2M"), M("ONES"), False, False)], xe + ["NSW", "TMN", "C2M", "ONES"], ["K0.a"], ["K0"])
+        cut = CUT[0 if nx else 1]
+        emit("S", [lambda: g.scalar.activation(out=T.HN[:, 0::2], in_=n, func=AF.Abs, bias=col("eg0"), scale=col("g0"))], ["OF%d" % b, "c_g0", "c_eg0"], ["HN1"])
+        for h in (1, 2, 3):
+            emit("S", [lambda: g.scalar.activation(out=T.U5[:, 16 * cut[h]:16 * cut[h + 1]], in_=Wt.indirect(T.OL[:, 64 * b + cut[h]:64 * b + cut[h + 1]]),
+                                                   func=AF.Copy)], WALL + ["OL%d" % b], ["U5%d" % h])
+        emit("V", [lambda: g.vector.tensor_copy(out=T.U5[:, 0:16 * cut[1]], in_=Wt.indirect(T.OL[:, 64 * b:64 * b + cut[1]]))], WALL + ["OL%d" % b], ["U50"])
+        ts(T.HN[:, 1::2], n, EMPTY, A.not_equal, col("h3"), A.mult, ["OF%d" % b, "c_h3"], ["HN2"])
+        mms([(T.K0[:, 0:128], M("ANY"), T.HN[:], False, True)], ["HN1", "HN2", "ANY"], ["K0.b"], ["K0"])
+        mms([(T.RV[:, 256:384], M("CM" if nx else "CM64"), M("ONES"), True, False)], ["CM", "CM64", "ONES"], ["RV.t"], ["RV"])
         for h in range(4):
-            emit("V", [lambda: g.vector.tensor_tensor_scan(out=T.MX[:, 256 * h:256 * h + 256], data0=T.RS[:], data1=T.U5[:, 256 * h:256 * h + 256],
-                                                           initial=-2.0 * BIG, op0=A.add, op1=A.max)], ["RS", "U5%d" % h], ["MX%d" % h])
-        for h, bank in ((0, "K0"), (1, "K1")):
-            tt(T.OWNW[:, 64 * h:64 * h + 64], T.MX[:, 7 + 8 * h::16], T[bank][:, 0:64], A.max, ["MX0", "MX1", "MX2", "MX3", bank + ".a", bank + ".b"],
-               ["OWN%d" % h], [bank])
-        mms([(T.RV[:, 256:384], M("ISWH"), T.OWNW[:], False, True)], ["OWN0", "OWN1", "ISWH"], ["RV.s"], ["RV"])
-        act(T.NP[:, 256:384], T.OWNW[:], 1.0, col("tm"), ["OWN0", "OWN1", "c_tm"], ["NP.t"], ["NP"])
-        if t == 0:
-            expand(1)
-        if not nx:
-            natural(b)
-        ts(T.M1[:], T.RV[:, 256:384], 0.0, A.min, MAGIC, A.add, ["RV.s", "RV.t"], ["M1"], ["RV"])
-        Y = T.K0[:, 256:384]
+            emit("V", [lambda: g.vector.tensor_tensor_scan(out=T.MX[:, 16 * cut[h]:16 * cut[h + 1]], data0=T.RS[:, 0:16 * (cut[h + 1] - cut[h])],
+                                                           data1=T.U5[:, 16 * cut[h]:16 * cut[h + 1]], initial=-2.0 * BIG, op0=A.add, op1=A.max)], ["RS", "U5%d" % h], ["MX%d" % h])
+        tt(T.OWNW[:], T.MX[:, 7::8], T.K0[:, 0:128], A.max, ["MX0", "MX1", "MX2", "MX3", "K0.a", "K0.b"], ["OW"], ["K0"])
+        ism, k = ("ISM", 1.0) if nx else ("ISM64", 64.0)
+        mms([(T.RV[:, 256 + 64 * h:320 + 64 * h], M(ism), T.OWNW[:, h::2], False, h == 1) for h in (0, 1)], ["OW", ism], ["RV.s"], ["RV"])
+        for h in (0, 1):
+            act(T.M1[:, 64 * h:64 * h + 64], T.OWNW[:, h::2], k, -k * MAGIC, ["OW"], ["M1%d" % h])
         if nx:
-            hi, lo = (T["LW" + nx][:, 0:128], T["LW" + nx][:, 128:256]) if TWO else (T.HI[:, 0:128], T.LO[:, 0:128])
-            tt(hi, T.NP[:, 256:384], T.M1[:], A.subtract, ["M1", "NP.t"], ["HI"], ["NP"])
-        tt(Y, T.NP[:, 256:384], T.M1[:], A.subtract, ["M1", "NP.t"], ["K0.y"], ["NP", "K0"])
-        if nx:
-            tt(lo, Y, hi, A.subtract, ["K0.y", "HI"], ["LW%ss0" % nx if TWO else "LO"], ["K0"])
-            if not TWO:
-                pack("LW" + nx, [(0, 0, 128)])
+            nb[0] = 0
+            rep("LO" + nx, 0, b, "S")
+            partners((2 * t + 2,))
+            Y = T.K1[:, 256:384]
+            tt(T.HI[:, 0:128], T.RV[:, 256:384], T.M1[:], A.max, ["RV.s", "RV.t", "M10", "M11"], ["HI"], ["RV"])
+            tt(Y, T.RV[:, 256:384], T.M1[:], A.max, ["RV.s", "RV.t", "M10", "M11"], ["K1.y"], ["RV", "K1"])
+            tt(T.LO[:, 0:128], Y, T.HI[:, 0:128], A.subtract, ["K1.y", "HI"], ["LO"], ["K1"])
+            partners((2 * t + 3,))
+            pack("LW" + nx, [(0, 0, 128)])
             send("LW" + nx)
             forward("LO" + nx)
             forward("LW" + nx)
-        if t > 0:
-            ts(T["YW%d" % b][:], Y, col("t64"), A.subtract, col("s64"), A.mult, ["K0.y", "c_t64", "c_s64"], ["YW%d" % b], ["K0"])
-            for q, y, r0 in (("Y", T.yl, 16), ("Y" if nx else "S", T.yr, 0)):
-                pre(q, ["YW%d" % b], [])
-                for P in range(4):
-                    for h in (0, 1):
-                        eng[q].dma_start(out=y[32 * P + 16 * h:32 * P + 16 * h + 16, 64 * b:64 * b + 64],
-                                         in_=T["YW%d" % b][32 * P + r0:32 * P + r0 + 16, 64 * h:64 * h + 64]).then_inc(T.sem["dY%d" % b], 16)
-            toks_all["dY%d" % b] = 16 * 16
-            if nx:
-                natural(b)
+        else:
+            natural(b)
+            tt(T.YI[:], T.RV[:, 256:384], T.M1[:], A.max, ["RV.s", "RV.t", "M10", "M11"], ["YI"], ["RV"])
+            ts(T.YW0[:], T.YI[:], col("sgn"), A.mult, None, None, ["YI", "c_sgn"], ["YW0"])
+            outputs(0)
+
+    def outputs(b):
+        if b == 1:
+            act(T.M1[:], T.K1[:, 256:384], 1.0, MAGIC, ["K1.y"], ["M10", "M11"], ["K1"])
+            act(T.YW1[:], T.M1[:], col("s64"), col("sm"), ["M10", "M11", "c_s64", "c_sm"], ["YW1"])
+        for q, y, r0 in (("Y", T.yl, 16), ("Y" if b else "S", T.yr, 0)):
+            pre(q, ["YW%d" % b], [])
+            for P in range(4):
+                for h in (0, 1):
+                    eng[q].dma_start(out=y[32 * P + 16 * h:32 * P + 16 * h + 16, 64 * b:64 * b + 64],
+                                     in_=T["YW%d" % b][32 * P + r0:32 * P + r0 + 16, 64 * h:64 * h + 64]).then_inc(T.sem["dY%d" % b], 16)
+        toks_all["dY%d" % b] = 16 * 16
 
     for j in (4, 1, 2, 3):
         rep("LOi", j, 0, "V")
@@ -527,32 +542,27 @@ def rank_program(g, core, T, topo):
         if j == 5:
             rep("LW1", ow[1], 1, "S")
             rep("LW1", ow[2], 1, "V")
-            rep("LW1", ow[3], 1, "VS")
     lists_gather(0)
-    for j in ow[4:6]:
+    for j in ow[3:7]:
         rep("LW1", j, 1, "S")
     for j in (5, 6, 7):
-        rep("LW0", j, 0, "SVS"[j - 5])
+        rep("LW0", j, 0, "VSV"[j - 5])
     rep("LW1", ow[7], 1, "S")
     lists(0)
-    rep("LW1", ow[6], 1, "SV")
-    swapped()
+    swapped(0)
     round_(0)
     for t, x, b in ((1, "2", 0), (2, "3", 1)):
         oo, ow = order("LO" + x), order("LW" + x)
-        for i, j in enumerate(oo):
-            rep("LO" + x, j, b, "VS"[i & 1])
-        if t == 1:
-            late3()
+        for i, j in enumerate(oo[1:]):
+            rep("LO" + x, j, b, "SV"[i & 1])
         lists_gather(t)
-        partners((2 * t, 2 * t + 1))
-        for j in ow[:3]:
-            rep("LW" + x, j, b, "S")
+        for i, j in enumerate(ow[:5]):
+            rep("LW" + x, j, b, "SSSVS"[i])
         lists(t)
-        rep("LW" + x, ow[3], b, "S")
-        swapped()
-        for j in ow[4:]:
-            rep("LW" + x, j, b, "VS")
+        rep("LW" + x, ow[5], b, "S")
+        rep("LW" + x, ow[6], b, "V")
+        swapped(t)
+        rep("LW" + x, ow[7], b, "SV")
         round_(t)
     for s in SEMAPHORES:
         if toks_all.get(s, 0) > known["G"].get(s, 0):

@@ -1,19 +1,19 @@
 from concourse.bass import DstId, RemoteDMATransfer
 from concourse.mybir import AluOpType as A, ActivationFunctionType as AF
 
-EX = {"LOi": (256, 0, ()), "LW0": (256, 0, ("LOi", "LW0")), "LW1": (256, 2, ("LW1",)), "LO2": (128, 3, ("LO2",)),
-      "LW2": (256, 2, ("LW2",)), "LO3": (128, 3, ("LO3",)), "LW3": (256, 2, ("LW3",))}
-CUT = [(0, 12, 32, 52, 64), (0, 16, 36, 52, 64)]
+EX = {"LOi": (256, 0, False), "LWi": (512, 1, True), "LO2": (128, 3, True), "LW2": (256, 2, True), "LO3": (128, 3, True), "LW3": (256, 2, True)}
+CUT = [(0, 12, 32, 52, 64), (0, 12, 32, 52, 64)]
 BIG = 2.0 ** 23
 MAGIC = 1.5 * 2.0 ** 17
 EMPTY = 4096.0
-KOFF = 8192.0 * 3
+LOW = 2.0 ** 17
 MATB = [("REP", 512), ("YM", 128), ("ZC", 132), ("ENT", 136), ("KEEPN", 128), ("ANY", 128), ("KX0", 128), ("KX1", 128),
         ("KN0", 128), ("KN1", 128), ("IB", 128), ("TMN", 128), ("CM", 128), ("CM64", 128), ("C2M", 128), ("ONES", 128),
-        ("OX", 272), ("INV1", 128), ("OWN", 152), ("R32", 144), ("OTH", 144), ("BKO", 144)] + [("BD%d" % d, 144) for d in range(6)]
-MATF = [("CH", 132), ("SW", 128), ("NSW", 128), ("ISM", 128), ("ISM64", 128), ("INVF", 128)]
-MATH = [("RW", 256), ("KP", 320), ("INV0", 128)]
-FLD = [("f31", [[32, 4], [0, 4], [1, 32]], 0), ("f63", [[64, 3], [200, 2], [1, 64]], -216), ("f16", [[0, 3], [1, 8], [0, 16]], 0), ("f8", [[1, 16], [0, 8]], 0), ("f4", [[1, 34], [0, 4]], -5),
+        ("OX", 272), ("INV1", 128), ("OWN", 152), ("NOWN", 152), ("R32", 144), ("OTH", 144), ("BKO", 144), ("BKX", 144),
+        ("TMP", 136)] + [("BD%d" % d, 144) for d in range(6)]
+MATF = [("CH", 132), ("SW", 128), ("NSW", 128), ("ISM", 128), ("INVF", 128)]
+MATH = [("RW", 256), ("INV0", 128)]
+FLD = [("f31", [[32, 4], [0, 4], [1, 32]], 0), ("f16", [[0, 3], [1, 8], [0, 16]], 0), ("f4", [[1, 34], [0, 4]], -5),
        ("f119", [[16, 8], [0, 2], [1, 8]], -16)]
 DELTA = [1, -1, 2, -2, 3, -3]
 F, B16, H16, I32, U16 = "float32", "bfloat16", "float16", "int32", "uint16"
@@ -24,15 +24,15 @@ for _n, _w, _d in (("W", 8256, F), ("OT", 8272, B16), ("MBF", sum(w for n, w in 
                    ("OL", 128, U16), ("XL", 64, U16), ("XE0", 1024, F), ("XE1", 1024, F), ("GM", 1024, B16), ("KL", 128, U16), ("KC", 64, F),
                    ("H1", 64, F), ("H2", 64, F), ("U", 1024, F), ("VO", 1024, B16), ("VX", 1024, B16), ("C", 1024, B16), ("R1", 64, F),
                    ("REV", 64, B16), ("FK", 64, F), ("KEEP", 64, B16), ("OK", 64, F), ("CL", 32, U16), ("E", 512, B16),
-                   ("OXA", 128, B16), ("HN", 128, B16), ("U5", 1024, F), ("MX", 1024, F), ("OWNW", 128, F), ("M1", 128, F), ("YI", 128, I32),
-                   ("HI", 256, H16), ("LO", 256, H16), ("YW0", 128, F), ("YW1", 128, F), ("YH", 64, H16), ("YB", 64, B16),
-                   ("YO0", 64, F), ("YO1", 64, F), ("LW0", 2048, H16), ("LW1", 2048, H16), ("LW2", 2048, H16), ("LW3", 2048, H16),
+                   ("OXA", 128, B16), ("HN", 128, B16), ("U5", 1024, F), ("MX", 1024, F), ("D", 128, F), ("M1", 128, F), ("YI", 128, I32),
+                   ("XS", 8, U16), ("XW", 128, F), ("YW0", 128, F), ("YW1", 128, F), ("YH", 64, H16), ("YB", 64, B16),
+                   ("YO0", 64, F), ("YO1", 64, F), ("LWi", 4096, H16), ("LW2", 2048, H16), ("LW3", 2048, H16),
                    ("LOi", 2048, B16), ("LO2", 1024, B16), ("LO3", 1024, B16)):
     SCRATCH[_n] = ("sbuf", [128, _w], _d)
-for _n in ("K0", "K1", "RV", "DD", "YY", "NP", "UP"):
-    SCRATCH[_n] = ("psum", [128, 1024 if _n == "UP" else 512], F)
+for _n in ("K0", "K1", "RV", "DD", "YY", "NP", "UA", "UB"):
+    SCRATCH[_n] = ("psum", [128, 512], F)
 SEMAPHORES = (["sV", "sS", "sP", "sG", "dOI", "dST"]
-              + [k + x for x in EX for k in ["r%d" % r for r in range(8)] + ["n1", "n2", "l", "f1", "f2"]]
+              + [k + x for x in EX for k in ["r%d" % r for r in range(8)] + ["n1", "n2", "l", "m", "f1", "f2"]]
               + ["dY0", "dY1", "dO0", "dO1"])
 
 
@@ -113,17 +113,22 @@ def rank_program(g, core, T, topo):
     def cp(q, out, i, R=(), W=(), B=()):
         if q == "V":
             emit("V", [lambda: g.vector.tensor_copy(out=out, in_=i)], R, W, B)
-        else:
+        elif q == "S":
             emit("S", [lambda: g.scalar.activation(out=out, in_=i, func=AF.Copy)], R, W, B)
+        else:
+            emit("G", [lambda: g.affine_select(out, i, [[0, out.shape[1]]], A.is_ge, 0.0, 0, 0)], R, W)
 
     def fill(out, c, W):
         emit("V", [lambda: g.vector.memset(out, c)], (), W)
 
-    def act(out, i, scale, bias, R=(), W=(), B=()):
-        emit("S", [lambda: g.scalar.activation(out=out, in_=i, func=AF.Identity, bias=bias, scale=scale)], R, W, B)
+    def act(out, i, scale, bias, R=(), W=(), B=(), func=AF.Identity):
+        emit("S", [lambda: g.scalar.activation(out=out, in_=i, func=func, bias=bias, scale=scale)], R, W, B)
 
     def sc(dst, src, scale, R, W):
         emit("S", [lambda: g.scalar.activation(out=dst, in_=src, func=AF.Copy, scale=float(scale))], R, W)
+
+    def sel(name, src, pat, op, c, base, cm):
+        emit("G", [lambda: g.affine_select(M(name), M(src), pat, op, c, base, cm)], [src], [name])
 
     def mms(groups, R=(), W=(), B=()):
         emit("P", [(lambda m=m: g.tensor.matmul(out=m[0], lhsT=m[1], rhs=m[2], start=m[3], stop=m[4])) for m in groups], R, W, B)
@@ -135,6 +140,10 @@ def rank_program(g, core, T, topo):
                 if name == n:
                     return buf[:, j:j + width] if a is None else buf[:, j + a:j + a + w]
                 j += width
+
+    def MS(n, a, w):
+        j = sum(x[1] for x in MATB[:[x[0] for x in MATB].index(n)])
+        return T.MBF[:, j + a:j + a + w:16]
 
     def SL(n, q):
         return M(n, (4 if n == "OWN" else 0) + 15 - q)
@@ -152,8 +161,8 @@ def rank_program(g, core, T, topo):
     emit("G", [lambda: g.iota(T.CI[:, 0:1], [[0, 1]], 0, 1)], (), ["ci0"])
     emit("G", [lambda: g.iota(T.XI[:], [[1, 312]], -48, 0, allow_small_or_imprecise_dtypes=True)], (), ["XI"])
 
-    def X(off, w):
-        return T.XI[:, 48 + off:48 + off + w]
+    def X(off, w, step=1):
+        return T.XI[:, 48 + off:48 + off + w * step:step]
 
     def fld(n, w=128):
         j = [x[0] for x in FLD].index(n)
@@ -166,9 +175,9 @@ def rank_program(g, core, T, topo):
                 w *= c
             emit("G", [lambda: g.iota(fld(n, w), pat, base, 0, allow_small_or_imprecise_dtypes=True)], (), [n])
 
-    field(0, 3)
-    ints = [("rho", 4, 1), ("h3", 3, 1), ("X0", 0, 103), ("i", 0, 15), ("k63", 0, 63),
-            ("s", 0, 7), ("g16", 0, 112), ("k96", 0, 96), ("blk", 3, 31), ("blk2", 2, 30), ("b0", 0, 1), ("b1", 1, 1)]
+    field(0, 2)
+    ints = [("rho", 4, 1), ("h3", 3, 1), ("X0", 0, 103), ("i", 0, 15), ("k63", 0, 63), ("s", 0, 7), ("g16", 0, 112), ("k96", 0, 96),
+            ("blk2", 2, 30), ("b0", 0, 1), ("b1", 1, 1), ("s2", 1, 7)]
     names = ["k"] + [x[0] for x in ints]
 
     def colints(lo, hi):
@@ -197,17 +206,35 @@ def rank_program(g, core, T, topo):
         src, fr = (X(f, n), "XI") if isinstance(f, int) else (fld(f, n), f)
         ts(dst, src, col(h), A.is_equal, col(w) if isinstance(w, str) else w, A.mult, [fr, "c_" + h] + (["c_" + w] if isinstance(w, str) else []), [name])
 
-    colints(0, 9)
+    def mats(f, h, n, outs):
+        act(M("TMP", 0, n), fld(f, n), -1.0, col(h), [f, "c_" + h], ["TMP"], (), AF.Abs)
+        for name, w in outs:
+            act(M(name), M("TMP", 0, n), -1.0, col(w) if isinstance(w, str) else w, ["TMP"] + (["c_" + w] if isinstance(w, str) else []), [name], (), AF.Relu)
+
+    fill(M("ONES"), 1.0, ["ONES"])
+    fill(T.RS[:], 1.0, ["RS"])
+    fill(T.OT[:, 4112:4160], 0.0, ["OTx"])
+    fill(T.W[:, 4096:4160], LOW, ["Wz"])
+    fill(T.RS[:, 0::8], 0.0, ["RS"])
+    colints(0, 8)
     lin("OXn", "h3", 16, "X0", "V")
     lin("OXm", "rho", 136, "OXn", "V")
     for n, a, m, add in (("sa", "rho", -32, "k"), ("sg64", "rho", 2.0 / 64, -1.0 / 64), ("cb", "i", -16, MAGIC), ("xa", "k96", 4, 0.0),
                          ("xb", "h3", 64, "xa"), ("sent", "h3", -64, 64.0), ("w64", "h3", -63, 64.0),
-                         ("ta", "rho", -16, "X0"), ("g0", "h3", -1, 1.0), ("ot", "rho", -32, "g16"), ("wz", "s", -65536, 13 * 32768.0)):
+                         ("ta", "rho", -16, "X0"), ("ot", "rho", -32, "g16"), ("kxa", "rho", -32, 16.0), ("kx", "k63", 1, "kxa")):
         lin(n, a, m, add)
-    fill(M("ONES"), 1.0, ["ONES"])
     mat("OX", -8, "OXm", 1.0)
     mat("OWN", -19, "g16", 1.0)
     mat("SW", -16, "sa", 1.0)
+    fill(M("YM"), -65536.0, ["YM"])
+    fill(M("ANY"), -BIG, ["ANY"])
+    for c0, reg in ((4096, "OTz"), (8256, "OTy")):
+        act(T.OT[:, c0:c0 + 16], M("ONES", 0, 16), col("sent"), 0.0, ["ONES", "c_sent"], [reg])
+    sc(M("R32"), M("OWN", 4, 144), 32.0, ["OWN"], ["R32"])
+    act(M("BKO"), M("OWN", 4, 144), col("w64"), 0.0, ["OWN", "c_w64"], ["BKO"])
+    sc(M("NOWN"), M("OWN"), -1.0, ["OWN"], ["NOWN"])
+    sc(M("NSW"), M("SW"), -1.0, ["SW"], ["NSW"])
+    sc(M("ISM"), M("SW"), -0.5, ["SW"], ["ISM"])
     for j, (sh, m) in enumerate([(6, 1), (7, 127), (0, 63)]):
         ts(T.FI[:, 128 * j:128 * j + 128], T.OI[:], sh, A.logical_shift_right, m, A.bitwise_and, ["OI"], ["FI%d" % j])
     ts(T.FB[:, 0:128], T.FI[:, 0:128], 65.0, A.mult, None, None, ["FI0"], ["FB0"])
@@ -218,25 +245,31 @@ def rank_program(g, core, T, topo):
 
     eo = topo.engines(core, cores[same[(idx + 1) % 4]])
     es = [e for e in topo.engines(core, mate) if e not in eo]
+    mo, ms_ = sum(1 << e for e in eo), sum(1 << e for e in es)
 
     def blocks(x, j0, j1):
         return T[x][:, EX[x][0] * j0:EX[x][0] * j1]
 
+    def own(x):
+        return [x + "s0", x + "s0a", x + "s0b", x + "s0c"]
+
     def send(x):
         w, k, near = EX[x]
-        pre("G", [y + "s0" for y in (x,) + near], [])
+        pre("G", own(x), [])
         one = [(same[(idx + j) % 4], j) for j in range(1, 4 - k)]
         both = [(side[(idx + j) % 4], j + o) for j in range(4 - k, 4) for side, o in ((same, 0), (other, 4))]
         to = one + both
-        trs = [RemoteDMATransfer(dst_ids=dst([cores[r] for r, j in to]), dma_engine_mask=sum(1 << e for e in eo), remote_sem=T.sem["r%d%s" % (rank, x)],
+        sem = T.sem["r%d%s" % (rank, x)]
+        trs = [RemoteDMATransfer(dst_ids=dst([cores[r] for r, j in to]), dma_engine_mask=mo, remote_sem=sem,
                                  srcs=[blocks(x, 0, 1)], dsts=[blocks(x, j, j + 1) for r, j in to])]
-        n = len(es) // max(len(near), 1)
-        for i, y in enumerate(near):
-            trs.append(RemoteDMATransfer(dst_ids=dst([mate]), dma_engine_mask=sum(1 << e for e in es[n * i:n * i + n]),
-                                         remote_sem=T.sem["r%d%s" % (rank, y)], srcs=[blocks(y, 0, 1)], dsts=[blocks(y, 4, 5)]))
-            arrive("r%d%s" % (at[4], y), n, [y + "s4"])
+        if near:
+            trs.append(RemoteDMATransfer(dst_ids=dst([mate]), dma_engine_mask=ms_, remote_sem=sem, srcs=[blocks(x, 0, 1)], dsts=[blocks(x, 4, 5)]))
         g.remote_dma_fused(trs, local_sem=T.sem["l" + x])
-        toks_all["l" + x] = len(eo) + n * len(near)
+        toks_all["l" + x] = len(eo) + (len(es) if near else 0)
+        if not near:
+            g.remote_dma(blocks(x, 4, 5), blocks(x, 0, 1), sem, T.sem["m" + x], topo.addr(mate)[1], topo.addr(mate)[0], ms_)
+            toks_all["m" + x] = len(es)
+        arrive("r%d%s" % (at[4], x), len(es), [x + "s4"])
         for j in [1, 2, 3] + list(range(8 - k, 8)):
             arrive("r%d%s" % (at[j], x), len(eo), [x + "s%d" % j])
 
@@ -247,42 +280,44 @@ def rank_program(g, core, T, topo):
             return
         n, f = "n%d%s" % (j0, x), "f%d%s" % (j0, x)
         pre("G", [x + "s%d" % j for j in range(j0, j1)], [])
-        g.remote_dma(blocks(x, 4 + j0, 4 + j1), blocks(x, j0, j1), T.sem[n], T.sem[f], topo.addr(mate)[1], topo.addr(mate)[0], sum(1 << i for i in es))
+        g.remote_dma(blocks(x, 4 + j0, 4 + j1), blocks(x, j0, j1), T.sem[n], T.sem[f], topo.addr(mate)[1], topo.addr(mate)[0], ms_)
         toks_all[f] = len(es)
         arrive(n, len(es), [x + "s%d" % j for j in range(4 + j0, 4 + j1)])
 
     mms([(T.RV[:, 128 * b + 64 * h:128 * b + 64 * h + 64], M("OX", 136 * h + (0 if j == 2 else 8)), T.FB[:, 128 * j + 64 * b:128 * j + 64 * b + 64], j == 0, j == 2)
          for b in (0, 1) for h in (0, 1) for j in range(3)], ["FB0", "FB1", "OX"], ["RV.r"], ["RV"])
 
-    def pack(x, cols):
-        for o, i, n in cols:
-            for hl, src, name in ((0, T.HI, "HI"), (1, T.LO, "LO")):
-                mms([(T.UP[:, 384 + 128 * a + o:384 + 128 * a + o + n], M("KP", 128 * a + 64 - 64 * hl), src[:, i:i + n], hl == 0, hl == 1) for a in (0, 1)],
-                    [name, "KP"], ["UPa.r", "UPb.r"] if hl == 0 and o == 0 else ["UP.%d.%d" % (hl, o)], ["UPa", "UPb"])
-        cp("V", blocks(x, 0, 1), T.UP[:, 384:640], ["UPa.r", "UPb.r", "UP.1.%d" % cols[-1][0]], [x + "s0"], ["UPa", "UPb"])
+    def pack(x, high, Y, yr, yb):
+        n = EX[x][0] // 2
+        for a in (0, 1):
+            high(T[x][64 * a:64 * a + 64, n * a:n * a + n], slice(64 * a, 64 * a + 64), x + ("s0", "s0a")[a])
+        for a in (0, 1):
+            tt(T[x][64 - 64 * a:128 - 64 * a, n * a:n * a + n], Y(slice(64 * a, 64 * a + 64)), T[x][64 * a:64 * a + 64, n * a:n * a + n], A.subtract,
+               [yr, x + ("s0", "s0a")[a]], [x + ("s0b", "s0c")[a]], [yb])
 
     OTALL = ["OTx", "OTz", "OTy"] + ["OT%d%d%s" % (b, r, z) for b in (0, 1) for r in range(8) for z in "ab"]
     WALL = ["Wz"] + ["W%d%d%s" % (b, r, z) for b in (0, 1) for r in range(8) for z in "ab"]
-    rb = [("YY", 0, "YY"), ("NP", 0, "NP"), ("DD", 0, "DD"), ("RV", 0, "RV"), ("UP", 0, "UPa"), ("UP", 512, "UPb")]
+    rb = ["YY", "UB", "DD", "UA", "RV", "NP"]
     nb = [0]
 
     def rep(x, j, b, q):
         w, d0 = EX[x][0], place(at[j], b)
         n = 4 // len(q)
         for i, qi in enumerate(q):
-            buf, c0, bank = rb[nb[0] % len(rb)]
+            bank = rb[nb[0] % len(rb)]
             nb[0] += 1
             ps = range(n * i, n * i + n)
-            outs = [T[buf][:, c0 + 128 * (p - n * i):c0 + 128 * (p - n * i) + 128] for p in ps]
             if x[1] == "O":
                 s0 = w * j + (128 * b if x == "LOi" else 0)
-                ms = [(o, M("REP", 128 * p), T[x][:, s0:s0 + 128], True, True) for o, p in zip(outs, ps)]
+                ms = [(T[bank][:, 128 * (p - n * i):128 * (p - n * i) + 128], M("REP", 128 * p), T[x][:, s0:s0 + 128], True, True) for p in ps]
                 mr, tab, reg = ["REP"], T.OT, "OT"
             else:
-                ms = [(o, M("RW", 128 * (p & 1)), T[x][:, w * j + 128 * (p >> 1):w * j + 128 * (p >> 1) + 128], True, True) for o, p in zip(outs, ps)]
+                cut = [(64 * h, 128 * h + 64 * b, 64) for h in (0, 1)] if x == "LWi" else [(0, 0, 128)]
+                ms = [(T[bank][:, 128 * (p - n * i) + o:128 * (p - n * i) + o + c], M("RW", 128 * (p & 1)),
+                       T[x][:, w * j + w // 2 * (p >> 1) + s:w * j + w // 2 * (p >> 1) + s + c], True, True) for p in ps for o, s, c in cut]
                 mr, tab, reg = ["RW"], T.W, "W"
-            mms(ms, [x + "s%d" % j] + mr, [bank + ".r"], [bank])
-            o, src = tab[:, d0 + 128 * n * i:d0 + 128 * n * (i + 1)], T[buf][:, c0:c0 + 128 * n]
+            mms(ms, (own(x) if j == 0 else [x + "s%d" % j]) + mr, [bank + ".r"], [bank])
+            o, src = tab[:, d0 + 128 * n * i:d0 + 128 * n * (i + 1)], T[bank][:, 0:128 * n]
             W = ["%s%d%d%s" % (reg, b, at[j], z) for z in ("ab" if n == 4 else "ab"[i])]
             if reg == "OT":
                 cp(qi, o, src, [bank + ".r"], W, [bank])
@@ -292,90 +327,94 @@ def rank_program(g, core, T, topo):
                 act(o, src, 1.0, col("cb"), [bank + ".r", "c_cb"], W, [bank])
 
     def order(x):
-        return [[0, 4, 1, 2, 3, 5, 6, 7], [0, 4, 1, 2, 3, 7, 5, 6], [0, 4, 1, 2, 6, 3, 5, 7], [0, 4, 1, 5, 2, 6, 3, 7]][EX[x][1]]
+        return [[0, 4, 1, 2, 3, 5, 6, 7], [0, 4, 1, 2, 3, 5, 7, 6], [0, 4, 1, 2, 6, 3, 5, 7], [0, 4, 1, 5, 2, 6, 3, 7]][EX[x][1]]
 
-    def expand(b):
-        d0 = place(rank, b)
-        emit("S", [lambda: g.scalar.activation(out=T["XE%d" % b][:], in_=T.W[:, d0:d0 + 512].indirect(T.XL[:]), func=AF.Copy)],
-             ["W%d%da" % (b, rank), "W%d%db" % (b, rank), "XL"], ["XE%d" % b])
+    def XE(b):
+        return ["XE%d.%d" % (b, s) for s in range(8)]
 
-    mat("KP", "f63", "sa", -1.0)
-    ts(T.HI[:], T.ST[:], col("sg64"), A.mult, None, None, ["ST", "c_sg64"], ["HI"])
-    cp("S", blocks("LOi", 0, 1), T.RV[:, 0:256], ["RV.r"], ["LOis0"], ["RV"])
-    send("LOi")
-    ts(T.K0[:, 256:512], T.ST[:], col("sg64"), A.mult, None, None, ["ST", "c_sg64"], ["K0.y"], ["K0"])
-    tt(T.LO[:], T.K0[:, 256:512], T.HI[:], A.subtract, ["K0.y", "HI"], ["LO"], ["K0"])
-    for c0, reg in ((4096, "OTz"), (8256, "OTy")):
-        act(T.OT[:, c0:c0 + 16], M("ONES", 0, 16), col("sent"), 0.0, ["ONES", "c_sent"], [reg])
-    sc(M("R32"), M("OWN", 4, 144), 32.0, ["OWN"], ["R32"])
-    act(M("BKO"), M("OWN", 4, 144), col("w64"), 0.0, ["OWN", "c_w64"], ["BKO"])
-    sc(M("NSW"), M("SW"), -1.0, ["SW"], ["NSW"])
-    sc(M("ISM"), M("SW"), -0.5, ["SW"], ["ISM"])
-    mat("RW", "f31", "k63", 1.0)
-    mat("REP", "f31", "k", 1.0)
-    ts(T.XL[:], X(0, 64), col("xb"), A.add, None, None, ["XI", "c_xb"], ["XL"])
-    mat("ENT", -24, "ta", "w64")
-    pack("LW0", [(64 * h, 128 * h, 64) for h in (0, 1)])
-    send("LW0")
-    rep("LW0", 0, 0, "S")
-    expand(0)
-    colints(9, len(ints))
-    pack("LW1", [(64 * h, 128 * h + 64, 64) for h in (0, 1)])
-    send("LW1")
-    field(3, len(FLD))
-    forward("LOi", 1, 2)
-    forward("LOi", 2, 4)
-    forward("LW0")
-    forward("LW1")
-    mms([(T.K0[:, 64 * b:64 * b + 64], M("ENT", 8 - 8 * h), T.LOi[:, 128 * b + 64 * h:128 * b + 64 * h + 64], h == 0, h == 1) for b in (0, 1) for h in (0, 1)],
-        ["LOis0", "ENT"], ["K0.o"], ["K0"])
-    for b in (0, 1):
-        rep("LOi", 0, b, "S")
+    def expand(b, q):
+        d0, R = place(rank, b), ["W%d%da" % (b, rank), "W%d%db" % (b, rank)]
+        if q == "S":
+            cp("S", T["XE%d" % b][:], T.W[:, d0:d0 + 512].indirect(T.XL[:]), R + ["XL"], XE(b))
+        elif q == "X":
+            cp("S", T.XW[:], T.W[:, d0:d0 + 512].indirect(T.XS[:]), R + ["XS"], ["XW"])
+        else:
+            for s in range(8):
+                cp("G", T["XE%d" % b][:, s::8], T.XW[:], ["XW"], XE(b)[s:s + 1])
 
     def partners(js):
         for j in js:
-            tt(M("BD%d" % j), M("R32"), M("OWN", 4 - DELTA[j], 144), A.subtract, ["R32", "OWN"], ["BD%d" % j])
+            c0 = (15 + DELTA[j]) % 16
+            cp("G", M("BD%d" % j), M("R32"), ["R32"], ["BD%d" % j])
+            cp("G", MS("BD%d" % j, c0, 144 - c0), MS("NOWN", 4 - DELTA[j] + c0, 144 - c0), ["NOWN"], ["BD%d" % j])
 
-    lin("bl", "rho", -8, "blk2", "V")
-    cp("V", T.OF[:], T.K0[:, 0:128], ["K0.o"], ["OF0", "OF1"], ["K0"])
-    rep("LW1", 0, 1, "V")
+    def stays(t):
+        b, thr = t & 1, "b0" if t == 0 else "b1"
+        ts(T.H1[:], T.OF[:, 64 * b:64 * b + 64], EMPTY, A.is_equal, col(thr), A.add, ["OF%d" % b, "c_" + thr], ["H1"])
+
+    cp("S", blocks("LOi", 0, 1), T.RV[:, 0:256], ["RV.r"], ["LOis0"], ["RV"])
+    send("LOi")
+    mat("REP", "f31", "k", 1.0)
+    ts(T.K0[:, 256:512], T.ST[:], col("sg64"), A.mult, None, None, ["ST", "c_sg64"], ["K0.y"], ["K0"])
+    pack("LWi", lambda o, p, W: ts(o, T.ST[p, :], T.CF[p, names.index("sg64"):names.index("sg64") + 1], A.mult, None, None, ["ST", "c_sg64"], [W]),
+         lambda p: T.K0[p, 256:512], "K0.y", "K0")
+    send("LWi")
+    for b in (0, 1):
+        rep("LOi", 0, b, "S")
+    mat("RW", "f31", "kx", -1.0)
     ts(T.MK[:, 0:288], fld("f16", 288), col("s"), A.is_equal, None, None, ["f16", "c_s"], ["MK0"])
-    cp("V", T.OL[:], T.K0[:, 0:128], ["K0.o"], ["OL0", "OL1"], ["K0"])
-    cp("V", T.MK[:, 288:544], T.MK[:, 32:288], ["MK0"], ["MK1"])
+    cp("G", T.MK[:, 288:544], T.MK[:, 32:288], ["MK0"], ["MK1"])
+    cp("G", T.MK[:, 544:1056], T.MK[:, 32:544], ["MK0", "MK1"], ["MK2"])
+    forward("LOi", 1, 2)
+    forward("LOi", 2, 4)
+    forward("LWi", 1, 2)
+    forward("LWi", 2, 3)
+    ts(T.XL[:], X(0, 64), col("xb"), A.add, None, None, ["XI", "c_xb"], ["XL"])
+    mat("ENT", -24, "ta", "w64")
+    rep("LWi", 0, 0, "S")
+    expand(0, "S")
+    mms([(T.K1[:, 64 * b:64 * b + 64], M("ENT", 8 - 8 * h), T.LOi[:, 128 * b + 64 * h:128 * b + 64 * h + 64], h == 0, h == 1) for b in (0, 1) for h in (0, 1)],
+        ["LOis0", "ENT"], ["K1.o"], ["K1"])
+    rep("LWi", 0, 1, "V")
+    cp("V", T.OF[:], T.K1[:, 0:128], ["K1.o"], ["OF0", "OF1"], ["K1"])
+    cp("V", T.OL[:], T.K1[:, 0:128], ["K1.o"], ["OL0", "OL1"], ["K1"])
     mat("OTH", -31, "ot", 1.0)
-    cp("V", T.MK[:, 544:1056], T.MK[:, 32:544], ["MK0", "MK1"], ["MK2"])
-    ts(M("ANY"), fld("f16"), 16.0, A.mult, col("g16"), A.is_equal, ["f16", "c_g16"], ["ANY"])
+    colints(8, len(ints))
+    lin("xc", "b0", 64, "xa", "V")
+    stays(0)
+    lin("xd", "s2", 1, "xc", "V")
+    ts(T.XS[:], X(0, 8, 8), col("xd"), A.add, None, None, ["XI", "c_xd"], ["XS"])
+    field(2, len(FLD))
+    sel("IB", "ONES", [[1, 128]], A.is_equal, 0.0, 0, -1)
     partners((0, 1))
-    mat("YM", "f8", "blk", -65536.0)
-    mat("CH", "f4", "bl", 1.0)
-    for h, gn in ((0, "g0"), (1, "h3")):
-        mat("KX%d" % h, "f119", "ta", gn)
-    emit("G", [lambda: g.iota(T.OT[:, 4112:4160], [[0, 48]], 0, 0, allow_small_or_imprecise_dtypes=True)], (), ["OTx"])
-    emit("G", [lambda: g.iota(T.W[:, 4096:4160], [[0, 64]], -int(BIG), 0, allow_small_or_imprecise_dtypes=True)], (), ["Wz"])
-    emit("G", [lambda: g.affine_select(M("IB"), M("ONES"), [[1, 128]], A.is_equal, 0.0, 0, -1)], ["ONES"], ["IB"])
-    emit("G", [lambda: g.affine_select(M("YM"), M("YM"), [[1, 128]], A.is_gt, 0.0, 0, -1)], ["YM"], ["YM"])
-    emit("G", [lambda: g.iota(T.RS[:], [[0, 384]], 0, 0, allow_small_or_imprecise_dtypes=True)], (), ["RS"])
-    emit("G", [lambda: g.affine_select(M("YM"), M("YM"), [[1, 128]], A.not_equal, 32768.0, 0, -1)], ["YM"], ["YM"])
-    emit("G", [lambda: g.affine_select(T.RS[:], T.RS[:], [[0, 48], [1, 8]], A.not_equal, -BIG, 0, 0)], ["RS"], ["RS"])
-    emit("G", [lambda: g.affine_select(M("ISM"), M("ISM"), [[1, 128]], A.not_equal, 0.5, 0, -1)], ["ISM"], ["ISM"])
+    sel("YM", "YM", [[-8, 16], [0, 8]], A.is_ge, 0.0, 0, 1)
+    sel("YM", "YM", [[1, 128]], A.is_gt, 0.0, 0, -1)
+    sel("YM", "YM", [[1, 128]], A.not_equal, 32768.0, 0, -1)
+    sel("ANY", "ANY", [[-16, 8], [0, 16]], A.is_ge, 0.0, 0, 1)
+    sel("ANY", "ANY", [[16, 8], [0, 16]], A.is_ge, 0.0, 15, -1)
+    sel("ISM", "ISM", [[1, 128]], A.not_equal, 0.5, 0, -1)
 
     def late2():
+        lin("bl", "rho", -8, "blk2")
+        lin("wz", "s", -65536, 13 * 32768.0)
+        lin("g0", "h3", -1, 1.0)
+        mats("f4", "bl", 132, [("CH", 1.0)])
         act(M("ZC"), M("CH"), col("wz"), 0.0, ["CH", "c_wz"], ["ZC"])
         sc(M("KEEPN"), M("IB"), -16384.0, ["IB"], ["KEEPN"])
+        mats("f119", "ta", 128, [("KX0", "g0"), ("KX1", "h3")])
+
+    def late3():
         for h in (0, 1):
             sc(M("KN%d" % h), M("KX%d" % h), -256.0, ["KX%d" % h], ["KN%d" % h])
         lin("nt64", "i", -16, 0.0)
         lin("eg0", "h3", EMPTY, -EMPTY)
         lin("c8", "rho", -2.0 / 256, 1.0 / 256)
         act(M("TMN"), M("IB"), col("nt64"), 0.0, ["IB", "c_nt64"], ["TMN"])
-
-    def late3():
-        sc(M("C2M"), M("IB"), 2 * MAGIC, ["IB"], ["C2M"])
-        sc(M("ANY"), M("ANY"), -BIG, ["ANY"], ["ANY"])
+        sc(M("C2M"), M("IB"), MAGIC, ["IB"], ["C2M"])
         act(M("CM"), M("IB"), col("c8"), 0.0, ["IB", "c_c8"], ["CM"])
 
     def late4():
-        sc(M("ISM64"), M("ISM"), 64.0, ["ISM"], ["ISM64"])
+        lin("iv", "rho", -8, "OXn")
         sc(M("CM64"), M("CM"), 64.0, ["CM"], ["CM64"])
         lin("sgn", "rho", 2, -1.0)
         lin("s64", "rho", 128, -64.0)
@@ -386,67 +425,58 @@ def rank_program(g, core, T, topo):
         tt(T.GM[:], T.OT[:].indirect(T.OL[:, 64 * b:64 * b + 64]), T.MK[:, 16 * t:16 * t + 1024], A.mult, OTALL + ["OL%d" % b, "MK0", "MK1", "MK2"], ["GM"])
 
     def lists(t):
-        b = t & 1
         mms([(T.K0[:, 0:64], SL("BKO", q), T.GM[:, q::16], q == 0, q == 15) for q in range(16)], ["GM", "BKO"], ["K0.k"], ["K0"])
-        ts(T.KC[:], T.K0[:, 0:64], 32768.0 - 8256.0, A.add, None, None, ["K0.k"], ["KC"], ["K0"])
         cp("V", T.KL[:, 0:64], T.K0[:, 0:64], ["K0.k"], ["KL0"], ["K0"])
 
-    def swapped(t):
-        mms([(T.K1[:, 0:64], M("SW"), T.KC[:], True, True)], ["KC", "SW"], ["K1.k"], ["K1"])
-        b = t & 1
-        thr = "b0" if t == 0 else "b1"
-        ts(T.H1[:], T.OF[:, 64 * b:64 * b + 64], EMPTY, A.is_equal, col(thr), A.add, ["OF%d" % b, "c_" + thr], ["H1"])
-        ts(T.KL[:, 64:128], T.K1[:, 0:64], 8256.0 - 32768.0, A.add, None, None, ["K1.k"], ["KL1"], ["K1"])
-
-    def natural(b):
+    def natural(b, part):
         n = T.OF[:, 64 * b:64 * b + 64]
-        ts(T.YH[:], n, 1.0 / 64, A.mult, 1025.0 - 63.0 / 128, A.add, ["OF%d" % b], ["YH"])
-        emit("S", [lambda: g.scalar.activation(out=T.YB[:], in_=n, func=AF.Sign, bias=-(EMPTY + 63.5))], ["OF%d" % b], ["YB"])
-        mms([(T.YY[:, 128:192], M("INVF"), n, True, False), (T.YY[:, 128:192], M("INV0"), T.YH[:], False, False),
-             (T.YY[:, 128:192], M("INV1"), T.YB[:], False, True)], ["OF%d" % b, "YH", "YB", "INVF", "INV0", "INV1"], ["YY.n"], ["YY"])
-        act(T["YO%d" % b][:], T.YY[:, 128:192], 1.0, -65600.0 - 4128.0, ["YY.n"], ["YO%d" % b], ["YY"])
-        dmas("Y", [(T.yo[:, 64 * b:64 * b + 64], T["YO%d" % b][:])], "dO%d" % b, ["YO%d" % b], [])
+        if part == 0:
+            ts(T.YH[:], n, 1.0 / 64, A.mult, 1025.0 - 63.0 / 128, A.add, ["OF%d" % b], ["YH"])
+            ts(T.YB[:], n, EMPTY + 63.5, A.is_gt, None, None, ["OF%d" % b], ["YB"])
+            mms([(T.NP[:, 128:192], M("INVF"), n, True, False), (T.NP[:, 128:192], M("INV0"), T.YH[:], False, False),
+                 (T.NP[:, 128:192], M("INV1"), T.YB[:], False, True)], ["OF%d" % b, "YH", "YB", "INVF", "INV0", "INV1"], ["NP.y"], ["NP"])
+        else:
+            act(T["YO%d" % b][:], T.NP[:, 128:192], 1.0, -65600.0, ["NP.y"], ["YO%d" % b], ["NP"])
+            dmas("Y", [(T.yo[:, 64 * b:64 * b + 64], T["YO%d" % b][:])], "dO%d" % b, ["YO%d" % b], [])
 
     def round_(t):
         b, m = t & 1, 1 + t
         nx = {0: "2", 1: "3", 2: None}[t]
-        xe = ["XE%d" % b]
+        xe, XEb = XE(b), T["XE%d" % b]
         Wt = T.W[:]
         ol = T.OL[:, 64 * b:64 * b + 64]
-        emit("S", [lambda: g.scalar.activation(out=T.U[:], in_=Wt.indirect(ol), func=AF.Copy)], WALL + ["OL%d" % b], ["U"])
-        cp("S", T.UP[:], T.U[:], ["U"], ["UPa.r", "UPb.r"], ["UPa", "UPb"])
+        st = {1: [(0, 1), (2, 3)], 2: [(0, 2), (1, 3)], 3: [(0, 3), (1, 2)]}[m]
+        thr = "b0" if m == 1 else "b1"
+        mms([(T.K1[:, 0:64], SL("BKX", q), T.GM[:, q::16], q == 0, q == 15) for q in range(16)], ["GM", "BKX"], ["K1.k"], ["K1"])
+        cp("S", T.U[:], Wt.indirect(ol), WALL + ["OL%d" % b], ["U"])
+        for i, (u, v) in enumerate(st):
+            cp("S", T.UA[:, 256 * i:256 * i + 256], T.U[:, v::4], ["U"], ["UA.r"] if i == 0 else ["UA.2"], ["UA"])
+        act(T.KC[:], T.K0[:, 0:64], 1.0, 32768.0 - 8256.0, ["K0.k"], ["KC"], ["K0"])
         if t == 0:
             late2()
-        if t == 1:
-            lin("iv", "rho", -8, "OXn")
-        if nx:
-            expand(1 - b)
+        tt(T.VO[:], Wt.indirect(T.KL[:, 0:64]), XEb[:], A.is_gt, WALL + ["KL0"] + xe, ["VO"])
+        mms([(T.RV[:, 0:64], SL("OWN", q), T.VO[:, q::16], q == 0, False) for q in range(16)], ["VO", "OWN"], ["RV.v"], ["RV"])
+        cp("V", T.KL[:, 64:128], T.K1[:, 0:64], ["K1.k"], ["KL1"], ["K1"])
         if t == 1:
             late4()
         if t == 2:
             outputs(1)
-        XE = T["XE%d" % b]
-        tt(T.VO[:], Wt.indirect(T.KL[:, 0:64]), XE[:], A.is_gt, WALL + ["KL0"] + xe, ["VO"])
-        mms([(T.RV[:, 0:64], SL("OWN", q), T.VO[:, q::16], q == 0, False) for q in range(16)], ["VO", "OWN"], ["RV.v"], ["RV"])
-        tt(T.VX[:], Wt.indirect(T.KL[:, 64:128]), XE[:], A.is_lt, WALL + ["KL1"] + xe, ["VX"])
+        tt(T.VX[:], Wt.indirect(T.KL[:, 64:128]), XEb[:], A.is_lt, WALL + ["KL1"] + xe, ["VX"])
         mms([(T.RV[:, 0:64], SL("OTH", q), T.VX[:, q::16], False, q == 15) for q in range(16)], ["VX", "OTH"], ["RV.v2"], ["RV"])
-        st = {1: [(0, 1, 4), (2, 3, 4)], 2: [(0, 2, 4), (1, 3, 4)], 3: [(0, 3, 4), (1, 2, 4)]}[m]
-        thr = "b0" if m == 1 else "b1"
+        act(T.R1[:], T.RV[:, 0:64], 1024.0, col(thr), ["RV.v", "RV.v2", "c_" + thr], ["R1"], ["RV"])
+        if t == 0:
+            late3()
         nq = 0
-        for u, v, s in st:
-            for y, z in ((u, v), (v, u)):
-                tt(T.C[:, y::s], T.U[:, y::s], T.UP[:, z::s], A.is_gt, ["U", "UPa.r", "UPb.r"], ["C%d" % y], ["UPa", "UPb"])
-                qs = range(y, 16, s)
-                mms([(T.DD[:, 0:64], SL("BD%d" % DELTA.index((q ^ m) - q), q), T.C[:, q::16], nq + j == 0, nq + j == 15) for j, q in enumerate(qs)],
-                    ["C%d" % y] + ["BD%d" % j for j in range(6)], ["DD.d%d" % y], ["DD"])
-                nq += len(qs)
-        dd = ["DD.d%d" % y for u, v, s in st for y in (u, v)]
-        ts(T.R1[:], T.RV[:, 0:64], 1024.0, A.mult, col(thr), A.add, ["RV.v", "RV.v2", "c_" + thr], ["R1"], ["RV"])
-        if t == 2:
-            natural(1)
+        for i, (u, v) in enumerate(st):
+            for y, op in ((u, A.is_gt), (v, A.is_lt)):
+                tt(T.C[:, y::4], T.U[:, u::4], T.UA[:, 256 * i:256 * i + 256], op, ["U", "UA.r", "UA.2"], ["C%d" % y], ["UA"])
+                mms([(T.DD[:, 0:64], SL("BD%d" % DELTA.index((q ^ m) - q), q), T.C[:, q::16], nq + j == 0, nq + j == 15) for j, q in enumerate(range(y, 16, 4))],
+                    ["C%d" % y, "BD%d" % (2 * t), "BD%d" % (2 * t + 1)] + (["BD0", "BD1"] if m == 3 else []), ["DD.d%d" % y], ["DD"])
+                nq += 4
+        dd = ["DD.d%d" % y for y in range(4)]
         if t == 1:
             mat("INVF", -8, "iv", 1.0)
-            sc(M("INV1"), M("INVF"), -4128.0, ["INVF"], ["INV1"])
+            sc(M("INV1"), M("INVF"), -8256.0, ["INVF"], ["INV1"])
         tt(T.REV[:], T.DD[:, 0:64], T.R1[:], A.is_ge, dd + ["R1"], ["REV"], ["DD"])
         mms([(T.YY[:, 0:64], M("YM"), T.REV[:], True, True)], ["REV", "YM"], ["YY.y"], ["YY"])
         if t == 1:
@@ -460,10 +490,8 @@ def rank_program(g, core, T, topo):
         ts(T.CL[:], T.K1[:, 64:96], 8256.0, A.add, None, None, ["K1.z", "K1.c"], ["CL"], ["K1"])
         if nx:
             mms([(T.RV[:, 64 * h + 128:64 * h + 192], M("KX%d" % h), T.KEEP[:], True, True) for h in (0, 1)], ["KEEP", "KX0", "KX1"], ["RV.k"], ["RV"])
-        emit("V", [lambda: g.vector.tensor_copy(out=T.E[:, 0:256], in_=T.OT[:].indirect(T.CL[:, 0:16]))], OTALL + ["CL"], ["E0"])
-        emit("S", [lambda: g.scalar.activation(out=T.E[:, 256:512], in_=T.OT[:].indirect(T.CL[:, 16:32]), func=AF.Copy)], OTALL + ["CL"], ["E1"])
-        if t == 0:
-            late3()
+        cp("V", T.E[:, 0:256], T.OT[:].indirect(T.CL[:, 0:16]), OTALL + ["CL"], ["E0"])
+        cp("S", T.E[:, 256:512], T.OT[:].indirect(T.CL[:, 16:32]), OTALL + ["CL"], ["E1"])
         mms([(T.NP[:, 32 * e:32 * e + 32], M("ENT", 8 - 8 * h), T.E[:, 8 * h + 4 * e::16], False, h == 1 and e == 1) for e in (0, 1) for h in (0, 1)],
             ["E0", "E1", "ENT"], ["NP.n2"], ["NP"])
         tt(T.OK[:], T.OF[:, 64 * b:64 * b + 64], T.KEEP[:], A.mult, ["OF%d" % b, "KEEP"], ["OK"])
@@ -480,41 +508,43 @@ def rank_program(g, core, T, topo):
         if nx:
             tt(blocks("LO" + nx, 0, 1), T.DD[:, 128:256], T.OXA[:], A.max, ["DD.x0", "DD.x1", "OXA"], ["LO%ss0" % nx], ["DD"])
             send("LO" + nx)
-        mms([(T.K0[:, 0:128], M("NSW"), XE[:, 0::8], True, False), (T.K0[:, 0:128], M("TMN"), M("ONES"), False, False),
+        mms([(T.K0[:, 0:128], M("NSW"), XEb[:, 0::8], True, False), (T.K0[:, 0:128], M("TMN"), M("ONES"), False, False),
              (T.K0[:, 0:128], M("C2M"), M("ONES"), False, False)], xe + ["NSW", "TMN", "C2M", "ONES"], ["K0.a"], ["K0"])
-        cut = CUT[0 if nx else 1]
-        emit("S", [lambda: g.scalar.activation(out=T.HN[:, 0::2], in_=n, func=AF.Abs, bias=col("eg0"), scale=col("g0"))], ["OF%d" % b, "c_g0", "c_eg0"], ["HN1"])
+        cut, k = CUT[0 if nx else 1], 1.0 if nx else 64.0
+        act(T.HN[:, 0::2], n, col("g0"), col("eg0"), ["OF%d" % b, "c_g0", "c_eg0"], ["HN1"], (), AF.Abs)
         for h in (1, 2, 3):
-            emit("S", [lambda: g.scalar.activation(out=T.U5[:, 16 * cut[h]:16 * cut[h + 1]], in_=Wt.indirect(T.OL[:, 64 * b + cut[h]:64 * b + cut[h + 1]]),
-                                                   func=AF.Copy)], WALL + ["OL%d" % b], ["U5%d" % h])
-        emit("V", [lambda: g.vector.tensor_copy(out=T.U5[:, 0:16 * cut[1]], in_=Wt.indirect(T.OL[:, 64 * b:64 * b + cut[1]]))], WALL + ["OL%d" % b], ["U50"])
+            act(T.U5[:, 16 * cut[h]:16 * cut[h + 1]], Wt.indirect(T.OL[:, 64 * b + cut[h]:64 * b + cut[h + 1]]), k, -k * LOW, WALL + ["OL%d" % b], ["U5%d" % h])
         ts(T.HN[:, 1::2], n, EMPTY, A.not_equal, col("h3"), A.mult, ["OF%d" % b, "c_h3"], ["HN2"])
+        ts(T.U5[:, 0:16 * cut[1]], Wt.indirect(T.OL[:, 64 * b:64 * b + cut[1]]), -LOW, A.add, k, A.mult, WALL + ["OL%d" % b], ["U50"])
         mms([(T.K0[:, 0:128], M("ANY"), T.HN[:], False, True)], ["HN1", "HN2", "ANY"], ["K0.b"], ["K0"])
-        mms([(T.RV[:, 256:384], M("CM" if nx else "CM64"), M("ONES"), True, False)], ["CM", "CM64", "ONES"], ["RV.t"], ["RV"])
+        mms([(T.RV[:, 256:384], M("CM" if nx else "CM64"), M("ONES"), True, False)], ["CM" if nx else "CM64", "ONES"], ["RV.t"], ["RV"])
         for h in range(4):
             emit("V", [lambda: g.vector.tensor_tensor_scan(out=T.MX[:, 16 * cut[h]:16 * cut[h + 1]], data0=T.RS[:, 0:16 * (cut[h + 1] - cut[h])],
-                                                           data1=T.U5[:, 16 * cut[h]:16 * cut[h + 1]], initial=-2.0 * BIG, op0=A.add, op1=A.max)], ["RS", "U5%d" % h], ["MX%d" % h])
-        tt(T.OWNW[:], T.MX[:, 7::8], T.K0[:, 0:128], A.max, ["MX0", "MX1", "MX2", "MX3", "K0.a", "K0.b"], ["OW"], ["K0"])
-        ism, k = ("ISM", 1.0) if nx else ("ISM64", 64.0)
-        mms([(T.RV[:, 256 + 64 * h:320 + 64 * h], M(ism), T.OWNW[:, h::2], False, h == 1) for h in (0, 1)], ["OW", ism], ["RV.s"], ["RV"])
+                                                           data1=T.U5[:, 16 * cut[h]:16 * cut[h + 1]], initial=0.0, op0=A.mult, op1=A.max)], ["RS", "U5%d" % h], ["MX%d" % h])
+            if h == 0:
+                ts(T.D[:], T.K0[:, 0:128], LOW - MAGIC, A.max, k, A.mult, ["K0.a", "K0.b"], ["D"], ["K0"])
+                mms([(T.RV[:, 256 + 64 * i:320 + 64 * i], M("ISM"), T.D[:, i::2], False, False) for i in (0, 1)], ["D", "ISM"], ["RV.d"], ["RV"])
+                if t:
+                    natural(b, 0)
+        if t:
+            natural(b, 1)
+        mx = ["MX0", "MX1", "MX2", "MX3"]
+        mms([(T.RV[:, 256 + 64 * h:320 + 64 * h], M("ISM"), T.MX[:, 7 + 8 * h::16], False, h == 1) for h in (0, 1)], mx + ["ISM"], ["RV.s"], ["RV"])
         for h in (0, 1):
-            act(T.M1[:, 64 * h:64 * h + 64], T.OWNW[:, h::2], k, -k * MAGIC, ["OW"], ["M1%d" % h])
+            tt(T.M1[:, 64 * h:64 * h + 64], T.MX[:, 7 + 8 * h::16], T.D[:, h::2], A.add, mx + ["D"], ["M1%d" % h])
+        new = ["RV.s", "RV.d", "RV.t", "M10", "M11"]
         if nx:
             nb[0] = 0
-            rep("LO" + nx, 0, b, "S")
-            partners((2 * t + 2,))
-            Y = T.K1[:, 256:384]
-            tt(T.HI[:, 0:128], T.RV[:, 256:384], T.M1[:], A.max, ["RV.s", "RV.t", "M10", "M11"], ["HI"], ["RV"])
-            tt(Y, T.RV[:, 256:384], T.M1[:], A.max, ["RV.s", "RV.t", "M10", "M11"], ["K1.y"], ["RV", "K1"])
-            tt(T.LO[:, 0:128], Y, T.HI[:, 0:128], A.subtract, ["K1.y", "HI"], ["LO"], ["K1"])
-            partners((2 * t + 3,))
-            pack("LW" + nx, [(0, 0, 128)])
+            for j in (0, 4):
+                rep("LO" + nx, j, b, "S")
+            tt(T.K1[:, 256:384], T.RV[:, 256:384], T.M1[:], A.max, new, ["K1.y"], ["RV", "K1"])
+            pack("LW" + nx, lambda o, p, W: tt(o, T.RV[p, 256:384], T.M1[p, :], A.max, new, [W], ["RV"]), lambda p: T.K1[p, 256:384], "K1.y", "K1")
             send("LW" + nx)
-            forward("LO" + nx)
             forward("LW" + nx)
+            partners((2 * t + 2, 2 * t + 3))
+            stays(t + 1)
         else:
-            natural(b)
-            tt(T.YI[:], T.RV[:, 256:384], T.M1[:], A.max, ["RV.s", "RV.t", "M10", "M11"], ["YI"], ["RV"])
+            tt(T.YI[:], T.RV[:, 256:384], T.M1[:], A.max, new, ["YI"], ["RV"])
             ts(T.YW0[:], T.YI[:], col("sgn"), A.mult, None, None, ["YI", "c_sgn"], ["YW0"])
             outputs(0)
 
@@ -530,38 +560,36 @@ def rank_program(g, core, T, topo):
                                      in_=T["YW%d" % b][32 * P + r0:32 * P + r0 + 16, 64 * h:64 * h + 64]).then_inc(T.sem["dY%d" % b], 16)
         toks_all["dY%d" % b] = 16 * 16
 
-    for j in (4, 1, 2, 3):
-        rep("LOi", j, 0, "V")
-        rep("LOi", j, 1, "S")
-    for j in (4, 1, 2, 3):
-        rep("LW0", j, 0, "VS"[j & 1])
-    ow = order("LW1")
-    for j in (5, 6, 7):
-        rep("LOi", j, 0, "S")
-        rep("LOi", j, 1, "V")
-        if j == 5:
-            rep("LW1", ow[1], 1, "S")
-            rep("LW1", ow[2], 1, "V")
+    expand(1, "X")
+    expand(1, "G")
+    rep("LOi", 4, 0, "V")
+    rep("LOi", 4, 1, "V")
+    rep("LWi", 4, 0, "V")
+    rep("LWi", 4, 1, "S")
+    act(M("BKX"), M("OTH"), col("w64"), 0.0, ["OTH", "c_w64"], ["BKX"])
+    for x, j in (("LOi", 1), ("LOi", 2), ("LOi", 3), ("LOi", 5), ("LWi", 1), ("LOi", 6), ("LOi", 7)):
+        rep(x, j, 0, "V")
+        rep(x, j, 1, "S")
     lists_gather(0)
-    for j in ow[3:7]:
-        rep("LW1", j, 1, "S")
-    for j in (5, 6, 7):
-        rep("LW0", j, 0, "VSV"[j - 5])
-    rep("LW1", ow[7], 1, "S")
-    lists(0)
-    swapped(0)
+    for j, qs in ((2, "SS"), (5, "SS"), (3, "VV"), (6, "SV"), (7, "SV")):
+        rep("LWi", j, 0, qs[0])
+        if j == 3:
+            lists(0)
+        rep("LWi", j, 1, qs[1])
     round_(0)
     for t, x, b in ((1, "2", 0), (2, "3", 1)):
         oo, ow = order("LO" + x), order("LW" + x)
-        for i, j in enumerate(oo[1:]):
+        for i, j in enumerate(oo[2:]):
             rep("LO" + x, j, b, "SV"[i & 1])
         lists_gather(t)
         for i, j in enumerate(ow[:5]):
             rep("LW" + x, j, b, "SSSVS"[i])
+            if i == 1 and t == 1:
+                expand(b, "X")
+                expand(b, "G")
         lists(t)
         rep("LW" + x, ow[5], b, "S")
         rep("LW" + x, ow[6], b, "V")
-        swapped(t)
         rep("LW" + x, ow[7], b, "SV")
         round_(t)
     for s in SEMAPHORES:

@@ -1,39 +1,44 @@
 from concourse.bass import DstId, RemoteDMATransfer
 from concourse.mybir import AluOpType as A, ActivationFunctionType as AF
 
-EX = {"LOi": (256, 0, False), "LWi": (512, 1, True), "LO2": (128, 3, True), "LW2": (256, 2, True), "LO3": (128, 3, True), "LW3": (256, 2, True)}
+EX = {"LOi": (256, 0, False), "LWi": (512, 1, True), "LO2": (128, 2, True), "LW2": (256, 1, True), "LO3": (128, 2, True), "LW3": (256, 1, True)}
 CUT = [(0, 12, 32, 52, 64), (0, 12, 32, 52, 64)]
+FIRST = ""
+START = "O1VS W4VS O2VS O3VS O5VS W1VS O6VS O7VS gather W2SS W5SS W3VS W6VS lists W7SV"
+LATER = "O1S O2V O6S O3V O7SV O5SV gather W0S W4S W1S W2S W3V lists W5SV W7SV W6SV"
+PASS = "T0 O1 O2 O3 W1 W2"
+XS = 20
 BIG = 2.0 ** 23
 MAGIC = 1.5 * 2.0 ** 17
 EMPTY = 4096.0
 LOW = 2.0 ** 17
-MATB = [("REP", 512), ("YM", 128), ("ZC", 132), ("ENT", 136), ("KEEPN", 128), ("ANY", 128), ("KX0", 128), ("KX1", 128),
+MATB = [("REP", 512), ("YM", 128), ("ZC", 132), ("ENT", 136), ("KEEPN", 128), ("ANY", 128), ("ANY0", 128), ("ANY1", 128), ("KX0", 128), ("KX1", 128),
         ("KN0", 128), ("KN1", 128), ("IB", 128), ("TMN", 128), ("CM", 128), ("CM64", 128), ("C2M", 128), ("ONES", 128),
-        ("OX", 272), ("INV1", 128), ("OWN", 152), ("NOWN", 152), ("R32", 144), ("OTH", 144), ("BKO", 144), ("BKX", 144),
-        ("TMP", 136)] + [("BD%d" % d, 144) for d in range(6)]
-MATF = [("CH", 132), ("SW", 128), ("NSW", 128), ("ISM", 128), ("INVF", 128)]
-MATH = [("RW", 256), ("INV0", 128)]
-FLD = [("f31", [[32, 4], [0, 4], [1, 32]], 0), ("f16", [[0, 3], [1, 8], [0, 16]], 0), ("f4", [[1, 34], [0, 4]], -5),
+        ("INV1", 128), ("OWN", 152), ("NOWN", 152), ("OTH", 144), ("BKO", 144),
+        ("TMP", 144)] + [("BD%d" % d, 144) for d in range(6)]
+MATF = [("CH", 132), ("SW", 128), ("NSW", 128), ("ISM", 128), ("INVF", 128), ("IF", 128)]
+MATH = [("RW", 256), ("INV0", 128), ("OX", 272), ("OXa", 272), ("OXb", 272)]
+FLD = [("f31", [[32, 4], [0, 4], [1, 32]], 0), ("f16", [[0, 2], [1, 8], [0, 16]], 0), ("f4", [[1, 34], [0, 4]], -5),
        ("f119", [[16, 8], [0, 2], [1, 8]], -16)]
 DELTA = [1, -1, 2, -2, 3, -3]
 F, B16, H16, I32, U16 = "float32", "bfloat16", "float16", "int32", "uint16"
 SCRATCH = {}
 for _n, _w, _d in (("W", 8256, F), ("OT", 8272, B16), ("MBF", sum(w for n, w in MATB), B16), ("MFF", sum(w for n, w in MATF), F),
                    ("MHF", sum(w for n, w in MATH), H16), ("CI", 16, I32), ("CF", 64, F), ("XI", 312, B16), ("MF", 512 * len(FLD), B16),
-                   ("MK", 1056, B16), ("RS", 384, B16), ("ST", 256, I32), ("OI", 128, I32), ("FI", 384, I32), ("FB", 384, B16), ("OF", 128, F),
-                   ("OL", 128, U16), ("XL", 64, U16), ("XE0", 1024, F), ("XE1", 1024, F), ("GM", 1024, B16), ("KL", 128, U16), ("KC", 64, F),
+                   ("MK", 1056, B16), ("RS", 384, B16), ("ST", 256, I32), ("OI", 128, I32), ("FI", 128, I32), ("FB", 384, H16), ("OF", 128, F),
+                   ("OL", 128, U16), ("XE0", 1024, F), ("XE1", 1024, F), ("GM", 1024, B16), ("KL", 128, U16), ("KC", 64, F),
                    ("H1", 64, F), ("H2", 64, F), ("U", 1024, F), ("VO", 1024, B16), ("VX", 1024, B16), ("C", 1024, B16), ("R1", 64, F),
                    ("REV", 64, B16), ("FK", 64, F), ("KEEP", 64, B16), ("OK", 64, F), ("CL", 32, U16), ("E", 512, B16),
-                   ("OXA", 128, B16), ("HN", 128, B16), ("U5", 1024, F), ("MX", 1024, F), ("D", 128, F), ("M1", 128, F), ("YI", 128, I32),
-                   ("XS", 8, U16), ("XW", 128, F), ("YW0", 128, F), ("YW1", 128, F), ("YH", 64, H16), ("YB", 64, B16),
+                   ("OXA", 128, B16), ("HN", 64, B16), ("U5", 1024, F), ("MX", 1024, F), ("D", 128, F), ("M1", 128, F), ("YI", 128, I32),
+                   ("XS", 8, U16), ("XW", 256, F), ("YW0", 128, F), ("YW1", 128, F), ("YH", 64, H16), ("YB", 64, B16),
                    ("YO0", 64, F), ("YO1", 64, F), ("LWi", 4096, H16), ("LW2", 2048, H16), ("LW3", 2048, H16),
                    ("LOi", 2048, B16), ("LO2", 1024, B16), ("LO3", 1024, B16)):
     SCRATCH[_n] = ("sbuf", [128, _w], _d)
 for _n in ("K0", "K1", "RV", "DD", "YY", "NP", "UA", "UB"):
     SCRATCH[_n] = ("psum", [128, 512], F)
 SEMAPHORES = (["sV", "sS", "sP", "sG", "dOI", "dST"]
-              + [k + x for x in EX for k in ["r%d" % r for r in range(8)] + ["n1", "n2", "l", "m", "f1", "f2"]]
-              + ["dY0", "dY1", "dO0", "dO1"])
+              + [k + x for x in EX for k in ["r%d" % r for r in range(8)] + ["n1", "n2", "n3", "l", "f1", "f2", "f3"]]
+              + [k + "%dOT" % j for k in "nf" for j in range(4)] + ["dY0", "dY1", "dO0", "dO1"])
 
 
 def rank_program(g, core, T, topo):
@@ -207,38 +212,33 @@ def rank_program(g, core, T, topo):
         ts(dst, src, col(h), A.is_equal, col(w) if isinstance(w, str) else w, A.mult, [fr, "c_" + h] + (["c_" + w] if isinstance(w, str) else []), [name])
 
     def mats(f, h, n, outs):
-        act(M("TMP", 0, n), fld(f, n), -1.0, col(h), [f, "c_" + h], ["TMP"], (), AF.Abs)
+        src, fr = (X(f, n), "XI") if isinstance(f, int) else (fld(f, n), f)
+        act(M("TMP", 0, n), src, -1.0, col(h), [fr, "c_" + h], ["TMP"], (), AF.Abs)
         for name, w in outs:
             act(M(name), M("TMP", 0, n), -1.0, col(w) if isinstance(w, str) else w, ["TMP"] + (["c_" + w] if isinstance(w, str) else []), [name], (), AF.Relu)
 
     fill(M("ONES"), 1.0, ["ONES"])
-    fill(T.RS[:], 1.0, ["RS"])
-    fill(T.OT[:, 4112:4160], 0.0, ["OTx"])
-    fill(T.W[:, 4096:4160], LOW, ["Wz"])
-    fill(T.RS[:, 0::8], 0.0, ["RS"])
-    colints(0, 8)
+    fill(M("YM"), -65536.0, ["YM"])
+    fill(M("ANY"), -BIG, ["ANY"])
+    sel("IB", "ONES", [[1, 128]], A.is_equal, 0.0, 0, -1)
+    colints(0, len(ints))
     lin("OXn", "h3", 16, "X0", "V")
     lin("OXm", "rho", 136, "OXn", "V")
     for n, a, m, add in (("sa", "rho", -32, "k"), ("sg64", "rho", 2.0 / 64, -1.0 / 64), ("cb", "i", -16, MAGIC), ("xa", "k96", 4, 0.0),
-                         ("xb", "h3", 64, "xa"), ("sent", "h3", -64, 64.0), ("w64", "h3", -63, 64.0),
-                         ("ta", "rho", -16, "X0"), ("ot", "rho", -32, "g16"), ("kxa", "rho", -32, 16.0), ("kx", "k63", 1, "kxa")):
+                         ("sent", "h3", -64, 64.0), ("w64", "h3", -63, 64.0), ("ta", "rho", -16, "X0"), ("ot", "rho", -32, "g16"),
+                         ("kxa", "rho", -32, 16.0), ("hi8", "h3", -64 * 1100, 64 * 1100.0), ("xc", "b0", 64, "xa"), ("kx", "k63", 1, "kxa"),
+                         ("bl", "rho", -8, "blk2"), ("xd", "s2", 1, "xc"), ("wz", "s", -65536, 13 * 32768.0), ("g0", "h3", -1, 1.0),
+                         ("nt64", "i", -16, 0.0), ("c8", "rho", -2.0 / 256, 1.0 / 256), ("t0", "b0", 1.0 / 32, 0.0),
+                         ("t1", "b1", 1.0 / 32, 0.0)):
         lin(n, a, m, add)
-    mat("OX", -8, "OXm", 1.0)
-    mat("OWN", -19, "g16", 1.0)
-    mat("SW", -16, "sa", 1.0)
-    fill(M("YM"), -65536.0, ["YM"])
-    fill(M("ANY"), -BIG, ["ANY"])
+    for n, w in (("OXa", 65.0), ("OXb", -129.0), ("OX", 1.0)):
+        mat(n, -8, "OXm", w)
     for c0, reg in ((4096, "OTz"), (8256, "OTy")):
         act(T.OT[:, c0:c0 + 16], M("ONES", 0, 16), col("sent"), 0.0, ["ONES", "c_sent"], [reg])
-    sc(M("R32"), M("OWN", 4, 144), 32.0, ["OWN"], ["R32"])
-    act(M("BKO"), M("OWN", 4, 144), col("w64"), 0.0, ["OWN", "c_w64"], ["BKO"])
-    sc(M("NOWN"), M("OWN"), -1.0, ["OWN"], ["NOWN"])
-    sc(M("NSW"), M("SW"), -1.0, ["SW"], ["NSW"])
-    sc(M("ISM"), M("SW"), -0.5, ["SW"], ["ISM"])
-    for j, (sh, m) in enumerate([(6, 1), (7, 127), (0, 63)]):
-        ts(T.FI[:, 128 * j:128 * j + 128], T.OI[:], sh, A.logical_shift_right, m, A.bitwise_and, ["OI"], ["FI%d" % j])
-    ts(T.FB[:, 0:128], T.FI[:, 0:128], 65.0, A.mult, None, None, ["FI0"], ["FB0"])
-    cp("V", T.FB[:, 128:384], T.FI[:, 128:384], ["FI1", "FI2"], ["FB1"])
+    ts(T.FI[:], T.OI[:], 63, A.bitwise_and, None, None, ["OI"], ["FI"])
+    for j, d in enumerate((64.0, 128.0)):
+        ts(T.FB[:, 128 * j:128 * j + 128], T.OI[:], 1 / d, A.mult, 1099.5 + 0.5 / d, A.add, ["OI"], ["FB%d" % j])
+    cp("V", T.FB[:, 256:384], T.FI[:], ["FI"], ["FB2"])
 
     def dst(cs):
         return [DstId(rid=topo.addr(c)[0], pnc=topo.addr(c)[1]) for c in cs]
@@ -266,10 +266,8 @@ def rank_program(g, core, T, topo):
             trs.append(RemoteDMATransfer(dst_ids=dst([mate]), dma_engine_mask=ms_, remote_sem=sem, srcs=[blocks(x, 0, 1)], dsts=[blocks(x, 4, 5)]))
         g.remote_dma_fused(trs, local_sem=T.sem["l" + x])
         toks_all["l" + x] = len(eo) + (len(es) if near else 0)
-        if not near:
-            g.remote_dma(blocks(x, 4, 5), blocks(x, 0, 1), sem, T.sem["m" + x], topo.addr(mate)[1], topo.addr(mate)[0], ms_)
-            toks_all["m" + x] = len(es)
-        arrive("r%d%s" % (at[4], x), len(es), [x + "s4"])
+        if near:
+            arrive("r%d%s" % (at[4], x), len(es), [x + "s4"])
         for j in [1, 2, 3] + list(range(8 - k, 8)):
             arrive("r%d%s" % (at[j], x), len(eo), [x + "s%d" % j])
 
@@ -284,8 +282,18 @@ def rank_program(g, core, T, topo):
         toks_all[f] = len(es)
         arrive(n, len(es), [x + "s%d" % j for j in range(4 + j0, 4 + j1)])
 
-    mms([(T.RV[:, 128 * b + 64 * h:128 * b + 64 * h + 64], M("OX", 136 * h + (0 if j == 2 else 8)), T.FB[:, 128 * j + 64 * b:128 * j + 64 * b + 64], j == 0, j == 2)
-         for b in (0, 1) for h in (0, 1) for j in range(3)], ["FB0", "FB1", "OX"], ["RV.r"], ["RV"])
+    def share(j):
+        n, f, h = "n%dOT" % j, "f%dOT" % j, len(es) // 2
+        pre("G", ["OT%d%d%s" % (b, at[j], z) for b in (0, 1) for z in "ab"], [])
+        g.remote_dma_fused([RemoteDMATransfer(dst_ids=dst([mate]), dma_engine_mask=sum(1 << e for e in es[h * b:h * b + h]), remote_sem=T.sem[n],
+                                              srcs=[T.OT[:, place(at[j], b):place(at[j], b) + 512]], dsts=[T.OT[:, place(at[j], b):place(at[j], b) + 512]])
+                            for b in (0, 1)], local_sem=T.sem[f])
+        post("G", (f, 2 * h), ["OT%d%d%s" % (b, at[j], z) for b in (0, 1) for z in "ab"], [])
+        arrive(n, 2 * h, ["OT%d%d%s" % (b, at[4 + j], z) for b in (0, 1) for z in "ab"])
+
+    mms([(T.RV[:, 128 * b + 64 * h:128 * b + 64 * h + 64], M(("OXa", "OXb", "OX")[j], 136 * h + (0 if j == 2 else 8)),
+          T.FB[:, 128 * j + 64 * b:128 * j + 64 * b + 64], j == 0, j == 2)
+         for b in (0, 1) for h in (0, 1) for j in range(3)], ["FB0", "FB1", "FB2", "OX", "OXa", "OXb"], ["RV.r"], ["RV"])
 
     def pack(x, high, Y, yr, yb):
         n = EX[x][0] // 2
@@ -326,35 +334,36 @@ def rank_program(g, core, T, topo):
             else:
                 act(o, src, 1.0, col("cb"), [bank + ".r", "c_cb"], W, [bank])
 
-    def order(x):
-        return [[0, 4, 1, 2, 3, 5, 6, 7], [0, 4, 1, 2, 3, 5, 7, 6], [0, 4, 1, 2, 6, 3, 5, 7], [0, 4, 1, 5, 2, 6, 3, 7]][EX[x][1]]
-
     def XE(b):
         return ["XE%d.%d" % (b, s) for s in range(8)]
 
-    def expand(b, q):
-        d0, R = place(rank, b), ["W%d%da" % (b, rank), "W%d%db" % (b, rank)]
-        if q == "S":
-            cp("S", T["XE%d" % b][:], T.W[:, d0:d0 + 512].indirect(T.XL[:]), R + ["XL"], XE(b))
-        elif q == "X":
-            cp("S", T.XW[:], T.W[:, d0:d0 + 512].indirect(T.XS[:]), R + ["XS"], ["XW"])
-        else:
-            for s in range(8):
-                cp("G", T["XE%d" % b][:, s::8], T.XW[:], ["XW"], XE(b)[s:s + 1])
+    def expand(b, slots=None, q="G"):
+        d0, xw = place(rank, b), T.XW[:, 128 * b:128 * b + 128]
+        if slots is None:
+            cp("S", xw, T.W[:, d0:d0 + 512].indirect(T.XS[:]), ["W%d%da" % (b, rank), "W%d%db" % (b, rank), "XS"], ["XW%d" % b])
+        for s in slots or ():
+            cp(q, T["XE%d" % b][:, s::8], xw, ["XW%d" % b], XE(b)[s:s + 1])
 
     def partners(js):
         for j in js:
             c0 = (15 + DELTA[j]) % 16
-            cp("G", M("BD%d" % j), M("R32"), ["R32"], ["BD%d" % j])
+            cp("G", M("BD%d" % j), M("OWN", 4, 144), ["OWN"], ["BD%d" % j])
             cp("G", MS("BD%d" % j, c0, 144 - c0), MS("NOWN", 4 - DELTA[j] + c0, 144 - c0), ["NOWN"], ["BD%d" % j])
 
     def stays(t):
-        b, thr = t & 1, "b0" if t == 0 else "b1"
+        b, thr = t & 1, "t0" if t == 0 else "t1"
         ts(T.H1[:], T.OF[:, 64 * b:64 * b + 64], EMPTY, A.is_equal, col(thr), A.add, ["OF%d" % b, "c_" + thr], ["H1"])
 
-    cp("S", blocks("LOi", 0, 1), T.RV[:, 0:256], ["RV.r"], ["LOis0"], ["RV"])
+    act(blocks("LOi", 0, 1), T.RV[:, 0:256], 1.0, col("hi8"), ["RV.r", "c_hi8"], ["LOis0"], ["RV"])
     send("LOi")
+    if "T0" not in PASS:
+        g.remote_dma(blocks("LOi", 4, 5), blocks("LOi", 0, 1), T.sem.n0OT, T.sem.f0OT, topo.addr(mate)[1], topo.addr(mate)[0], ms_)
+        toks_all["f0OT"] = len(es)
+        arrive("n0OT", len(es), ["LOis4"])
+    mat("OWN", -19, "g16", 1.0)
     mat("REP", "f31", "k", 1.0)
+    act(M("BKO"), M("OWN", 4, 144), col("w64"), 0.0, ["OWN", "c_w64"], ["BKO"])
+    sc(M("NOWN"), M("OWN"), -1.0 / 32, ["OWN"], ["NOWN"])
     ts(T.K0[:, 256:512], T.ST[:], col("sg64"), A.mult, None, None, ["ST", "c_sg64"], ["K0.y"], ["K0"])
     pack("LWi", lambda o, p, W: ts(o, T.ST[p, :], T.CF[p, names.index("sg64"):names.index("sg64") + 1], A.mult, None, None, ["ST", "c_sg64"], [W]),
          lambda p: T.K0[p, 256:512], "K0.y", "K0")
@@ -362,59 +371,70 @@ def rank_program(g, core, T, topo):
     for b in (0, 1):
         rep("LOi", 0, b, "S")
     mat("RW", "f31", "kx", -1.0)
-    ts(T.MK[:, 0:288], fld("f16", 288), col("s"), A.is_equal, None, None, ["f16", "c_s"], ["MK0"])
-    cp("G", T.MK[:, 288:544], T.MK[:, 32:288], ["MK0"], ["MK1"])
-    cp("G", T.MK[:, 544:1056], T.MK[:, 32:544], ["MK0", "MK1"], ["MK2"])
-    forward("LOi", 1, 2)
-    forward("LOi", 2, 4)
-    forward("LWi", 1, 2)
-    forward("LWi", 2, 3)
-    ts(T.XL[:], X(0, 64), col("xb"), A.add, None, None, ["XI", "c_xb"], ["XL"])
+    ts(T.MK[:, 0:256], fld("f16", 256), col("s"), A.is_equal, None, None, ["f16", "c_s"], ["MK0"])
+    emit("G", [lambda: g.iota(T.OT[:, 4112:4160], [[0, 48]], 0, 0, allow_small_or_imprecise_dtypes=True)], (), ["OTx"])
+    emit("G", [lambda: g.iota(T.W[:, 4096:4160], [[0, 64]], int(LOW), 0, allow_small_or_imprecise_dtypes=True)], (), ["Wz"])
+    ts(T.XS[:], X(0, 8, 8), col("xd"), A.add, None, None, ["XI", "c_xd"], ["XS"])
     mat("ENT", -24, "ta", "w64")
+    mat("SW", -16, "sa", 1.0)
+    for c0, n in ((256, 256), (512, 512), (1024, 32)):
+        cp("V", T.MK[:, c0:c0 + n], T.MK[:, 0:n], ["MK0", "MK256"], ["MK%d" % c0])
+    mat("IF", 0, "k", 1.0)
     rep("LWi", 0, 0, "S")
-    expand(0, "S")
+    expand(0)
     mms([(T.K1[:, 64 * b:64 * b + 64], M("ENT", 8 - 8 * h), T.LOi[:, 128 * b + 64 * h:128 * b + 64 * h + 64], h == 0, h == 1) for b in (0, 1) for h in (0, 1)],
         ["LOis0", "ENT"], ["K1.o"], ["K1"])
     rep("LWi", 0, 1, "V")
-    cp("V", T.OF[:], T.K1[:, 0:128], ["K1.o"], ["OF0", "OF1"], ["K1"])
     cp("V", T.OL[:], T.K1[:, 0:128], ["K1.o"], ["OL0", "OL1"], ["K1"])
-    mat("OTH", -31, "ot", 1.0)
-    colints(8, len(ints))
-    lin("xc", "b0", 64, "xa", "V")
-    stays(0)
-    lin("xd", "s2", 1, "xc", "V")
-    ts(T.XS[:], X(0, 8, 8), col("xd"), A.add, None, None, ["XI", "c_xd"], ["XS"])
+
+    def steps(names, x, t):
+        for step in names.split():
+            if step[0] not in "OW":
+                {"gather": lists_gather, "lists": lists}[step](t)
+            elif t:
+                rep("L" + step[0] + x, int(step[1]), 1 - (t & 1), step[2:])
+            else:
+                for b in (0, 1):
+                    rep("L" + step[0] + x, int(step[1]), b, step[2 + b])
+
+    steps(FIRST, "i", 0)
+    for step in PASS.split():
+        if step[0] == "T":
+            share(int(step[1]))
+        else:
+            forward("L" + step[0] + "i", int(step[1]), int(step[1]) + 1)
+    expand(0, range(8))
     field(2, len(FLD))
-    sel("IB", "ONES", [[1, 128]], A.is_equal, 0.0, 0, -1)
     partners((0, 1))
     sel("YM", "YM", [[-8, 16], [0, 8]], A.is_ge, 0.0, 0, 1)
     sel("YM", "YM", [[1, 128]], A.is_gt, 0.0, 0, -1)
     sel("YM", "YM", [[1, 128]], A.not_equal, 32768.0, 0, -1)
     sel("ANY", "ANY", [[-16, 8], [0, 16]], A.is_ge, 0.0, 0, 1)
     sel("ANY", "ANY", [[16, 8], [0, 16]], A.is_ge, 0.0, 15, -1)
-    sel("ISM", "ISM", [[1, 128]], A.not_equal, 0.5, 0, -1)
+    sel("ISM", "SW", [[1, 128]], A.not_equal, -1.0, 0, -1)
 
     def late2():
-        lin("bl", "rho", -8, "blk2")
-        lin("wz", "s", -65536, 13 * 32768.0)
-        lin("g0", "h3", -1, 1.0)
         mats("f4", "bl", 132, [("CH", 1.0)])
         act(M("ZC"), M("CH"), col("wz"), 0.0, ["CH", "c_wz"], ["ZC"])
         sc(M("KEEPN"), M("IB"), -16384.0, ["IB"], ["KEEPN"])
-        mats("f119", "ta", 128, [("KX0", "g0"), ("KX1", "h3")])
 
     def late3():
+        mats("f119", "ta", 128, [("KX0", "g0"), ("KX1", "h3")])
         for h in (0, 1):
             sc(M("KN%d" % h), M("KX%d" % h), -256.0, ["KX%d" % h], ["KN%d" % h])
-        lin("nt64", "i", -16, 0.0)
-        lin("eg0", "h3", EMPTY, -EMPTY)
-        lin("c8", "rho", -2.0 / 256, 1.0 / 256)
+        sc(M("NSW"), M("SW"), -1.0, ["SW"], ["NSW"])
         act(M("TMN"), M("IB"), col("nt64"), 0.0, ["IB", "c_nt64"], ["TMN"])
         sc(M("C2M"), M("IB"), MAGIC, ["IB"], ["C2M"])
+
+    def late3b():
+        sc(M("ISM"), M("ISM"), -0.5, ["ISM"], ["ISM"])
         act(M("CM"), M("IB"), col("c8"), 0.0, ["IB", "c_c8"], ["CM"])
+        for h, gn in ((0, "g0"), (1, "h3")):
+            act(M("ANY%d" % h), M("ANY"), col(gn), 0.0, ["ANY", "c_" + gn], ["ANY%d" % h])
 
     def late4():
-        lin("iv", "rho", -8, "OXn")
+        mats(-8, "iv", 128, [("INVF", 1.0)])
+        sc(M("INV1"), M("INVF"), -4128.0, ["INVF"], ["INV1"])
         sc(M("CM64"), M("CM"), 64.0, ["CM"], ["CM64"])
         lin("sgn", "rho", 2, -1.0)
         lin("s64", "rho", 128, -64.0)
@@ -422,7 +442,7 @@ def rank_program(g, core, T, topo):
 
     def lists_gather(t):
         b = t & 1
-        tt(T.GM[:], T.OT[:].indirect(T.OL[:, 64 * b:64 * b + 64]), T.MK[:, 16 * t:16 * t + 1024], A.mult, OTALL + ["OL%d" % b, "MK0", "MK1", "MK2"], ["GM"])
+        tt(T.GM[:], T.OT[:].indirect(T.OL[:, 64 * b:64 * b + 64]), T.MK[:, 16 * t:16 * t + 1024], A.mult, OTALL + ["OL%d" % b, "MK0", "MK256", "MK512", "MK1024"], ["GM"])
 
     def lists(t):
         mms([(T.K0[:, 0:64], SL("BKO", q), T.GM[:, q::16], q == 0, q == 15) for q in range(16)], ["GM", "BKO"], ["K0.k"], ["K0"])
@@ -432,11 +452,11 @@ def rank_program(g, core, T, topo):
         n = T.OF[:, 64 * b:64 * b + 64]
         if part == 0:
             ts(T.YH[:], n, 1.0 / 64, A.mult, 1025.0 - 63.0 / 128, A.add, ["OF%d" % b], ["YH"])
-            ts(T.YB[:], n, EMPTY + 63.5, A.is_gt, None, None, ["OF%d" % b], ["YB"])
-            mms([(T.NP[:, 128:192], M("INVF"), n, True, False), (T.NP[:, 128:192], M("INV0"), T.YH[:], False, False),
-                 (T.NP[:, 128:192], M("INV1"), T.YB[:], False, True)], ["OF%d" % b, "YH", "YB", "INVF", "INV0", "INV1"], ["NP.y"], ["NP"])
+            act(T.YB[:], n, 1.0, -(EMPTY + 63.5), ["OF%d" % b], ["YB"], (), AF.Sign)
         else:
-            act(T["YO%d" % b][:], T.NP[:, 128:192], 1.0, -65600.0, ["NP.y"], ["YO%d" % b], ["NP"])
+            mms([(T.UB[:, 0:64], M("INVF"), n, True, False), (T.UB[:, 0:64], M("INV0"), T.YH[:], False, False),
+                 (T.UB[:, 0:64], M("INV1"), T.YB[:], False, True)], ["OF%d" % b, "YH", "YB", "INVF", "INV0", "INV1"], ["UB.r"], ["UB"])
+            act(T["YO%d" % b][:], T.UB[:, 0:64], 1.0, -65600.0 - 4128.0, ["UB.r"], ["YO%d" % b], ["UB"])
             dmas("Y", [(T.yo[:, 64 * b:64 * b + 64], T["YO%d" % b][:])], "dO%d" % b, ["YO%d" % b], [])
 
     def round_(t):
@@ -446,26 +466,36 @@ def rank_program(g, core, T, topo):
         Wt = T.W[:]
         ol = T.OL[:, 64 * b:64 * b + 64]
         st = {1: [(0, 1), (2, 3)], 2: [(0, 2), (1, 3)], 3: [(0, 3), (1, 2)]}[m]
-        thr = "b0" if m == 1 else "b1"
-        mms([(T.K1[:, 0:64], SL("BKX", q), T.GM[:, q::16], q == 0, q == 15) for q in range(16)], ["GM", "BKX"], ["K1.k"], ["K1"])
+        thr = "t0" if m == 1 else "t1"
+        mms([(T.UB[:, 0:16 * XS], M("IF"), XEb[:, 0:16 * XS], True, True)], xe + ["IF"], ["UB.r"], ["UB"])
+        act(T.KC[:], T.K0[:, 0:64], 1.0, 32768.0 - 8256.0, ["K0.k"], ["KC"], ["K0"])
+        mms([(T.K1[:, 0:64], M("SW"), T.KC[:], True, True)], ["KC", "SW"], ["K1.k"], ["K1"])
+        cp("S", T.U5[:, 0:16 * XS], Wt.indirect(T.KL[:, 0:XS]), WALL + ["KL0"], ["U50", "U51", "U52", "U53"])
         cp("S", T.U[:], Wt.indirect(ol), WALL + ["OL%d" % b], ["U"])
         for i, (u, v) in enumerate(st):
             cp("S", T.UA[:, 256 * i:256 * i + 256], T.U[:, v::4], ["U"], ["UA.r"] if i == 0 else ["UA.2"], ["UA"])
-        act(T.KC[:], T.K0[:, 0:64], 1.0, 32768.0 - 8256.0, ["K0.k"], ["KC"], ["K0"])
         if t == 0:
-            late2()
-        tt(T.VO[:], Wt.indirect(T.KL[:, 0:64]), XEb[:], A.is_gt, WALL + ["KL0"] + xe, ["VO"])
-        mms([(T.RV[:, 0:64], SL("OWN", q), T.VO[:, q::16], q == 0, False) for q in range(16)], ["VO", "OWN"], ["RV.v"], ["RV"])
-        cp("V", T.KL[:, 64:128], T.K1[:, 0:64], ["K1.k"], ["KL1"], ["K1"])
-        if t == 1:
-            late4()
-        if t == 2:
-            outputs(1)
+            mats(-31, "ot", 144, [("OTH", 1.0)])
+            expand(1)
+            expand(1, range(4))
+        tt(T.VO[:, 16 * XS:], Wt.indirect(T.KL[:, XS:64]), XEb[:, 16 * XS:], A.is_gt, WALL + ["KL0"] + xe, ["VO"])
+        ts(T.KL[:, 64:128], T.K1[:, 0:64], 8256.0 - 32768.0, A.add, None, None, ["K1.k"], ["KL1"], ["K1"])
+        tt(T.VO[:, 0:16 * XS], T.U5[:, 0:16 * XS], T.UB[:, 0:16 * XS], A.is_gt, ["U50", "U51", "U52", "U53", "UB.r"], ["VO2"], ["UB"])
+        mms([(T.RV[:, 0:64], SL("OWN", q), T.VO[:, q::16], q == 0, False) for q in range(16)], ["VO", "VO2", "OWN"], ["RV.v"], ["RV"])
         tt(T.VX[:], Wt.indirect(T.KL[:, 64:128]), XEb[:], A.is_lt, WALL + ["KL1"] + xe, ["VX"])
         mms([(T.RV[:, 0:64], SL("OTH", q), T.VX[:, q::16], False, q == 15) for q in range(16)], ["VX", "OTH"], ["RV.v2"], ["RV"])
+        if t == 0:
+            late2()
+        if t == 1:
+            expand(0)
+            expand(0, range(4))
+            expand(0, range(4, 8), "S")
+            lin("iv", "rho", -8, "OXn")
         act(T.R1[:], T.RV[:, 0:64], 1024.0, col(thr), ["RV.v", "RV.v2", "c_" + thr], ["R1"], ["RV"])
         if t == 0:
             late3()
+        if t == 2:
+            outputs(1)
         nq = 0
         for i, (u, v) in enumerate(st):
             for y, op in ((u, A.is_gt), (v, A.is_lt)):
@@ -474,27 +504,38 @@ def rank_program(g, core, T, topo):
                     ["C%d" % y, "BD%d" % (2 * t), "BD%d" % (2 * t + 1)] + (["BD0", "BD1"] if m == 3 else []), ["DD.d%d" % y], ["DD"])
                 nq += 4
         dd = ["DD.d%d" % y for y in range(4)]
+        if nx:
+            cp("V", T.OF[:, 64 * b:64 * b + 64], ol, ["OL%d" % b], ["OF%d" % b])
+        if t == 0:
+            fill(T.RS[:], 1.0, ["RS"])
+        stays(t)
         if t == 1:
-            mat("INVF", -8, "iv", 1.0)
-            sc(M("INV1"), M("INVF"), -8256.0, ["INVF"], ["INV1"])
+            late4()
+            mat("INV0", -8, "iv", 64.0)
+        if t == 2:
+            natural(1, 0)
         tt(T.REV[:], T.DD[:, 0:64], T.R1[:], A.is_ge, dd + ["R1"], ["REV"], ["DD"])
         mms([(T.YY[:, 0:64], M("YM"), T.REV[:], True, True)], ["REV", "YM"], ["YY.y"], ["YY"])
-        if t == 1:
-            mat("INV0", -8, "iv", 64.0)
+        if t == 0:
+            fill(T.RS[:, 0::8], 0.0, ["RS"])
         mms([(T.K1[:, 64:96], M("ZC", 4 - 4 * e), T.REV[:, 32 * e:32 * e + 32], e == 0, False) for e in (0, 1)], ["REV", "ZC"], ["K1.z"], ["K1"])
+        if t == 2:
+            natural(1, 1)
         tt(T.FK[:], T.YY[:, 0:64], T.KC[:], A.min, ["YY.y", "KC"], ["FK"], ["YY"])
         mms([(T.K1[:, 64:96], M("CH", 4 - 4 * e), T.FK[:, 32 * e:32 * e + 32], False, e == 1) for e in (0, 1)], ["FK", "CH"], ["K1.c"], ["K1"])
         tt(T.H2[:], T.YY[:, 0:64], T.H1[:], A.max, ["YY.y", "H1"], ["H2"], ["YY"])
         tt(T.KEEP[:], T.DD[:, 0:64], T.H2[:], A.is_ge, dd + ["H2"], ["KEEP"], ["DD"])
         mms([(T.NP[:, 0:64], M("KEEPN"), T.KEEP[:], True, False)], ["KEEP", "KEEPN"], ["NP.n"], ["NP"])
+        tt(T.OK[:], T.OF[:, 64 * b:64 * b + 64], T.KEEP[:], A.mult, ["OF%d" % b, "KEEP"], ["OK"])
         ts(T.CL[:], T.K1[:, 64:96], 8256.0, A.add, None, None, ["K1.z", "K1.c"], ["CL"], ["K1"])
         if nx:
             mms([(T.RV[:, 64 * h + 128:64 * h + 192], M("KX%d" % h), T.KEEP[:], True, True) for h in (0, 1)], ["KEEP", "KX0", "KX1"], ["RV.k"], ["RV"])
         cp("V", T.E[:, 0:256], T.OT[:].indirect(T.CL[:, 0:16]), OTALL + ["CL"], ["E0"])
         cp("S", T.E[:, 256:512], T.OT[:].indirect(T.CL[:, 16:32]), OTALL + ["CL"], ["E1"])
+        if t == 0:
+            late3b()
         mms([(T.NP[:, 32 * e:32 * e + 32], M("ENT", 8 - 8 * h), T.E[:, 8 * h + 4 * e::16], False, h == 1 and e == 1) for e in (0, 1) for h in (0, 1)],
             ["E0", "E1", "ENT"], ["NP.n2"], ["NP"])
-        tt(T.OK[:], T.OF[:, 64 * b:64 * b + 64], T.KEEP[:], A.mult, ["OF%d" % b, "KEEP"], ["OK"])
         if nx:
             old = T.LOi[:, 128 * b:128 * b + 128]
             tt(T.OXA[:], T.RV[:, 128:256], old, A.mult, ["RV.k", "LOis0"], ["OXA"], ["RV"])
@@ -508,42 +549,44 @@ def rank_program(g, core, T, topo):
         if nx:
             tt(blocks("LO" + nx, 0, 1), T.DD[:, 128:256], T.OXA[:], A.max, ["DD.x0", "DD.x1", "OXA"], ["LO%ss0" % nx], ["DD"])
             send("LO" + nx)
-        mms([(T.K0[:, 0:128], M("NSW"), XEb[:, 0::8], True, False), (T.K0[:, 0:128], M("TMN"), M("ONES"), False, False),
-             (T.K0[:, 0:128], M("C2M"), M("ONES"), False, False)], xe + ["NSW", "TMN", "C2M", "ONES"], ["K0.a"], ["K0"])
+            forward("LO" + nx)
+        mms([(T.K0[:, 0:128], M("TMN"), M("ONES"), True, False), (T.K0[:, 0:128], M("C2M"), M("ONES"), False, False)]
+            + [(T.K0[:, 64 * h:64 * h + 64], M("NSW"), XEb[:, 8 * h::16], False, False) for h in (0, 1)], xe + ["NSW", "TMN", "C2M", "ONES"], ["K0.a"], ["K0"])
         cut, k = CUT[0 if nx else 1], 1.0 if nx else 64.0
-        act(T.HN[:, 0::2], n, col("g0"), col("eg0"), ["OF%d" % b, "c_g0", "c_eg0"], ["HN1"], (), AF.Abs)
         for h in (1, 2, 3):
             act(T.U5[:, 16 * cut[h]:16 * cut[h + 1]], Wt.indirect(T.OL[:, 64 * b + cut[h]:64 * b + cut[h + 1]]), k, -k * LOW, WALL + ["OL%d" % b], ["U5%d" % h])
-        ts(T.HN[:, 1::2], n, EMPTY, A.not_equal, col("h3"), A.mult, ["OF%d" % b, "c_h3"], ["HN2"])
+        ts(T.HN[:], n, EMPTY, A.not_equal, None, None, ["OF%d" % b], ["HN"])
         ts(T.U5[:, 0:16 * cut[1]], Wt.indirect(T.OL[:, 64 * b:64 * b + cut[1]]), -LOW, A.add, k, A.mult, WALL + ["OL%d" % b], ["U50"])
-        mms([(T.K0[:, 0:128], M("ANY"), T.HN[:], False, True)], ["HN1", "HN2", "ANY"], ["K0.b"], ["K0"])
+        mms([(T.K0[:, 64 * h:64 * h + 64], M("ANY%d" % h), T.HN[:], False, h == 1) for h in (0, 1)], ["HN", "ANY0", "ANY1"], ["K0.b"], ["K0"])
         mms([(T.RV[:, 256:384], M("CM" if nx else "CM64"), M("ONES"), True, False)], ["CM" if nx else "CM64", "ONES"], ["RV.t"], ["RV"])
         for h in range(4):
             emit("V", [lambda: g.vector.tensor_tensor_scan(out=T.MX[:, 16 * cut[h]:16 * cut[h + 1]], data0=T.RS[:, 0:16 * (cut[h + 1] - cut[h])],
                                                            data1=T.U5[:, 16 * cut[h]:16 * cut[h + 1]], initial=0.0, op0=A.mult, op1=A.max)], ["RS", "U5%d" % h], ["MX%d" % h])
             if h == 0:
                 ts(T.D[:], T.K0[:, 0:128], LOW - MAGIC, A.max, k, A.mult, ["K0.a", "K0.b"], ["D"], ["K0"])
-                mms([(T.RV[:, 256 + 64 * i:320 + 64 * i], M("ISM"), T.D[:, i::2], False, False) for i in (0, 1)], ["D", "ISM"], ["RV.d"], ["RV"])
-                if t:
+                mms([(T.RV[:, 256 + 64 * i:320 + 64 * i], M("ISM"), T.D[:, 64 * i:64 * i + 64], False, False) for i in (0, 1)], ["D", "ISM"], ["RV.d"], ["RV"])
+                if nx:
+                    nb[0] = 0
+                    rep("LO" + nx, 0, b, "S")
+                else:
                     natural(b, 0)
-        if t:
-            natural(b, 1)
         mx = ["MX0", "MX1", "MX2", "MX3"]
         mms([(T.RV[:, 256 + 64 * h:320 + 64 * h], M("ISM"), T.MX[:, 7 + 8 * h::16], False, h == 1) for h in (0, 1)], mx + ["ISM"], ["RV.s"], ["RV"])
         for h in (0, 1):
-            tt(T.M1[:, 64 * h:64 * h + 64], T.MX[:, 7 + 8 * h::16], T.D[:, h::2], A.add, mx + ["D"], ["M1%d" % h])
+            tt(T.M1[:, 64 * h:64 * h + 64], T.MX[:, 7 + 8 * h::16], T.D[:, 64 * h:64 * h + 64], A.add, mx + ["D"], ["M1%d" % h])
         new = ["RV.s", "RV.d", "RV.t", "M10", "M11"]
         if nx:
-            nb[0] = 0
-            for j in (0, 4):
-                rep("LO" + nx, j, b, "S")
+            rep("LO" + nx, 4, b, "S")
             tt(T.K1[:, 256:384], T.RV[:, 256:384], T.M1[:], A.max, new, ["K1.y"], ["RV", "K1"])
             pack("LW" + nx, lambda o, p, W: tt(o, T.RV[p, 256:384], T.M1[p, :], A.max, new, [W], ["RV"]), lambda p: T.K1[p, 256:384], "K1.y", "K1")
             send("LW" + nx)
-            forward("LW" + nx)
+            for j in range(1, 4 - EX["LW" + nx][1]):
+                forward("LW" + nx, j, j + 1)
+            if t == 0:
+                expand(1, range(4, 8))
             partners((2 * t + 2, 2 * t + 3))
-            stays(t + 1)
         else:
+            natural(b, 1)
             tt(T.YI[:], T.RV[:, 256:384], T.M1[:], A.max, new, ["YI"], ["RV"])
             ts(T.YW0[:], T.YI[:], col("sgn"), A.mult, None, None, ["YI", "c_sgn"], ["YW0"])
             outputs(0)
@@ -560,37 +603,10 @@ def rank_program(g, core, T, topo):
                                      in_=T["YW%d" % b][32 * P + r0:32 * P + r0 + 16, 64 * h:64 * h + 64]).then_inc(T.sem["dY%d" % b], 16)
         toks_all["dY%d" % b] = 16 * 16
 
-    expand(1, "X")
-    expand(1, "G")
-    rep("LOi", 4, 0, "V")
-    rep("LOi", 4, 1, "V")
-    rep("LWi", 4, 0, "V")
-    rep("LWi", 4, 1, "S")
-    act(M("BKX"), M("OTH"), col("w64"), 0.0, ["OTH", "c_w64"], ["BKX"])
-    for x, j in (("LOi", 1), ("LOi", 2), ("LOi", 3), ("LOi", 5), ("LWi", 1), ("LOi", 6), ("LOi", 7)):
-        rep(x, j, 0, "V")
-        rep(x, j, 1, "S")
-    lists_gather(0)
-    for j, qs in ((2, "SS"), (5, "SS"), (3, "VV"), (6, "SV"), (7, "SV")):
-        rep("LWi", j, 0, qs[0])
-        if j == 3:
-            lists(0)
-        rep("LWi", j, 1, qs[1])
+    steps(START, "i", 0)
     round_(0)
-    for t, x, b in ((1, "2", 0), (2, "3", 1)):
-        oo, ow = order("LO" + x), order("LW" + x)
-        for i, j in enumerate(oo[2:]):
-            rep("LO" + x, j, b, "SV"[i & 1])
-        lists_gather(t)
-        for i, j in enumerate(ow[:5]):
-            rep("LW" + x, j, b, "SSSVS"[i])
-            if i == 1 and t == 1:
-                expand(b, "X")
-                expand(b, "G")
-        lists(t)
-        rep("LW" + x, ow[5], b, "S")
-        rep("LW" + x, ow[6], b, "V")
-        rep("LW" + x, ow[7], b, "SV")
+    for t, x in ((1, "2"), (2, "3")):
+        steps(LATER, x, t)
         round_(t)
     for s in SEMAPHORES:
         if toks_all.get(s, 0) > known["G"].get(s, 0):

from concourse.bass import DstId, RemoteDMATransfer
from concourse.mybir import AluOpType as A, ActivationFunctionType as AF

EX = {"LOi": (256, 0, False), "LWi": (512, 1, True), "LO2": (128, 2, True), "LW2": (256, 1, True), "LO3": (128, 2, True), "LW3": (256, 1, True)}
CUT = [(0, 12, 32, 52, 64), (0, 12, 32, 52, 64)]
FIRST = ""
START = "O1VS W4VS O2VS O3VS O5VS W1VS O6VS O7VS gather W2SS W5SS W3VS W6VS lists W7SV"
LATER = "O1S O2V O6S O3V O7SV O5SV gather W0S W4S W1S W2S W3V lists W5SV W7SV W6SV"
PASS = "T0 O1 O2 O3 W1 W2"
XS = 20
BIG = 2.0 ** 23
MAGIC = 1.5 * 2.0 ** 17
EMPTY = 4096.0
LOW = 2.0 ** 17
MATB = [("REP", 512), ("YM", 128), ("ZC", 132), ("ENT", 136), ("KEEPN", 128), ("ANY", 128), ("ANY0", 128), ("ANY1", 128), ("KX0", 128), ("KX1", 128),
        ("KN0", 128), ("KN1", 128), ("IB", 128), ("TMN", 128), ("CM", 128), ("CM64", 128), ("C2M", 128), ("ONES", 128),
        ("INV1", 128), ("OWN", 152), ("NOWN", 152), ("OTH", 144), ("BKO", 144),
        ("TMP", 144)] + [("BD%d" % d, 144) for d in range(6)]
MATF = [("CH", 132), ("SW", 128), ("NSW", 128), ("ISM", 128), ("INVF", 128), ("IF", 128)]
MATH = [("RW", 256), ("INV0", 128), ("OX", 272), ("OXa", 272), ("OXb", 272)]
FLD = [("f31", [[32, 4], [0, 4], [1, 32]], 0), ("f16", [[0, 2], [1, 8], [0, 16]], 0), ("f4", [[1, 34], [0, 4]], -5),
       ("f119", [[16, 8], [0, 2], [1, 8]], -16)]
DELTA = [1, -1, 2, -2, 3, -3]
F, B16, H16, I32, U16 = "float32", "bfloat16", "float16", "int32", "uint16"
SCRATCH = {}
for _n, _w, _d in (("W", 8256, F), ("OT", 8272, B16), ("MBF", sum(w for n, w in MATB), B16), ("MFF", sum(w for n, w in MATF), F),
                   ("MHF", sum(w for n, w in MATH), H16), ("CI", 16, I32), ("CF", 64, F), ("XI", 312, B16), ("MF", 512 * len(FLD), B16),
                   ("MK", 1056, B16), ("RS", 384, B16), ("ST", 256, I32), ("OI", 128, I32), ("FI", 128, I32), ("FB", 384, H16), ("OF", 128, F),
                   ("OL", 128, U16), ("XE0", 1024, F), ("XE1", 1024, F), ("GM", 1024, B16), ("KL", 128, U16), ("KC", 64, F),
                   ("H1", 64, F), ("H2", 64, F), ("U", 1024, F), ("VO", 1024, B16), ("VX", 1024, B16), ("C", 1024, B16), ("R1", 64, F),
                   ("REV", 64, B16), ("FK", 64, F), ("KEEP", 64, B16), ("OK", 64, F), ("CL", 32, U16), ("E", 512, B16),
                   ("OXA", 128, B16), ("HN", 64, B16), ("U5", 1024, F), ("MX", 1024, F), ("D", 128, F), ("M1", 128, F), ("YI", 128, I32),
                   ("XS", 8, U16), ("XW", 256, F), ("YW0", 128, F), ("YW1", 128, F), ("YH", 64, H16), ("YB", 64, B16),
                   ("YO0", 64, F), ("YO1", 64, F), ("LWi", 4096, H16), ("LW2", 2048, H16), ("LW3", 2048, H16),
                   ("LOi", 2048, B16), ("LO2", 1024, B16), ("LO3", 1024, B16)):
    SCRATCH[_n] = ("sbuf", [128, _w], _d)
for _n in ("K0", "K1", "RV", "DD", "YY", "NP", "UA", "UB"):
    SCRATCH[_n] = ("psum", [128, 512], F)
SEMAPHORES = (["sV", "sS", "sP", "sG", "dOI", "dST"]
              + [k + x for x in EX for k in ["r%d" % r for r in range(8)] + ["n1", "n2", "n3", "l", "f1", "f2", "f3"]]
              + [k + "%dOT" % j for k in "nf" for j in range(4)] + ["dY0", "dY1", "dO0", "dO1"])


def rank_program(g, core, T, topo):
    rank = T.rank_of(core)
    if rank is None:
        return
    cores = list(T.cores)
    same = [r for r in range(len(cores)) if topo.die(cores[r]) == topo.die(core)]
    other = [r for r in range(len(cores)) if topo.die(cores[r]) != topo.die(core)]
    idx = same.index(rank)
    mate = cores[other[idx]]
    assert topo.chip(mate) == topo.chip(core) and len(same) == len(other) == 4
    at = [same[(idx - j) % 4] for j in range(4)] + [other[(idx - j) % 4] for j in range(4)]
    eng = {"V": g.vector, "S": g.scalar, "P": g.tensor, "G": g, "Y": g.sync}
    cnt, known, clk, wr, rd, bk, toks_all = {q: 0 for q in eng}, {q: {} for q in eng}, {}, {}, {}, {}, {}

    def need(q, toks):
        best = {}
        for s, v in toks:
            best[s] = max(best.get(s, 0), v)
        todo = [(s, v) for s, v in best.items() if known[q].get(s, 0) < v]
        todo = [t for t in todo if not any(o != t and clk[o].get(t[0], 0) >= t[1] for o in todo)]
        for s, v in todo:
            eng[q].wait_ge(T.sem[s], v)
            for a, b in clk[(s, v)].items():
                known[q][a] = max(known[q].get(a, 0), b)
            known[q][s] = max(known[q].get(s, 0), v)

    def pre(q, R, W, B=()):
        toks = []
        for r in R:
            toks += wr.get(r, [])
        for w in W:
            toks += wr.get(w, []) + rd.get(w, [])
        for b in B:
            toks += [t for e, t in bk.get(b, {}).items() if e != q]
        need(q, toks)

    def post(q, tok, R, W, B=()):
        clk[tok] = dict(known[q])
        toks_all[tok[0]] = max(toks_all.get(tok[0], 0), tok[1])
        for r in R:
            rd[r] = [t for t in rd.get(r, []) if t[0] != tok[0]] + [tok]
        for w in W:
            wr[w], rd[w] = [tok], []
        for b in B:
            bk.setdefault(b, {})[q] = tok

    def emit(q, calls, R=(), W=(), B=()):
        pre(q, R, W, B)
        for c in calls:
            c().then_inc(T.sem["s" + q], 1)
            cnt[q] += 1
        post(q, ("s" + q, cnt[q]), R, W, B)

    def dmas(q, pairs, sem, R=(), W=()):
        pre(q, R, W)
        for o, i in pairs:
            eng[q].dma_start(out=o, in_=i).then_inc(T.sem[sem], 16)
        post(q, (sem, 16 * len(pairs)), R, W)

    def arrive(sem, val, W):
        clk[(sem, val)] = {}
        toks_all[sem] = val
        for w in W:
            wr[w] = wr.get(w, []) + [(sem, val)]

    def ts(out, in0, s1, op0, s2=None, op1=None, R=(), W=(), B=()):
        if op1 is None:
            emit("V", [lambda: g.vector.tensor_scalar(out=out, in0=in0, scalar1=s1, scalar2=None, op0=op0)], R, W, B)
        else:
            emit("V", [lambda: g.vector.tensor_scalar(out=out, in0=in0, scalar1=s1, scalar2=s2, op0=op0, op1=op1)], R, W, B)

    def tt(out, a, b, op, R=(), W=(), B=()):
        emit("V", [lambda: g.vector.tensor_tensor(out=out, in0=a, in1=b, op=op)], R, W, B)

    def cp(q, out, i, R=(), W=(), B=()):
        if q == "V":
            emit("V", [lambda: g.vector.tensor_copy(out=out, in_=i)], R, W, B)
        elif q == "S":
            emit("S", [lambda: g.scalar.activation(out=out, in_=i, func=AF.Copy)], R, W, B)
        else:
            emit("G", [lambda: g.affine_select(out, i, [[0, out.shape[1]]], A.is_ge, 0.0, 0, 0)], R, W)

    def fill(out, c, W):
        emit("V", [lambda: g.vector.memset(out, c)], (), W)

    def act(out, i, scale, bias, R=(), W=(), B=(), func=AF.Identity):
        emit("S", [lambda: g.scalar.activation(out=out, in_=i, func=func, bias=bias, scale=scale)], R, W, B)

    def sc(dst, src, scale, R, W):
        emit("S", [lambda: g.scalar.activation(out=dst, in_=src, func=AF.Copy, scale=float(scale))], R, W)

    def sel(name, src, pat, op, c, base, cm):
        emit("G", [lambda: g.affine_select(M(name), M(src), pat, op, c, base, cm)], [src], [name])

    def mms(groups, R=(), W=(), B=()):
        emit("P", [(lambda m=m: g.tensor.matmul(out=m[0], lhsT=m[1], rhs=m[2], start=m[3], stop=m[4])) for m in groups], R, W, B)

    def M(n, a=None, w=128):
        for buf, lst in ((T.MBF, MATB), (T.MFF, MATF), (T.MHF, MATH)):
            j = 0
            for name, width in lst:
                if name == n:
                    return buf[:, j:j + width] if a is None else buf[:, j + a:j + a + w]
                j += width

    def MS(n, a, w):
        j = sum(x[1] for x in MATB[:[x[0] for x in MATB].index(n)])
        return T.MBF[:, j + a:j + a + w:16]

    def SL(n, q):
        return M(n, (4 if n == "OWN" else 0) + 15 - q)

    def place(r, b):
        return 64 * (8 * r + 65 * b)

    dmas("Y", [(T.OI[:], T.opts[:])], "dOI", (), ["OI"])
    for q, r0, src in (("Y", 16, T.lw), ("S", 0, T.rw)):
        for P in range(4):
            for h in (0, 1):
                eng[q].dma_start(out=T.ST[32 * P + r0:32 * P + r0 + 16, 128 * h:128 * h + 128],
                                 in_=src[32 * P + 16 * h:32 * P + 16 * h + 16, :]).then_inc(T.sem.dST, 16)
    arrive("dST", 16 * 16, ["ST"])
    emit("G", [lambda: g.iota(T.CI[:, 0:1], [[0, 1]], 0, 1)], (), ["ci0"])
    emit("G", [lambda: g.iota(T.XI[:], [[1, 312]], -48, 0, allow_small_or_imprecise_dtypes=True)], (), ["XI"])

    def X(off, w, step=1):
        return T.XI[:, 48 + off:48 + off + w * step:step]

    def fld(n, w=128):
        j = [x[0] for x in FLD].index(n)
        return T.MF[:, 512 * j:512 * j + w]

    def field(lo, hi):
        for n, pat, base in FLD[lo:hi]:
            w = 1
            for st, c in pat:
                w *= c
            emit("G", [lambda: g.iota(fld(n, w), pat, base, 0, allow_small_or_imprecise_dtypes=True)], (), [n])

    field(0, 2)
    ints = [("rho", 4, 1), ("h3", 3, 1), ("X0", 0, 103), ("i", 0, 15), ("k63", 0, 63), ("s", 0, 7), ("g16", 0, 112), ("k96", 0, 96),
            ("blk2", 2, 30), ("b0", 0, 1), ("b1", 1, 1), ("s2", 1, 7)]
    names = ["k"] + [x[0] for x in ints]

    def colints(lo, hi):
        for j in range(lo, hi):
            n, sh, m = ints[j]
            ts(T.CI[:, j + 1:j + 2], T.CI[:, 0:1], sh, A.logical_shift_right, m, A.bitwise_and, ["ci0"], ["ci%d" % (j + 1)])
        a = lo + 1 if lo else 0
        cp("V", T.CF[:, a:hi + 1], T.CI[:, a:hi + 1], ["ci%d" % j for j in range(a, hi + 1)], ["c_" + n for n in names[a:hi + 1]])

    def col(n):
        j = names.index(n)
        return T.CF[:, j:j + 1]

    def lin(n, a, m, add, q="S"):
        names.append(n)
        d = add if not isinstance(add, str) else col(add)
        R = ["c_" + a] + (["c_" + add] if isinstance(add, str) else [])
        if q == "S":
            act(col(n), col(a), float(m), d, R, ["c_" + n])
        else:
            ts(col(n), col(a), float(m), A.mult, d, A.add, R, ["c_" + n])

    def mat(name, f, h, w):
        dst = M(name)
        n = dst.shape[1]
        src, fr = (X(f, n), "XI") if isinstance(f, int) else (fld(f, n), f)
        ts(dst, src, col(h), A.is_equal, col(w) if isinstance(w, str) else w, A.mult, [fr, "c_" + h] + (["c_" + w] if isinstance(w, str) else []), [name])

    def mats(f, h, n, outs):
        src, fr = (X(f, n), "XI") if isinstance(f, int) else (fld(f, n), f)
        act(M("TMP", 0, n), src, -1.0, col(h), [fr, "c_" + h], ["TMP"], (), AF.Abs)
        for name, w in outs:
            act(M(name), M("TMP", 0, n), -1.0, col(w) if isinstance(w, str) else w, ["TMP"] + (["c_" + w] if isinstance(w, str) else []), [name], (), AF.Relu)

    fill(M("ONES"), 1.0, ["ONES"])
    fill(M("YM"), -65536.0, ["YM"])
    fill(M("ANY"), -BIG, ["ANY"])
    sel("IB", "ONES", [[1, 128]], A.is_equal, 0.0, 0, -1)
    colints(0, len(ints))
    lin("OXn", "h3", 16, "X0", "V")
    lin("OXm", "rho", 136, "OXn", "V")
    for n, a, m, add in (("sa", "rho", -32, "k"), ("sg64", "rho", 2.0 / 64, -1.0 / 64), ("cb", "i", -16, MAGIC), ("xa", "k96", 4, 0.0),
                         ("sent", "h3", -64, 64.0), ("w64", "h3", -63, 64.0), ("ta", "rho", -16, "X0"), ("ot", "rho", -32, "g16"),
                         ("kxa", "rho", -32, 16.0), ("hi8", "h3", -64 * 1100, 64 * 1100.0), ("xc", "b0", 64, "xa"), ("kx", "k63", 1, "kxa"),
                         ("bl", "rho", -8, "blk2"), ("xd", "s2", 1, "xc"), ("wz", "s", -65536, 13 * 32768.0), ("g0", "h3", -1, 1.0),
                         ("nt64", "i", -16, 0.0), ("c8", "rho", -2.0 / 256, 1.0 / 256), ("t0", "b0", 1.0 / 32, 0.0),
                         ("t1", "b1", 1.0 / 32, 0.0)):
        lin(n, a, m, add)
    for n, w in (("OXa", 65.0), ("OXb", -129.0), ("OX", 1.0)):
        mat(n, -8, "OXm", w)
    for c0, reg in ((4096, "OTz"), (8256, "OTy")):
        act(T.OT[:, c0:c0 + 16], M("ONES", 0, 16), col("sent"), 0.0, ["ONES", "c_sent"], [reg])
    ts(T.FI[:], T.OI[:], 63, A.bitwise_and, None, None, ["OI"], ["FI"])
    for j, d in enumerate((64.0, 128.0)):
        ts(T.FB[:, 128 * j:128 * j + 128], T.OI[:], 1 / d, A.mult, 1099.5 + 0.5 / d, A.add, ["OI"], ["FB%d" % j])
    cp("V", T.FB[:, 256:384], T.FI[:], ["FI"], ["FB2"])

    def dst(cs):
        return [DstId(rid=topo.addr(c)[0], pnc=topo.addr(c)[1]) for c in cs]

    eo = topo.engines(core, cores[same[(idx + 1) % 4]])
    es = [e for e in topo.engines(core, mate) if e not in eo]
    mo, ms_ = sum(1 << e for e in eo), sum(1 << e for e in es)

    def blocks(x, j0, j1):
        return T[x][:, EX[x][0] * j0:EX[x][0] * j1]

    def own(x):
        return [x + "s0", x + "s0a", x + "s0b", x + "s0c"]

    def send(x):
        w, k, near = EX[x]
        pre("G", own(x), [])
        one = [(same[(idx + j) % 4], j) for j in range(1, 4 - k)]
        both = [(side[(idx + j) % 4], j + o) for j in range(4 - k, 4) for side, o in ((same, 0), (other, 4))]
        to = one + both
        sem = T.sem["r%d%s" % (rank, x)]
        trs = [RemoteDMATransfer(dst_ids=dst([cores[r] for r, j in to]), dma_engine_mask=mo, remote_sem=sem,
                                 srcs=[blocks(x, 0, 1)], dsts=[blocks(x, j, j + 1) for r, j in to])]
        if near:
            trs.append(RemoteDMATransfer(dst_ids=dst([mate]), dma_engine_mask=ms_, remote_sem=sem, srcs=[blocks(x, 0, 1)], dsts=[blocks(x, 4, 5)]))
        g.remote_dma_fused(trs, local_sem=T.sem["l" + x])
        toks_all["l" + x] = len(eo) + (len(es) if near else 0)
        if near:
            arrive("r%d%s" % (at[4], x), len(es), [x + "s4"])
        for j in [1, 2, 3] + list(range(8 - k, 8)):
            arrive("r%d%s" % (at[j], x), len(eo), [x + "s%d" % j])

    def forward(x, j0=1, j1=0):
        w, k, near = EX[x]
        j1 = j1 or 4 - k
        if j0 == j1:
            return
        n, f = "n%d%s" % (j0, x), "f%d%s" % (j0, x)
        pre("G", [x + "s%d" % j for j in range(j0, j1)], [])
        g.remote_dma(blocks(x, 4 + j0, 4 + j1), blocks(x, j0, j1), T.sem[n], T.sem[f], topo.addr(mate)[1], topo.addr(mate)[0], ms_)
        toks_all[f] = len(es)
        arrive(n, len(es), [x + "s%d" % j for j in range(4 + j0, 4 + j1)])

    def share(j):
        n, f, h = "n%dOT" % j, "f%dOT" % j, len(es) // 2
        pre("G", ["OT%d%d%s" % (b, at[j], z) for b in (0, 1) for z in "ab"], [])
        g.remote_dma_fused([RemoteDMATransfer(dst_ids=dst([mate]), dma_engine_mask=sum(1 << e for e in es[h * b:h * b + h]), remote_sem=T.sem[n],
                                              srcs=[T.OT[:, place(at[j], b):place(at[j], b) + 512]], dsts=[T.OT[:, place(at[j], b):place(at[j], b) + 512]])
                            for b in (0, 1)], local_sem=T.sem[f])
        post("G", (f, 2 * h), ["OT%d%d%s" % (b, at[j], z) for b in (0, 1) for z in "ab"], [])
        arrive(n, 2 * h, ["OT%d%d%s" % (b, at[4 + j], z) for b in (0, 1) for z in "ab"])

    mms([(T.RV[:, 128 * b + 64 * h:128 * b + 64 * h + 64], M(("OXa", "OXb", "OX")[j], 136 * h + (0 if j == 2 else 8)),
          T.FB[:, 128 * j + 64 * b:128 * j + 64 * b + 64], j == 0, j == 2)
         for b in (0, 1) for h in (0, 1) for j in range(3)], ["FB0", "FB1", "FB2", "OX", "OXa", "OXb"], ["RV.r"], ["RV"])

    def pack(x, high, Y, yr, yb):
        n = EX[x][0] // 2
        for a in (0, 1):
            high(T[x][64 * a:64 * a + 64, n * a:n * a + n], slice(64 * a, 64 * a + 64), x + ("s0", "s0a")[a])
        for a in (0, 1):
            tt(T[x][64 - 64 * a:128 - 64 * a, n * a:n * a + n], Y(slice(64 * a, 64 * a + 64)), T[x][64 * a:64 * a + 64, n * a:n * a + n], A.subtract,
               [yr, x + ("s0", "s0a")[a]], [x + ("s0b", "s0c")[a]], [yb])

    OTALL = ["OTx", "OTz", "OTy"] + ["OT%d%d%s" % (b, r, z) for b in (0, 1) for r in range(8) for z in "ab"]
    WALL = ["Wz"] + ["W%d%d%s" % (b, r, z) for b in (0, 1) for r in range(8) for z in "ab"]
    rb = ["YY", "UB", "DD", "UA", "RV", "NP"]
    nb = [0]

    def rep(x, j, b, q):
        w, d0 = EX[x][0], place(at[j], b)
        n = 4 // len(q)
        for i, qi in enumerate(q):
            bank = rb[nb[0] % len(rb)]
            nb[0] += 1
            ps = range(n * i, n * i + n)
            if x[1] == "O":
                s0 = w * j + (128 * b if x == "LOi" else 0)
                ms = [(T[bank][:, 128 * (p - n * i):128 * (p - n * i) + 128], M("REP", 128 * p), T[x][:, s0:s0 + 128], True, True) for p in ps]
                mr, tab, reg = ["REP"], T.OT, "OT"
            else:
                cut = [(64 * h, 128 * h + 64 * b, 64) for h in (0, 1)] if x == "LWi" else [(0, 0, 128)]
                ms = [(T[bank][:, 128 * (p - n * i) + o:128 * (p - n * i) + o + c], M("RW", 128 * (p & 1)),
                       T[x][:, w * j + w // 2 * (p >> 1) + s:w * j + w // 2 * (p >> 1) + s + c], True, True) for p in ps for o, s, c in cut]
                mr, tab, reg = ["RW"], T.W, "W"
            mms(ms, (own(x) if j == 0 else [x + "s%d" % j]) + mr, [bank + ".r"], [bank])
            o, src = tab[:, d0 + 128 * n * i:d0 + 128 * n * (i + 1)], T[bank][:, 0:128 * n]
            W = ["%s%d%d%s" % (reg, b, at[j], z) for z in ("ab" if n == 4 else "ab"[i])]
            if reg == "OT":
                cp(qi, o, src, [bank + ".r"], W, [bank])
            elif qi == "V":
                ts(o, src, col("cb"), A.add, None, None, [bank + ".r", "c_cb"], W, [bank])
            else:
                act(o, src, 1.0, col("cb"), [bank + ".r", "c_cb"], W, [bank])

    def XE(b):
        return ["XE%d.%d" % (b, s) for s in range(8)]

    def expand(b, slots=None, q="G"):
        d0, xw = place(rank, b), T.XW[:, 128 * b:128 * b + 128]
        if slots is None:
            cp("S", xw, T.W[:, d0:d0 + 512].indirect(T.XS[:]), ["W%d%da" % (b, rank), "W%d%db" % (b, rank), "XS"], ["XW%d" % b])
        for s in slots or ():
            cp(q, T["XE%d" % b][:, s::8], xw, ["XW%d" % b], XE(b)[s:s + 1])

    def partners(js):
        for j in js:
            c0 = (15 + DELTA[j]) % 16
            cp("G", M("BD%d" % j), M("OWN", 4, 144), ["OWN"], ["BD%d" % j])
            cp("G", MS("BD%d" % j, c0, 144 - c0), MS("NOWN", 4 - DELTA[j] + c0, 144 - c0), ["NOWN"], ["BD%d" % j])

    def stays(t):
        b, thr = t & 1, "t0" if t == 0 else "t1"
        ts(T.H1[:], T.OF[:, 64 * b:64 * b + 64], EMPTY, A.is_equal, col(thr), A.add, ["OF%d" % b, "c_" + thr], ["H1"])

    act(blocks("LOi", 0, 1), T.RV[:, 0:256], 1.0, col("hi8"), ["RV.r", "c_hi8"], ["LOis0"], ["RV"])
    send("LOi")
    if "T0" not in PASS:
        g.remote_dma(blocks("LOi", 4, 5), blocks("LOi", 0, 1), T.sem.n0OT, T.sem.f0OT, topo.addr(mate)[1], topo.addr(mate)[0], ms_)
        toks_all["f0OT"] = len(es)
        arrive("n0OT", len(es), ["LOis4"])
    mat("OWN", -19, "g16", 1.0)
    mat("REP", "f31", "k", 1.0)
    act(M("BKO"), M("OWN", 4, 144), col("w64"), 0.0, ["OWN", "c_w64"], ["BKO"])
    sc(M("NOWN"), M("OWN"), -1.0 / 32, ["OWN"], ["NOWN"])
    ts(T.K0[:, 256:512], T.ST[:], col("sg64"), A.mult, None, None, ["ST", "c_sg64"], ["K0.y"], ["K0"])
    pack("LWi", lambda o, p, W: ts(o, T.ST[p, :], T.CF[p, names.index("sg64"):names.index("sg64") + 1], A.mult, None, None, ["ST", "c_sg64"], [W]),
         lambda p: T.K0[p, 256:512], "K0.y", "K0")
    send("LWi")
    for b in (0, 1):
        rep("LOi", 0, b, "S")
    mat("RW", "f31", "kx", -1.0)
    ts(T.MK[:, 0:256], fld("f16", 256), col("s"), A.is_equal, None, None, ["f16", "c_s"], ["MK0"])
    emit("G", [lambda: g.iota(T.OT[:, 4112:4160], [[0, 48]], 0, 0, allow_small_or_imprecise_dtypes=True)], (), ["OTx"])
    emit("G", [lambda: g.iota(T.W[:, 4096:4160], [[0, 64]], int(LOW), 0, allow_small_or_imprecise_dtypes=True)], (), ["Wz"])
    ts(T.XS[:], X(0, 8, 8), col("xd"), A.add, None, None, ["XI", "c_xd"], ["XS"])
    mat("ENT", -24, "ta", "w64")
    mat("SW", -16, "sa", 1.0)
    for c0, n in ((256, 256), (512, 512), (1024, 32)):
        cp("V", T.MK[:, c0:c0 + n], T.MK[:, 0:n], ["MK0", "MK256"], ["MK%d" % c0])
    mat("IF", 0, "k", 1.0)
    rep("LWi", 0, 0, "S")
    expand(0)
    mms([(T.K1[:, 64 * b:64 * b + 64], M("ENT", 8 - 8 * h), T.LOi[:, 128 * b + 64 * h:128 * b + 64 * h + 64], h == 0, h == 1) for b in (0, 1) for h in (0, 1)],
        ["LOis0", "ENT"], ["K1.o"], ["K1"])
    rep("LWi", 0, 1, "V")
    cp("V", T.OL[:], T.K1[:, 0:128], ["K1.o"], ["OL0", "OL1"], ["K1"])

    def steps(names, x, t):
        for step in names.split():
            if step[0] not in "OW":
                {"gather": lists_gather, "lists": lists}[step](t)
            elif t:
                rep("L" + step[0] + x, int(step[1]), 1 - (t & 1), step[2:])
            else:
                for b in (0, 1):
                    rep("L" + step[0] + x, int(step[1]), b, step[2 + b])

    steps(FIRST, "i", 0)
    for step in PASS.split():
        if step[0] == "T":
            share(int(step[1]))
        else:
            forward("L" + step[0] + "i", int(step[1]), int(step[1]) + 1)
    expand(0, range(8))
    field(2, len(FLD))
    partners((0, 1))
    sel("YM", "YM", [[-8, 16], [0, 8]], A.is_ge, 0.0, 0, 1)
    sel("YM", "YM", [[1, 128]], A.is_gt, 0.0, 0, -1)
    sel("YM", "YM", [[1, 128]], A.not_equal, 32768.0, 0, -1)
    sel("ANY", "ANY", [[-16, 8], [0, 16]], A.is_ge, 0.0, 0, 1)
    sel("ANY", "ANY", [[16, 8], [0, 16]], A.is_ge, 0.0, 15, -1)
    sel("ISM", "SW", [[1, 128]], A.not_equal, -1.0, 0, -1)

    def late2():
        mats("f4", "bl", 132, [("CH", 1.0)])
        act(M("ZC"), M("CH"), col("wz"), 0.0, ["CH", "c_wz"], ["ZC"])
        sc(M("KEEPN"), M("IB"), -16384.0, ["IB"], ["KEEPN"])

    def late3():
        mats("f119", "ta", 128, [("KX0", "g0"), ("KX1", "h3")])
        for h in (0, 1):
            sc(M("KN%d" % h), M("KX%d" % h), -256.0, ["KX%d" % h], ["KN%d" % h])
        sc(M("NSW"), M("SW"), -1.0, ["SW"], ["NSW"])
        act(M("TMN"), M("IB"), col("nt64"), 0.0, ["IB", "c_nt64"], ["TMN"])
        sc(M("C2M"), M("IB"), MAGIC, ["IB"], ["C2M"])

    def late3b():
        sc(M("ISM"), M("ISM"), -0.5, ["ISM"], ["ISM"])
        act(M("CM"), M("IB"), col("c8"), 0.0, ["IB", "c_c8"], ["CM"])
        for h, gn in ((0, "g0"), (1, "h3")):
            act(M("ANY%d" % h), M("ANY"), col(gn), 0.0, ["ANY", "c_" + gn], ["ANY%d" % h])

    def late4():
        mats(-8, "iv", 128, [("INVF", 1.0)])
        sc(M("INV1"), M("INVF"), -4128.0, ["INVF"], ["INV1"])
        sc(M("CM64"), M("CM"), 64.0, ["CM"], ["CM64"])
        lin("sgn", "rho", 2, -1.0)
        lin("s64", "rho", 128, -64.0)
        lin("sm", "rho", -128 * MAGIC, 64 * MAGIC)

    def lists_gather(t):
        b = t & 1
        tt(T.GM[:], T.OT[:].indirect(T.OL[:, 64 * b:64 * b + 64]), T.MK[:, 16 * t:16 * t + 1024], A.mult, OTALL + ["OL%d" % b, "MK0", "MK256", "MK512", "MK1024"], ["GM"])

    def lists(t):
        mms([(T.K0[:, 0:64], SL("BKO", q), T.GM[:, q::16], q == 0, q == 15) for q in range(16)], ["GM", "BKO"], ["K0.k"], ["K0"])
        cp("V", T.KL[:, 0:64], T.K0[:, 0:64], ["K0.k"], ["KL0"], ["K0"])

    def natural(b, part):
        n = T.OF[:, 64 * b:64 * b + 64]
        if part == 0:
            ts(T.YH[:], n, 1.0 / 64, A.mult, 1025.0 - 63.0 / 128, A.add, ["OF%d" % b], ["YH"])
            act(T.YB[:], n, 1.0, -(EMPTY + 63.5), ["OF%d" % b], ["YB"], (), AF.Sign)
        else:
            mms([(T.UB[:, 0:64], M("INVF"), n, True, False), (T.UB[:, 0:64], M("INV0"), T.YH[:], False, False),
                 (T.UB[:, 0:64], M("INV1"), T.YB[:], False, True)], ["OF%d" % b, "YH", "YB", "INVF", "INV0", "INV1"], ["UB.r"], ["UB"])
            act(T["YO%d" % b][:], T.UB[:, 0:64], 1.0, -65600.0 - 4128.0, ["UB.r"], ["YO%d" % b], ["UB"])
            dmas("Y", [(T.yo[:, 64 * b:64 * b + 64], T["YO%d" % b][:])], "dO%d" % b, ["YO%d" % b], [])

    def round_(t):
        b, m = t & 1, 1 + t
        nx = {0: "2", 1: "3", 2: None}[t]
        xe, XEb = XE(b), T["XE%d" % b]
        Wt = T.W[:]
        ol = T.OL[:, 64 * b:64 * b + 64]
        st = {1: [(0, 1), (2, 3)], 2: [(0, 2), (1, 3)], 3: [(0, 3), (1, 2)]}[m]
        thr = "t0" if m == 1 else "t1"
        mms([(T.UB[:, 0:16 * XS], M("IF"), XEb[:, 0:16 * XS], True, True)], xe + ["IF"], ["UB.r"], ["UB"])
        act(T.KC[:], T.K0[:, 0:64], 1.0, 32768.0 - 8256.0, ["K0.k"], ["KC"], ["K0"])
        mms([(T.K1[:, 0:64], M("SW"), T.KC[:], True, True)], ["KC", "SW"], ["K1.k"], ["K1"])
        cp("S", T.U5[:, 0:16 * XS], Wt.indirect(T.KL[:, 0:XS]), WALL + ["KL0"], ["U50", "U51", "U52", "U53"])
        cp("S", T.U[:], Wt.indirect(ol), WALL + ["OL%d" % b], ["U"])
        for i, (u, v) in enumerate(st):
            cp("S", T.UA[:, 256 * i:256 * i + 256], T.U[:, v::4], ["U"], ["UA.r"] if i == 0 else ["UA.2"], ["UA"])
        if t == 0:
            mats(-31, "ot", 144, [("OTH", 1.0)])
            expand(1)
            expand(1, range(4))
        tt(T.VO[:, 16 * XS:], Wt.indirect(T.KL[:, XS:64]), XEb[:, 16 * XS:], A.is_gt, WALL + ["KL0"] + xe, ["VO"])
        ts(T.KL[:, 64:128], T.K1[:, 0:64], 8256.0 - 32768.0, A.add, None, None, ["K1.k"], ["KL1"], ["K1"])
        tt(T.VO[:, 0:16 * XS], T.U5[:, 0:16 * XS], T.UB[:, 0:16 * XS], A.is_gt, ["U50", "U51", "U52", "U53", "UB.r"], ["VO2"], ["UB"])
        mms([(T.RV[:, 0:64], SL("OWN", q), T.VO[:, q::16], q == 0, False) for q in range(16)], ["VO", "VO2", "OWN"], ["RV.v"], ["RV"])
        tt(T.VX[:], Wt.indirect(T.KL[:, 64:128]), XEb[:], A.is_lt, WALL + ["KL1"] + xe, ["VX"])
        mms([(T.RV[:, 0:64], SL("OTH", q), T.VX[:, q::16], False, q == 15) for q in range(16)], ["VX", "OTH"], ["RV.v2"], ["RV"])
        if t == 0:
            late2()
        if t == 1:
            expand(0)
            expand(0, range(4))
            expand(0, range(4, 8), "S")
            lin("iv", "rho", -8, "OXn")
        act(T.R1[:], T.RV[:, 0:64], 1024.0, col(thr), ["RV.v", "RV.v2", "c_" + thr], ["R1"], ["RV"])
        if t == 0:
            late3()
        if t == 2:
            outputs(1)
        nq = 0
        for i, (u, v) in enumerate(st):
            for y, op in ((u, A.is_gt), (v, A.is_lt)):
                tt(T.C[:, y::4], T.U[:, u::4], T.UA[:, 256 * i:256 * i + 256], op, ["U", "UA.r", "UA.2"], ["C%d" % y], ["UA"])
                mms([(T.DD[:, 0:64], SL("BD%d" % DELTA.index((q ^ m) - q), q), T.C[:, q::16], nq + j == 0, nq + j == 15) for j, q in enumerate(range(y, 16, 4))],
                    ["C%d" % y, "BD%d" % (2 * t), "BD%d" % (2 * t + 1)] + (["BD0", "BD1"] if m == 3 else []), ["DD.d%d" % y], ["DD"])
                nq += 4
        dd = ["DD.d%d" % y for y in range(4)]
        if nx:
            cp("V", T.OF[:, 64 * b:64 * b + 64], ol, ["OL%d" % b], ["OF%d" % b])
        if t == 0:
            fill(T.RS[:], 1.0, ["RS"])
        stays(t)
        if t == 1:
            late4()
            mat("INV0", -8, "iv", 64.0)
        if t == 2:
            natural(1, 0)
        tt(T.REV[:], T.DD[:, 0:64], T.R1[:], A.is_ge, dd + ["R1"], ["REV"], ["DD"])
        mms([(T.YY[:, 0:64], M("YM"), T.REV[:], True, True)], ["REV", "YM"], ["YY.y"], ["YY"])
        if t == 0:
            fill(T.RS[:, 0::8], 0.0, ["RS"])
        mms([(T.K1[:, 64:96], M("ZC", 4 - 4 * e), T.REV[:, 32 * e:32 * e + 32], e == 0, False) for e in (0, 1)], ["REV", "ZC"], ["K1.z"], ["K1"])
        if t == 2:
            natural(1, 1)
        tt(T.FK[:], T.YY[:, 0:64], T.KC[:], A.min, ["YY.y", "KC"], ["FK"], ["YY"])
        mms([(T.K1[:, 64:96], M("CH", 4 - 4 * e), T.FK[:, 32 * e:32 * e + 32], False, e == 1) for e in (0, 1)], ["FK", "CH"], ["K1.c"], ["K1"])
        tt(T.H2[:], T.YY[:, 0:64], T.H1[:], A.max, ["YY.y", "H1"], ["H2"], ["YY"])
        tt(T.KEEP[:], T.DD[:, 0:64], T.H2[:], A.is_ge, dd + ["H2"], ["KEEP"], ["DD"])
        mms([(T.NP[:, 0:64], M("KEEPN"), T.KEEP[:], True, False)], ["KEEP", "KEEPN"], ["NP.n"], ["NP"])
        tt(T.OK[:], T.OF[:, 64 * b:64 * b + 64], T.KEEP[:], A.mult, ["OF%d" % b, "KEEP"], ["OK"])
        ts(T.CL[:], T.K1[:, 64:96], 8256.0, A.add, None, None, ["K1.z", "K1.c"], ["CL"], ["K1"])
        if nx:
            mms([(T.RV[:, 64 * h + 128:64 * h + 192], M("KX%d" % h), T.KEEP[:], True, True) for h in (0, 1)], ["KEEP", "KX0", "KX1"], ["RV.k"], ["RV"])
        cp("V", T.E[:, 0:256], T.OT[:].indirect(T.CL[:, 0:16]), OTALL + ["CL"], ["E0"])
        cp("S", T.E[:, 256:512], T.OT[:].indirect(T.CL[:, 16:32]), OTALL + ["CL"], ["E1"])
        if t == 0:
            late3b()
        mms([(T.NP[:, 32 * e:32 * e + 32], M("ENT", 8 - 8 * h), T.E[:, 8 * h + 4 * e::16], False, h == 1 and e == 1) for e in (0, 1) for h in (0, 1)],
            ["E0", "E1", "ENT"], ["NP.n2"], ["NP"])
        if nx:
            old = T.LOi[:, 128 * b:128 * b + 128]
            tt(T.OXA[:], T.RV[:, 128:256], old, A.mult, ["RV.k", "LOis0"], ["OXA"], ["RV"])
            for h in (0, 1):
                mms([(T.DD[:, 128 + 64 * h:192 + 64 * h], M("KN%d" % h), T.KEEP[:], True, False)]
                    + [(T.DD[:, 128 + 64 * h + 32 * e:160 + 64 * h + 32 * e], M("IB"), T.E[:, 8 * h + 4 * e::16], False, e == 1) for e in (0, 1)],
                    ["KEEP", "E0", "E1", "IB", "KN%d" % h], ["DD.x%d" % h], ["DD"])
        n = T.OF[:, 64 * b:64 * b + 64]
        tt(n, T.NP[:, 0:64], T.OK[:], A.max, ["NP.n", "NP.n2", "OK"], ["OF%d" % b], ["NP"])
        cp("V", ol, n, ["OF%d" % b], ["OL%d" % b])
        if nx:
            tt(blocks("LO" + nx, 0, 1), T.DD[:, 128:256], T.OXA[:], A.max, ["DD.x0", "DD.x1", "OXA"], ["LO%ss0" % nx], ["DD"])
            send("LO" + nx)
            forward("LO" + nx)
        mms([(T.K0[:, 0:128], M("TMN"), M("ONES"), True, False), (T.K0[:, 0:128], M("C2M"), M("ONES"), False, False)]
            + [(T.K0[:, 64 * h:64 * h + 64], M("NSW"), XEb[:, 8 * h::16], False, False) for h in (0, 1)], xe + ["NSW", "TMN", "C2M", "ONES"], ["K0.a"], ["K0"])
        cut, k = CUT[0 if nx else 1], 1.0 if nx else 64.0
        for h in (1, 2, 3):
            act(T.U5[:, 16 * cut[h]:16 * cut[h + 1]], Wt.indirect(T.OL[:, 64 * b + cut[h]:64 * b + cut[h + 1]]), k, -k * LOW, WALL + ["OL%d" % b], ["U5%d" % h])
        ts(T.HN[:], n, EMPTY, A.not_equal, None, None, ["OF%d" % b], ["HN"])
        ts(T.U5[:, 0:16 * cut[1]], Wt.indirect(T.OL[:, 64 * b:64 * b + cut[1]]), -LOW, A.add, k, A.mult, WALL + ["OL%d" % b], ["U50"])
        mms([(T.K0[:, 64 * h:64 * h + 64], M("ANY%d" % h), T.HN[:], False, h == 1) for h in (0, 1)], ["HN", "ANY0", "ANY1"], ["K0.b"], ["K0"])
        mms([(T.RV[:, 256:384], M("CM" if nx else "CM64"), M("ONES"), True, False)], ["CM" if nx else "CM64", "ONES"], ["RV.t"], ["RV"])
        for h in range(4):
            emit("V", [lambda: g.vector.tensor_tensor_scan(out=T.MX[:, 16 * cut[h]:16 * cut[h + 1]], data0=T.RS[:, 0:16 * (cut[h + 1] - cut[h])],
                                                           data1=T.U5[:, 16 * cut[h]:16 * cut[h + 1]], initial=0.0, op0=A.mult, op1=A.max)], ["RS", "U5%d" % h], ["MX%d" % h])
            if h == 0:
                ts(T.D[:], T.K0[:, 0:128], LOW - MAGIC, A.max, k, A.mult, ["K0.a", "K0.b"], ["D"], ["K0"])
                mms([(T.RV[:, 256 + 64 * i:320 + 64 * i], M("ISM"), T.D[:, 64 * i:64 * i + 64], False, False) for i in (0, 1)], ["D", "ISM"], ["RV.d"], ["RV"])
                if nx:
                    nb[0] = 0
                    rep("LO" + nx, 0, b, "S")
                else:
                    natural(b, 0)
        mx = ["MX0", "MX1", "MX2", "MX3"]
        mms([(T.RV[:, 256 + 64 * h:320 + 64 * h], M("ISM"), T.MX[:, 7 + 8 * h::16], False, h == 1) for h in (0, 1)], mx + ["ISM"], ["RV.s"], ["RV"])
        for h in (0, 1):
            tt(T.M1[:, 64 * h:64 * h + 64], T.MX[:, 7 + 8 * h::16], T.D[:, 64 * h:64 * h + 64], A.add, mx + ["D"], ["M1%d" % h])
        new = ["RV.s", "RV.d", "RV.t", "M10", "M11"]
        if nx:
            rep("LO" + nx, 4, b, "S")
            tt(T.K1[:, 256:384], T.RV[:, 256:384], T.M1[:], A.max, new, ["K1.y"], ["RV", "K1"])
            pack("LW" + nx, lambda o, p, W: tt(o, T.RV[p, 256:384], T.M1[p, :], A.max, new, [W], ["RV"]), lambda p: T.K1[p, 256:384], "K1.y", "K1")
            send("LW" + nx)
            for j in range(1, 4 - EX["LW" + nx][1]):
                forward("LW" + nx, j, j + 1)
            if t == 0:
                expand(1, range(4, 8))
            partners((2 * t + 2, 2 * t + 3))
        else:
            natural(b, 1)
            tt(T.YI[:], T.RV[:, 256:384], T.M1[:], A.max, new, ["YI"], ["RV"])
            ts(T.YW0[:], T.YI[:], col("sgn"), A.mult, None, None, ["YI", "c_sgn"], ["YW0"])
            outputs(0)

    def outputs(b):
        if b == 1:
            act(T.M1[:], T.K1[:, 256:384], 1.0, MAGIC, ["K1.y"], ["M10", "M11"], ["K1"])
            act(T.YW1[:], T.M1[:], col("s64"), col("sm"), ["M10", "M11", "c_s64", "c_sm"], ["YW1"])
        for q, y, r0 in (("Y", T.yl, 16), ("Y" if b else "S", T.yr, 0)):
            pre(q, ["YW%d" % b], [])
            for P in range(4):
                for h in (0, 1):
                    eng[q].dma_start(out=y[32 * P + 16 * h:32 * P + 16 * h + 16, 64 * b:64 * b + 64],
                                     in_=T["YW%d" % b][32 * P + r0:32 * P + r0 + 16, 64 * h:64 * h + 64]).then_inc(T.sem["dY%d" % b], 16)
        toks_all["dY%d" % b] = 16 * 16

    steps(START, "i", 0)
    round_(0)
    for t, x in ((1, "2"), (2, "3")):
        steps(LATER, x, t)
        round_(t)
    for s in SEMAPHORES:
        if toks_all.get(s, 0) > known["G"].get(s, 0):
            g.wait_ge(T.sem[s], toks_all[s])
